import numpy as np, ml_dtypes
CORES = [35,38,43,46]
N = 4
import mx_ref
BF = ml_dtypes.bfloat16
def cols(t, e):
    v = np.concatenate([t.reshape(128, -1, 4), np.zeros((128, 1, 4), BF)], axis=1)
    return np.ascontiguousarray(v[:, e]).reshape(128, -1)
def pick(q, e):
    c = np.concatenate([q[0].reshape(128, -1, 4), np.zeros((128, 1, 4), np.uint8)], axis=1); s = np.concatenate([q[1], np.ones((16, 1), np.uint8)], axis=1)
    return (np.ascontiguousarray(c[:, e].reshape(128, -1)), np.ascontiguousarray(s[:, e]))
def join(*qs):
    return (np.concatenate([q[0] for q in qs], axis=1), np.concatenate([q[1] for q in qs], axis=1))
def put(q, e, v):
    c, s = q[0].reshape(128, -1, 4).copy(), q[1].copy(); c[:, e] = v[0].reshape(128, -1, 4); s[:, e] = v[1]
    return (c.reshape(128, -1), s)
def pk(c, s):
    return (np.ascontiguousarray(c), mx_ref.live(s))
def emit(q):
    return q[0], q[1]
def decode(q):
    o = []
    for b in range(4):
        e = np.zeros((128, 128, 4), np.float32); e[np.arange(128), np.arange(128), b] = 1
        o.append(mx_ref.matmul(mx_ref.quantize(e.reshape(128, 512).astype(BF)), q))
    return np.stack(o, axis=2).reshape(128, -1)
def f(rng, *shape):
    return mx_ref.flush((rng.standard_normal(shape, dtype=np.float32) * np.exp2(rng.integers(-2, 3, shape[:-1] + (1,)))).astype(BF))
def wide(rng, *shape, cols=0):
    v = rng.standard_normal(shape, dtype=np.float32) * np.exp2(rng.integers(-12, 13, shape)).astype(np.float32)
    if cols: v *= np.repeat(np.exp2(rng.integers(-cols, cols + 1, shape[:-2] + (1, shape[-1] // 4))) * (rng.random(shape[:-2] + (1, shape[-1] // 4)) > 0.0625), 4, axis=-1).astype(np.float32)
    return mx_ref.flush(v.astype(BF))
P, K, O = 256, 64, 1
def big(v):
    v = np.array(v.astype(np.float32))
    v[np.abs(v) < np.float32(2.0 ** -16)] = 0
    return v.astype(BF)
def sized(t, a):
    return big(t.astype(np.float32) * np.repeat(np.asarray(a, np.float32), 4, axis=-1))
def query(rng):
    v = np.zeros((N, 128, 512), BF)
    v[:, :, :4] = f(rng, 1, 128, 4)
    return v
def plain(rng):
    return {"lv": big(f(rng, N, 128, 4 * P)), "dm": big(f(rng, N, 128, 4 * P)), "nz": big(f(rng, N, 128, 4 * P)), "u": query(rng), "z": query(rng), "w": f(rng, N, 128, 512 * O)}
def positive(d):
    return {k: v if k == "w" else np.abs(v.astype(np.float32)).astype(BF) for k, v in d.items()}
def onto(t, e, rng):
    at, far = np.arange(N * P), e[e >= P]
    free = rng.permutation(np.setdiff1d(np.arange(P), e))[:far.size]
    at[free], at[far] = far, free
    return np.stack(np.split(cols(np.concatenate(t, axis=1), at), N, axis=1))
def setup_inputs(rng):
    return plain(rng)
def setup_inputs_ties(rng):
    d = plain(rng)
    for k in ("lv", "dm", "nz"):
        v = big((1 + rng.random((128, 48))) * 2.0 ** 27)
        d[k] = np.stack([big(cols(v, rng.permutation(np.arange(P) % 12)).astype(np.float32) * np.repeat(1 - 2 * rng.integers(0, 2, P), 4)) for r in range(N)])
    for k in ("u", "z"): d[k][:, :, :4] = big((1 + rng.random((1, 128, 4))) * 2.0 ** 29)
    return d
def setup_inputs_one(rng):
    d = positive(plain(rng))
    a, b = rng.permutation(N)[:2]
    g, h = np.ones((N, P)), np.ones((N, P))
    g[a, rng.permutation(P)[:K]] = 2.0 ** -8
    g[b, rng.permutation(P)[:K]] = 2.0 ** -4
    h[b, rng.permutation(P)[:K]] = 2.0 ** 8
    h[a, rng.permutation(P)[:K]] = 2.0 ** 4
    d["lv"], d["dm"] = sized(d["lv"], g[:, None]), sized(d["dm"], h[:, None])
    return d
def setup_inputs_again(rng):
    d = positive(plain(rng))
    n, top = K // N, (np.arange(128) < 64)[None, :, None]
    lt, lb, dt, db, nt = np.ones((5, N, P))
    for r in range(N):
        at, to = rng.permutation(P), rng.permutation(P)
        lt[r, at[:n]], lt[r, at[n:2 * n]] = 2.0 ** -6, 2.0 ** -3
        lb[r, at[:n:2]] = 2.0 ** 8
        nt[r, at[:n // 2]], nt[r, at[n // 2:n]] = 2.0 ** -8, 2.0 ** 4
        dt[r, to[:n]] = 2.0 ** -8
        db[r, to[:n]], db[r, to[n:2 * n]] = 2.0 ** 6, 2.0 ** 3
    d["lv"] = sized(d["lv"], np.where(top, lt[:, None], lb[:, None]))
    d["dm"] = sized(d["dm"], np.where(top, dt[:, None], db[:, None]))
    d["nz"] = sized(d["nz"], np.where(top, nt[:, None], 1.0))
    d["u"], d["z"] = big(d["u"].astype(np.float32) * top), big(d["z"].astype(np.float32) * ~top)
    return d
def setup_inputs_zero(rng):
    d = plain(rng)
    g, h, e = np.ones((3, N, P))
    for r in range(N):
        g[r, rng.permutation(P)[:3 * K // (2 * N)]] = 0
        h[r, rng.permutation(P)[K // (2 * N):]] = 0
        e[r, rng.permutation(P)[:P // 2]] = 0
    d["lv"], d["dm"], d["nz"] = sized(d["lv"], g[:, None]), sized(d["dm"], h[:, None]), sized(d["nz"], e[:, None])
    return d
def setup_inputs_spread(rng):
    d = plain(rng)
    d["lv"] = sized(wide(rng, N, 128, 4 * P), 32 * np.exp2(rng.integers(-6, 7, (N, 1, P))))
    for k in ("dm", "nz"): d[k] = sized(wide(rng, N, 128, 4 * P, cols=6), np.full((1, 1, P), 32.0))
    for k in ("u", "z"): d[k] = sized(d[k], np.full((1, 1, 128), 2.0 ** 24))
    low = np.concatenate([score(d["u"][r], mx_ref.quantize(np.ascontiguousarray(d["lv"][r]))) for r in range(N)])
    high = np.concatenate([score(d["z"][r], mx_ref.quantize(np.ascontiguousarray(d["dm"][r]))) for r in range(N)])
    d["lv"] = onto(d["lv"], np.argsort(low, kind="stable")[:K], rng)
    d["dm"] = onto(d["dm"], np.argsort(-high, kind="stable")[:K], rng)
    return d
def check_inputs(d):
    b = []
    for k, lo, hi in (("lv", -16, 28), ("dm", -16, 28), ("nz", -16, 28), ("u", -30, 30), ("z", -30, 30), ("w", -30, 30)):
        v = np.abs(d[k].astype(np.float32))
        if not (np.isfinite(v).all() and ((v == 0) | (v >= 2.0 ** lo) & (v <= 2.0 ** hi)).all()): b.append("a value of " + k)
    for k in ("u", "z"):
        v = d[k].astype(np.float32)
        if (v[:, :, 4:] != 0).any(): b.append(k + " has numbers behind its column 0")
        if (v != v[:1]).any(): b.append(k + " isn't the same on all ranks")
    return b
def score(t, q):
    return np.abs(mx_ref.matmul(mx_ref.quantize(np.ascontiguousarray(t)), q)[0]) + np.float32(0)
def reference(lv, dm, nz, u, z, w):
    L = [mx_ref.quantize(np.ascontiguousarray(lv[r])) for r in range(N)]
    X = [mx_ref.quantize(np.ascontiguousarray(dm[r])) for r in range(N)]
    noise = join(*[mx_ref.quantize(np.ascontiguousarray(nz[r])) for r in range(N)])
    oc, osc = np.zeros((N, 128, 8 * P), np.uint8), np.zeros((N, 16, 2 * P), np.uint8)
    sw, lw, y = np.zeros((N, 2, K), np.float32), np.zeros((N, 2, K), np.float32), np.zeros((N, 128, O * P), np.float32)
    for t in range(2):
        low = np.argsort(np.concatenate([score(u[r], L[r]) for r in range(N)]), kind="stable")[:K]
        high = np.argsort(-np.concatenate([score(z[r], X[r]) for r in range(N)]), kind="stable")[:K]
        lw[:, t], sw[:, t] = low, high
        gone, come = pick(join(*L), low), pick(join(*X), high)
        v = decode(come) * np.float32(0.5) + decode(pick(noise, low)) * np.float32(0.5)
        new = mx_ref.quantize(np.ascontiguousarray(v.astype(BF)))
        for r in range(N):
            a, b = np.flatnonzero(low // P == r), np.flatnonzero(high // P == r)
            L[r] = put(L[r], low[a] - P * r, pick(new, a))
            X[r] = put(X[r], high[b] - P * r, pick(gone, b))
    for r in range(N):
        oc[r], osc[r] = emit(join(L[r], X[r]))
        for o in range(O):
            y[r, :, P * o:P * o + P] = mx_ref.matmul(mx_ref.quantize(np.ascontiguousarray(w[r][:, 512 * o:512 * o + 512])), L[r])
    return {"oc": oc, "osc": osc, "sw": sw, "lw": lw, "y": y}

@@ -1,0 +1,484 @@
+from concourse.bass import DstId, RemoteDMATransfer
+from concourse.mybir import dt, AluOpType as A, AxisListType, ActivationFunctionType as AF
+
+F8 = "float8_e4m3fn_x4"
+TINY = 2.0 ** -118
+R16, R64 = 1.5 * 2.0 ** 27, 1.5 * 2.0 ** 29
+ROUNDS = 2
+LB, XB = 192, 448
+
+SCRATCH = {
+    "pA": ("psum", [128, 512], "float32"), "pB": ("psum", [128, 512], "float32"), "pC": ("psum", [128, 2048], "float32"),
+    "pD": ("psum", [128, 1024], "float32"),
+}
+for _n, _w, _d in (
+        ("t_lv", 1024, "bfloat16"), ("t_dm", 1024, "bfloat16"), ("t_nz", 1024, "bfloat16"), ("t_w", 512, "bfloat16"),
+        ("u0", 4, "bfloat16"), ("z0", 4, "bfloat16"), ("uz", 1024, "bfloat16"), ("qU", 256, F8), ("sU", 256, "uint8"),
+        ("qW", 128, F8), ("sW", 128, "uint8"), ("ones", 516, "bfloat16"), ("zer", 128, "bfloat16"),
+        ("SS", 1024, "bfloat16"), ("SI", 1024, "bfloat16"), ("EM", 516, "bfloat16"), ("qS", 256, F8), ("sS", 256, "uint8"),
+        ("qI", 256, F8), ("sI", 256, "uint8"), ("qE", 512, F8), ("sE", 512, "uint8"), ("NZ", 256, F8), ("NZs", 256, "uint8"),
+        ("pI", 1, "int32"), ("ii", 8, "int32"), ("fc", 8, "float32"), ("cc", 16, "float32"),
+        ("tin", 256, "bfloat16"), ("Mneg", 256, "bfloat16"), ("Mtri", 256, "bfloat16"), ("Kn", 128, "bfloat16"), ("RC", 128, "bfloat16"),
+        ("sel", 4, "float32"), ("io8", 8, "float32"), ("dmp", 4, "float32"), ("io32", 32, "float32"), ("DG", 32, "bfloat16"),
+        ("sgt", 32, "float32"), ("VO", 64, "bfloat16"), ("OE", 8, "float32"), ("urow", 512, "bfloat16"),
+        ("yt", 256, "float32"), ("FN", 512, F8), ("FNs", 512, "uint8")):
+    SCRATCH[_n] = ("sbuf", [128, _w], _d)
+ONCE = ("yd", "yo", "DD", "Dc", "tr2", "trU", "qH", "sH", "H", "Gs", "sC", "Vc", "rk", "trA", "wk",
+        "VT", "XR", "R", "pw", "ow", "ix", "own", "NEW", "lo16", "qF", "sF", "qG", "sG")
+for _n, _w, _d in (
+        ("SW", 704, F8), ("SWs", 704, "uint8"), ("LW", 704, F8), ("LWs", 704, "uint8"), ("XW", 384, F8), ("XWs", 384, "uint8"),
+        ("LN", 384, F8), ("LNs", 384, "uint8"), ("PS", 64, F8), ("PSs", 64, "uint8"), ("NP", 128, F8), ("NPs", 128, "uint8"),
+        ("qH", 128, F8), ("sH", 128, "uint8"), ("qF", 128, F8), ("sF", 128, "uint8"), ("qG", 128, F8), ("sG", 128, "uint8"),
+        ("H", 512, "bfloat16"), ("F", 2560, "bfloat16"), ("NEW", 512, "bfloat16"), ("VT", 96, "bfloat16"),
+        ("sC", 4, "float32"), ("Vc", 512, "float32"), ("yd", 512, "float32"), ("yo", 512, "float32"), ("DD", 1024, "bfloat16"),
+        ("rk", 4, "float32"), ("trA", 128, "float32"), ("Gs", 64, "float32"), ("trG", 64, "float32"), ("dg", 4, "float32"), ("wk", 5, "float32"),
+        ("own", 2, "float32"), ("landM", 6, "float32"), ("landP", 6, "float32"), ("XR", 256, "float32"), ("R", 256, "float32"),
+        ("Dc", 1040, "bfloat16"), ("cn", 4, "float32"), ("pw", 8, "float32"), ("ow", 16, "float32"),
+        ("tr2", 256, "float32"), ("ix", 40, "float32"), ("UL", 704, "bfloat16"),
+        ("trU", 512, "bfloat16"), ("lo16", 128, "uint16"), ("wl", 8, "float32"), ("fo", 4, "float32")):
+    for _t in range(1 if _n in ONCE else ROUNDS):
+        SCRATCH[_n + str(_t)] = ("sbuf", [128, _w], _d)
+
+SEMAPHORES = ["v", "s", "p", "gc", "ls"] + ["d%d" % k for k in range(80)] + \
+    [n + str(t) for n in ("aM", "aP", "aC") for t in range(ROUNDS)]
+
+
+def rank_program(g, core, T, topo):
+    rank = T.rank_of(core)
+    if rank is None:
+        return
+    cores = list(T.cores)
+    others = [q for q in range(4) if q != rank]
+    Q = {"v": g.vector, "s": g.scalar, "p": g.tensor, "gc": g, "y": g.sync}
+    cnt, seen, top, nd = {}, {}, {}, [0]
+
+    def need(qn, deps):
+        for d in deps:
+            if d is None:
+                continue
+            if isinstance(d, list):
+                need(qn, d)
+            elif seen.get((qn, d[0]), 0) < d[1]:
+                Q[qn].wait_ge(T.sem[d[0]], d[1])
+                seen[(qn, d[0])] = d[1]
+                top[d[0]] = max(top.get(d[0], 0), d[1])
+
+    def do(qn, deps, f):
+        need(qn, deps)
+        f(Q[qn]).then_inc(T.sem[qn], 1)
+        cnt[qn] = cnt.get(qn, 0) + 1
+        return (qn, cnt[qn])
+
+    def dma(qn, deps, out, in_):
+        need(qn, deps)
+        s = "d%d" % nd[0]
+        nd[0] += 1
+        Q[qn].dma_start(out, in_).then_inc(T.sem[s], 16)
+        cnt[s] = 16
+        return (s, 16)
+
+    def B(n, t):
+        return T[n + ("0" if n in ONCE else str(t))]
+
+    dst = [cores[q] for q in others]
+    far = [c for c in dst if topo.chip(c) != topo.chip(core)]
+    fe = topo.engines(core, far[0])
+    eng = {}
+    for n, c in enumerate(far):
+        w = len(fe) // len(far)
+        eng[c] = fe[n * w:(n + 1) * w]
+    for c in dst:
+        if c not in eng:
+            eng[c] = [e for e in topo.engines(core, c) if e not in fe][::len(far)]
+    arrive = sum(len(e) for e in eng.values())
+
+    def send(deps, sem, view, land):
+        need("gc", deps)
+        tr = []
+        for q, c in zip(others, dst):
+            rid, pid, _ = topo.addr(c)
+            s = [x for x in range(4) if x != q].index(rank)
+            tr.append(RemoteDMATransfer(dst_ids=[DstId(rid=rid, pnc=pid)], dma_engine_mask=sum(1 << e for e in eng[c]),
+                                        remote_sem=T.sem[sem], src=view, dst=land(s)))
+        g.remote_dma_fused(tr, local_sem=T.sem["ls"])
+        cnt["ls"] = cnt.get("ls", 0) + arrive
+        cnt[sem] = cnt.get(sem, 0) + arrive
+
+    def ts(o, i, s1, s2, *ops):
+        if len(ops) == 1:
+            return lambda q: q.tensor_scalar(o, i, s1, None, ops[0])
+        return lambda q: q.tensor_scalar(o, i, s1, s2, ops[0], ops[1])
+
+    def tt(o, a, b, op):
+        return lambda q: q.tensor_tensor(o, a, b, op)
+
+    def cp(o, i):
+        return lambda q: q.tensor_copy(o, i)
+
+    def act(o, i, fn=AF.Identity, **k):
+        return lambda q: q.activation(o, i, fn, **k)
+
+    def red(o, i):
+        return lambda q: q.tensor_reduce(o, i, AxisListType.X, A.add)
+
+    def trn(o, i):
+        return lambda q: q.transpose(o, i)
+
+    def fill(o, c):
+        return lambda q: q.memset(o, c)
+
+    def iota(o, pat, base=0, cm=0):
+        return lambda q: q.iota(o, pat, base, cm, allow_small_or_imprecise_dtypes=True)
+
+    def quant(o, s, i):
+        return lambda q: q.quantize_mx(o, s, i)
+
+    def mm(o, a, sa, b, sb, st=True, sp=True):
+        return lambda q: q.matmul_mx(o, a, sa, b, sb, st, sp)
+
+    U8, U32 = dt.uint8, dt.uint32
+
+    def after(p0):
+        return ("gc", cnt["gc"]) if p0 else None
+
+    d_u = dma("s", [], T.u0[:], T.u[:, 0:4])
+    d_z = dma("s", [], T.z0[:], T.z[:, 0:4])
+    d_lv = dma("y", [], T.t_lv[:], T.lv[:])
+    d_dm = dma("y", [], T.t_dm[:], T.dm[:])
+    d_nz = dma("y", [], T.t_nz[:], T.nz[:])
+    d_w = dma("y", [], T.t_w[:], T.w[:])
+
+    K = {}
+    i_p = do("gc", [], lambda q: q.iota(T.pI[:], [[0, 1]], 0, 1))
+    v_zer = do("v", [], fill(T.zer[:], 0.0))
+    v_tin = do("v", [], fill(T.tin[:], TINY))
+    bits = []
+    for c, m in enumerate((15, 32, 64, 63, 48, 112, 16)):
+        bits.append(do("v", [i_p], ts(T.ii[:, c:c + 1], T.pI[:, 0:1], m, None, A.bitwise_and)))
+    v_fc = do("v", bits, cp(T.fc[:, 0:7], T.ii[:, 0:7]))
+    v_one = do("v", [], fill(T.ones[:], 1.0))
+    v_ss = do("v", [], fill(T.SS[:], 0.0))
+    v_si = do("v", [], fill(T.SI[:], 0.0))
+    i_mn = do("gc", [v_tin], lambda q: q.affine_select(T.Mneg[:], T.tin[:], [[0, 2], [1, 128]], A.is_ge, -TINY, 0, -1))
+    i_mt = do("gc", [v_tin], lambda q: q.affine_select(T.Mtri[:], T.tin[:], [[0, 2], [-1, 128]], A.is_gt, -TINY, 0, 1))
+    i_kn = do("gc", [], iota(T.Kn[:], [[16, 4], [0, 2], [1, 16]]))
+    K["io32"] = do("gc", [], iota(T.io32[:], [[0, 2], [1, 16]]))
+    K["io8"] = do("gc", [], iota(T.io8[:], [[16, 8]]))
+    K["OE"] = [do("gc", [], iota(T.OE[:, 0:6], [[1, 3], [64, 2]], 542)), do("gc", [], iota(T.OE[:, 6:8], [[64, 2]], 32))]
+    K["EM"] = do("gc", [v_one], lambda q: q.affine_select(T.EM[:], T.ones[:], [[1, 516]], A.is_equal, 0.0, -3, -4))
+    K["SI"] = [v_si]
+    for p0, p1, at, end, step, c in ((0, 128, 0, 512, 32, 1), (0, 128, 1, 512, 32, 1), (0, 128, 2, 512, 32, 1), (0, 64, 4, 512, 32, 1), (0, 64, 5, 512, 64, 2),
+                                     (0, 64, 37, 512, 64, 1), (0, 64, 6, 512, 64, 1), (0, 64, 38, 512, 128, 1), (0, 1, 15, 512, 32, 1), (0, 64, 526, 1024, 128, 1),
+                                     (64, 128, 8, 512, 32, 1), (64, 128, 9, 512, 64, 2), (64, 128, 41, 512, 64, 1), (64, 128, 10, 512, 32, 1),
+                                     (64, 128, 558, 1024, 128, 1), (64, 65, 15, 512, 32, 1)):
+        K["SI"].append(do("gc", [v_si, after(p0)], iota(T.SI[p0:p1, at:end:step], [[0, len(range(at, end, step))]], c)))
+    K["177"] = [do("gc", [K["SI"]], iota(B("Dc", 0)[:, 208 * j + 193:208 * j + 194], [[0, 1]], 177)) for j in range(2)]
+    F_ = lambda c: T.fc[:, c:c + 1]
+    C_ = lambda c: T.cc[:, c:c + 1]
+    SG, M1, M0, SM1, SM0, AQ, CD, H1, EV, OD, OB = range(11)
+
+    SW0, SWs0 = B("SW", 0), B("SWs", 0)
+    uz, cst = [], []
+    for c, src, a, b in ((H1, 5, 1.0, 128.0), (AQ, 2, 4.0, 0.0), (SG, 2, -1 / 32, 1.0)):
+        cst.append(do("s", [v_fc], act(C_(c), F_(src), scale=a, bias=b)))
+    for b in range(4):
+        uz.append(do("v", [d_u, v_one], ts(T.uz[:, b:512:4], T.ones[:, 0:128], T.u0[:, b:b + 1], None, A.mult)))
+    for b in range(4):
+        uz.append(do("s", [d_z, v_zer], act(T.uz[:, 512 + b:1024:4], T.zer[:], bias=T.z0[:, b:b + 1])))
+    q_u = [do("v", uz[0:4], quant(T.qU[:, 0:128], T.sU[:, 0:128], T.uz[:, 0:512]))]
+    q_l = do("v", [d_lv], quant(SW0[:, LB:XB], SWs0[:, LB:XB], T.t_lv[:]))
+    q_u.append(do("v", uz[4:8], quant(T.qU[:, 128:256], T.sU[:, 128:256], T.uz[:, 512:1024])))
+    q_x = do("v", [d_dm], quant(SW0[:, XB:704], SWs0[:, XB:704], T.t_dm[:]))
+    sst = []
+    for b in range(4):
+        t, h = divmod(b, 2)
+        hi = C_(H1) if h else F_(5)
+        sst.append(do("s", [v_ss, v_one, v_fc], act(T.SS[:, 256 * t + b:256 * t + 256:4], T.ones[:, 0:64], AF.Copy, scale=F_(0))))
+        sst.append(do("s", [cst], act(T.SS[:, 512 + 256 * t + b:768 + 256 * t:4], T.ones[:, 0:64], AF.Copy, scale=hi)))
+    K["DG"] = do("v", [K["io32"], v_fc], ts(T.DG[:], T.io32[:], F_(0), None, A.is_equal))
+    K["sel"] = do("v", [K["io8"]], ts(T.sel[:], T.io8[:, 0:4], F_(4), None, A.is_equal))
+    v_qs = do("v", sst, quant(T.qS[:], T.sS[:], T.SS[:]))
+
+    def consts_s():
+        for c, src, a, b in ((M1, 1, 1 / 32, 0.0), (M0, 1, -1 / 32, 1.0), (CD, 2, 4.0, float(LB)),
+                             (EV, 6, -1 / 16, 1.0), (OD, 6, 1 / 16, 0.0), (OB, 6, -16.0, 0.0)):
+            cst.append(do("s", [v_fc], act(C_(c), F_(src), scale=a, bias=b)))
+        cst.append(do("s", [cst], act(C_(SM1), C_(M1), scale=C_(SG))))
+        cst.append(do("s", [], act(C_(SM0), C_(M0), scale=C_(SG))))
+        K["sgt"] = do("s", [v_one], act(T.sgt[:], T.ones[:, 0:32], AF.Copy, scale=C_(SG)))
+        Dc = B("Dc", 0)
+        K["Dc"] = K["177"] + [do("s", [], act(Dc[:, 816:817], F_(3), scale=4.0, bias=-30.0))]
+        for j in range(2):
+            K["Dc"].append(do("s", [], act(Dc[:, 208 * j + 192:208 * j + 193], F_(3), scale=2.0)))
+        K["wk"] = do("v", [], fill(B("wk", 0)[:, 4:5], -7.5))
+        K["VTc"] = do("v", [K["DG"], cst], ts(B("VT", 0)[:, 64:96], T.DG[:], C_(CD), None, A.mult))
+
+    def slots(t):
+        F = B("F", t)
+        z = do("v", [], fill(F[:, 0:1024], 0.0))
+        return [z, do("gc", [z], iota(F[0:64, 515:1024:4], [[0, 4], [0, 2], [1, 16]])),
+                do("gc", [z, after(64)], iota(F[64:128, 515:1024:4], [[16, 4], [0, 2], [0, 16]]))]
+
+    def consts_v():
+        K["F"] = [slots(0)]
+        K["VO"] = [do("v", [K["DG"]], ts(T.VO[:, 32 * s:32 * s + 32], T.DG[:], 64.0 * (s + 1), None, A.mult)) for s in range(2)]
+        K["nz"] = do("v", [d_nz], quant(T.NZ[:], T.NZs[:], T.t_nz[:]))
+        K["dmp"] = do("v", [K["io8"]], ts(T.dmp[:], T.io8[:, 0:8:2], F_(0), None, A.add))
+        K["qE"] = [do("v", [K["EM"]], quant(T.qE[:, 128 * b:128 * b + 128], T.sE[:, 128 * b:128 * b + 128], T.EM[:, 3 - b:515 - b])) for b in range(4)]
+        K["np"] = [do("v", [d_nz], quant(B("NP", 0)[:], B("NPs", 0)[:], T.t_nz[:, 0:512]))]
+        K["NEW"] = do("v", [], fill(B("NEW", 0)[:, 256:512], 0.0))
+        K["qI"] = do("v", K["SI"], quant(T.qI[:], T.sI[:], T.SI[:]))
+
+    def rows():
+        K["RC"] = do("gc", K["F"][0], iota(T.RC[:], [[16, 4], [0, 2], [1, 16]], 128))
+        K["ur"] = do("gc", [], iota(T.urow[:], [[16, 16], [0, 2], [1, 16]], -128))
+        for t in range(ROUNDS):
+            K["U%d" % t] = dma("y", [K["ur"]], B("UL", t)[:, 192:704], T.urow[:])
+
+    def consts_2():
+        K["F"].append(slots(1))
+        K["qW"] = do("v", [d_w], quant(T.qW[:], T.sW[:], T.t_w[:]))
+        K["np"].append(do("v", [d_nz], quant(B("NP", 1)[:], B("NPs", 1)[:], T.t_nz[:, 0:512])))
+
+    st = {"prev": []}
+
+    def copies(t, x, dep, r):
+        SW, SWs = B("SW", t), B("SWs", t)
+        c0 = XB if x else LB
+        for dn, o, key in ((("XW", 0, "X"), ("LW", XB, "W")) if x else (("LN", 0, "L"), ("LW", LB, "W"))):
+            r.setdefault(key, []).append(dma("y", [dep], B(dn, t)[:, o:o + 256].bitcast(U8), SW[:, c0:c0 + 256].bitcast(U8)))
+            r[key].append(dma("y", [dep], B(dn + "s", t)[:, o:o + 256], SWs[:, c0:c0 + 256]))
+
+    def score(t, ty, tk, k):
+        SW, SWs, sC, Vc, yd = (B(n, t) for n in ("SW", "SWs", "sC", "Vc", "yd"))
+        pr, w = st["prev"], LB + 256 * ty
+        qu, su = T.qU[:, 128 * ty:128 * ty + 128], T.sU[:, 128 * ty:128 * ty + 128]
+        pX, pY = ((T.pA, T.pC), (T.pB, T.pD))[ty]
+        r = do("p", [q_u[ty], tk, pr], mm(pX[:, 0:256], qu, su, SW[:, w:w + 256], SWs[:, w:w + 256]))
+        for h in range(2):
+            c = do("p", [], mm(pY[:, 512 * h:512 * h + 128], SW[:, w + 128 * h:w + 128 * h + 128],
+                               SWs[:, w + 128 * h:w + 128 * h + 128], qu, su))
+        ra = do("s", [r, pr], act(Vc[:, 256 * ty:256 * ty + 256], pX[:, 0:256], AF.Abs))
+        ca = do("s", [c], act(sC[:, 2 * ty:2 * ty + 2], pY[:, 0:1024:512], AF.Abs))
+        ys = [do("s", [ca, ra], act(yd[:, 256 * ty + 128 * h:256 * ty + 128 * h + 128], Vc[:, 256 * ty + 128 * h:256 * ty + 128 * h + 128],
+                                    bias=sC[:, 2 * ty + h:2 * ty + h + 1], scale=-1.0)) for h in range(2)]
+        k["sc"][ty] = (ca, ra, ys)
+
+    def ahead(t, ty, k):
+        sC, Vc, yd, DD = (B(n, t) for n in ("sC", "Vc", "yd", "DD"))
+        ca, ra, ys = k["sc"][ty]
+        o = 512 * ty
+        f0, f1, f2 = ((A.is_lt, A.is_le, A.is_gt), (A.is_gt, A.is_ge, A.is_lt))[ty]
+        a = do("v", [ca, ra, st["prev"]], ts(DD[:, o:o + 128], Vc[:, 256 * ty + 128:256 * ty + 256], sC[:, 2 * ty:2 * ty + 1], None, f0))
+        b = do("v", [ca, ra], ts(DD[:, o + 384:o + 512], Vc[:, 256 * ty:256 * ty + 128], sC[:, 2 * ty + 1:2 * ty + 2], None, f1))
+        d = do("v", [ys, i_mn, i_mt], tt(DD[:, o + 128:o + 384], yd[:, 256 * ty:256 * ty + 256], (T.Mneg, T.Mtri)[ty][:], f2))
+        return [a, b, d]
+
+    def order_and_send(t, k):
+        Vc, DD, rk, H = (B(n, t) for n in ("Vc", "DD", "rk", "H"))
+        pr, r = st["prev"], {}
+
+        def hot(b):
+            return do("v", [r[b], i_kn, pr], ts(H[:, b:512:4], T.Kn[:], rk[:, b:b + 1], None, A.is_equal))
+
+        def total(b, dd):
+            r[b] = do("s", dd, act(DD[:, 256 * b:256 * b + 256], DD[:, 256 * b:256 * b + 256], accum_out=rk[:, b:b + 1]))
+
+        f, l = k["first"], 1 - k["first"]
+        dd = ahead(t, f, k)
+        total(2 * f, dd)
+        total(2 * f + 1, dd)
+        dd = ahead(t, l, k)
+        total(2 * l, dd)
+        r[2 * l + 1] = do("v", dd, red(rk[:, 2 * l + 1:2 * l + 2], DD[:, 512 * l + 256:512 * l + 512]))
+        hs = [hot(b) for b in (2 * f, 2 * f + 1, 2 * l + 1, 2 * l)]
+        qh = do("v", hs, quant(B("qH", t)[:], B("sH", t)[:], H[:]))
+        do("p", [qh, v_qs, pr], mm(T.pD[:, 0:128], T.qS[:, 0:128], T.sS[:, 0:128], B("qH", t)[:], B("sH", t)[:], True, False))
+        m = do("p", [], mm(T.pD[:, 0:128], T.qS[:, 128:256], T.sS[:, 128:256], B("qH", t)[:], B("sH", t)[:], False, True))
+        trA, lo, G, trG = B("trA", t), B("lo16", t), B("Gs", t), B("trG", t)
+        k["trA"] = a = do("v", [m], trn(trA[:], T.pD[:, 0:128]))
+        of = do("v", [a, cst[1]], ts(lo[:, 0:4], trA[:, 0:128:32], C_(AQ), None, A.add))
+        gs = do("v", [of, k["sc"][0][1], k["sc"][1][1], pr], cp(G[:], Vc[:, 0:512].indirect(lo[:, 0:4])))
+        k["M"] = tg = do("v", [gs], trn(trG[:], G[:]))
+        send([tg], "aM%d" % t, trG[:, 31:33], lambda s: B("landM", t)[:, 2 * s:2 * s + 2])
+
+    def prepare(t, k):
+        own, wk, dg, VT, trA, trG, XR = (B(n, t) for n in ("own", "wk", "dg", "VT", "trA", "trG", "XR"))
+        w = do("v", [k["trA"], K["sel"]], tt(wk[:, 0:4], trA[:, 0:128:32], T.sel[:], A.mult))
+        a = do("v", [k["M"], cst], ts(own[:, 1:2], trG[:, 32:33], C_(SM1), None, A.mult))
+        pl = do("v", [w, K["wk"]], red(dg[:, 0:1], wk[:]))
+        k["s"] = do("v", [a], ts(own[:, 0:1], trG[:, 31:32], C_(SM0), own[:, 1:2], A.mult, A.add))
+        hi = do("v", [pl], ts(dg[:, 1:2], dg[:, 0:1], R16, R16, A.add, A.subtract))
+        xo = [do("s", [k["M"], K["sgt"]], act(XR[:, 192 + 32 * j:224 + 32 * j], T.sgt[:], AF.Copy, scale=trG[:, 31 + j:32 + j])) for j in range(2)]
+        v1 = do("v", [hi], ts(VT[:, 32:64], T.DG[:], dg[:, 1:2], None, A.mult))
+        lo_ = do("v", [hi], ts(dg[:, 2:3], dg[:, 0:1], dg[:, 1:2], 7.5, A.subtract, A.add))
+        k["Ro"] = do("v", xo, trn(B("R", t)[:, 192:256], XR[:, 192:256]))
+        v0 = do("v", [lo_], ts(VT[:, 0:32], T.DG[:], dg[:, 2:3], None, A.mult))
+        k["VT"] = [v0, v1, K["VTc"]]
+
+    def before(s, q, t, deps, at, x_of, neg=None):
+        R, Dc, out, seg = B("R", t), B("Dc", t), [], []
+        for x in x_of:
+            op = A.is_le if (others + [rank])[x] < q else A.is_lt
+            if seg and seg[-1][1] == 64 * x and seg[-1][2] == op:
+                seg[-1][1] += 64
+            else:
+                seg.append([64 * x, 64 * x + 64, op])
+        for (c0, c1, op) in seg:
+            if neg is None:
+                out.append(do("v", deps, ts(Dc[:, at:at + c1 - c0], R[:, c0:c1], s, 4.0, op, A.mult)))
+            else:
+                out.append(do("s", deps, act(Dc[:, at:at + c1 - c0], neg[0][:, neg[1] + c0:neg[1] + c1], AF.Sign, bias=TINY if op == A.is_le else -TINY)))
+            at += c1 - c0
+        return out
+
+    def merge_and_send(t, k):
+        LM, XR, R, Dc, cn, pw, lo, own, F, ow, yo = (B(n, t) for n in ("landM", "XR", "R", "Dc", "cn", "pw", "lo16", "own", "F", "ow", "yo"))
+        aM = ("aM%d" % t, arrive)
+        xs = []
+        for j in range(6):
+            if j % 2 == 0:
+                xs.append(do("v", [aM, cst], ts(XR[:, 32 * j:32 * j + 32], T.ones[:, 0:32], LM[:, j:j + 1], C_(SG), A.mult, A.mult)))
+            else:
+                xs.append(do("s", [aM, K["sgt"]], act(XR[:, 32 * j:32 * j + 32], T.sgt[:], AF.Copy, scale=LM[:, j:j + 1])))
+        k["R"] = do("v", xs, trn(R[:, 0:192], XR[:, 0:192]))
+        d = before(own[:, 0:1], rank, t, [k["R"], k["s"], st["prev"]], 624, range(3))
+        k["cn"] = c = do("v", [d, K["Dc"]], red(cn[:, 3:4], Dc[:, 624:817]))
+        fl = do("v", [c], ts(pw[:, 0:1], cn[:, 3:4], R64, R64, A.add, A.subtract))
+        of = do("v", [fl, K["OE"]], ts(lo[:, 4:10], T.OE[:, 0:6], pw[:, 0:1], cn[:, 3:4], A.add, A.add))
+        sc = do("v", [of, k["VT"], K["F"][t]], cp(F[:, 0:2560].indirect(lo[:, 4:10]), B("VT", t)[:]))
+        k["qF"] = do("v", [sc], quant(B("qF", t)[:], B("sF", t)[:], F[:, 512:1024]))
+        m = do("p", [k["qF"], K["qI"], st["prev"]], mm(T.pD[:, 512:640], T.qI[:, 0:128], T.sI[:, 0:128], B("qF", t)[:], B("sF", t)[:]))
+        k["own2"] = do("p", [k["sc"][1][1]], mm(T.pB[:, 0:128], B("qF", t)[:], B("sF", t)[:], T.qI[:, 0:128], T.sI[:, 0:128]))
+        o2 = [do("s", [aM, cst], act(ow[:, s:s + 1], LM[:, 2 * s:2 * s + 1], scale=C_(SM0))) for s in range(2)]
+        for s in range(2):
+            o2[s] = do("s", [o2[s]], act(ow[:, 8 + s:9 + s], LM[:, 2 * s + 1:2 * s + 2], scale=C_(SM1), bias=ow[:, s:s + 1]))
+        ys = [do("s", [o2[s], k["R"], k["Ro"]], act(yo[:, 256 * s + 64 - 64 * s:256 * s + 256], R[:, 64 - 64 * s:256], bias=ow[:, 8 + s:9 + s], scale=-1.0)) for s in range(2)]
+        sg = [before(None, others[s], t, [ys[s], st["prev"]], 208 * s, [x for x in range(4) if x != s], (yo, 256 * s)) for s in range(2)]
+        k["c2"] = [do("s", [sg[s], K["Dc"]], act(Dc[:, 416 + 416 * s:610 + 416 * s], Dc[:, 208 * s:208 * s + 194], scale=2.0, accum_out=cn[:, s:s + 1])) for s in range(2)]
+        a = do("v", [m], trn(B("tr2", t)[:, 0:128], T.pD[:, 512:640]))
+        of = do("v", [a], ts(lo[:, 10:14], B("tr2", t)[:, 0:128:32], float(LB), 703.0, A.max, A.min))
+        k["tr2"] = a
+        pd = [of, k["lt"], k["xt"]]
+        ps = do("v", pd, cp(B("PS", t)[:].bitcast(U32), B("SW", t)[:, 0:704].bitcast(U32).indirect(lo[:, 10:14])))
+        pss = do("s", pd, act(B("PSs", t)[:], B("SWs", t)[:, 0:704].indirect(lo[:, 10:14]), AF.Copy))
+        LW, LWs = B("LW", t), B("LWs", t)
+        o = (64, 128, 0)
+        send([ps], "aC%d" % t, B("PS", t)[:, 0:64].bitcast(U8), lambda s: LW[:, o[s]:o[s] + 64].bitcast(U8))
+        send([pss], "aC%d" % t, B("PSs", t)[:, 0:64], lambda s: LWs[:, o[s]:o[s] + 64])
+
+    def lists(t, k):
+        cn, pw, lo, F, ix, tr2, wl, UL, trU = (B(n, t) for n in ("cn", "pw", "lo16", "F", "ix", "tr2", "wl", "UL", "trU"))
+        tok = k["tr2"]
+        row = lambda r, g=0: tr2[:, 128 * g + r:128 * g + 128:32]
+        nl = do("v", [tok], cp(lo[:, 24:28], row(25)))
+        e = [do("s", [tok, cst], act(ix[:, 0:4], row(1), AF.Copy, scale=C_(EV))),
+             do("s", [tok, cst], act(ix[:, 4:8], row(2), scale=C_(OD), bias=C_(OB)))]
+        fl = do("v", k["c2"], ts(pw[:, 2:4], cn[:, 0:2], R64, R64, A.add, A.subtract))
+        nd_ = [nl, K["nz"], K["np"][t], st["prev"]]
+        k["np"] = [do("s", nd_, act(B("NPs", t)[:, 64:128], T.NZs[:, 0:256].indirect(lo[:, 24:28]), AF.Copy))]
+        of = [do("v", [fl, K["OE"]], ts(lo[:, 16 + 2 * s:18 + 2 * s], T.OE[:, 6:8], pw[:, 2 + s:3 + s], cn[:, s:s + 1], A.add, A.add)) for s in range(2)]
+        u1 = do("v", e, tt(ix[:, 8:12], ix[:, 0:4], ix[:, 4:8], A.max))
+        sc = do("v", [of, K["VO"], k["qF"]], cp(F[:, 0:2560].indirect(lo[:, 16:20]), T.VO[:]))
+        u2 = do("v", [u1, K["dmp"]], tt(ix[:, 12:16], ix[:, 8:12], T.dmp[:], A.max))
+        qg = do("v", [sc], quant(B("qG", t)[:], B("sG", t)[:], F[:, 0:512]))
+        do("p", [k["qF"], k["trA"]], mm(T.pD[:, 0:128], T.qI[:, 0:128], T.sI[:, 0:128], B("qF", t)[:], B("sF", t)[:], True, False))
+        mo = do("p", [qg], mm(T.pD[:, 0:128], T.qI[:, 128:256], T.sI[:, 128:256], B("qG", t)[:], B("sG", t)[:], False, True))
+        uo = [do("v", [u2], ts(lo[:, 48 + h:56:2], ix[:, 12:16], 16.0 * h, None, A.add)) for h in range(2)]
+        k["np"].append(do("v", nd_, cp(B("NP", t)[:, 64:128].bitcast(U32), T.NZ[:, 0:256].bitcast(U32).indirect(lo[:, 24:28]))))
+        k["dn"] = [do("p", [k["np"], K["qE"], st["prev"]], mm(T.pC[:, 512 * b:512 * b + 128], T.qE[:, 128 * b:128 * b + 128], T.sE[:, 128 * b:128 * b + 128],
+                                                              B("NP", t)[:], B("NPs", t)[:], True, False)) for b in range(4)]
+        w1 = do("s", [k["own2"]], act(wl[:, 0:2], T.pB[:, 9:11], AF.Sign))
+        k["w"] = []
+        for j in range(2):
+            w2 = do("s", [w1], act(wl[:, 2 + j:3 + j], wl[:, j:j + 1], AF.Copy, scale=256.0 * rank - (LB, XB)[j]))
+            k["w"].append(do("s", [w2], act(wl[:, 4 + j:5 + j], T.pB[:, 9 + j:10 + j], bias=wl[:, 2 + j:3 + j])))
+        send([k["w"]], "aP%d" % t, wl[:, 4:6], lambda s: B("landP", t)[:, 2 * s:2 * s + 2])
+        us = do("v", [uo, K["RC"], K["U%d" % t]], cp(UL[:, 0:704].indirect(lo[:, 48:56]), T.RC[:]))
+        a = do("v", [mo], trn(tr2[:, 128:256], T.pD[:, 0:128]))
+        m = [do("v", [a], tt(ix[:, 16 + 4 * j:20 + 4 * j], row(9 + j), row(3 + 8 * j, 1), A.max)) for j in range(2)]
+        k["AB"] = do("v", m, cp(lo[:, 32:40], ix[:, 16:24]))
+        a = do("v", [us], trn(trU[:], UL[:, 192:704]))
+        k["pl"] = [do("v", [a], ts(lo[:, 64 + 16 * x:80 + 16 * x], trU[:, 16 * x:512:32], 128.0, None, A.add)) for x in range(2)]
+
+    def renew(t, k, oq, os_, o):
+        LW, LWs, XW, XWs, LN, LNs, NEW, lo = (B(n, t) for n in ("LW", "LWs", "XW", "XWs", "LN", "LNs", "NEW", "lo16"))
+        ad = [("aC%d" % t, 2 * arrive), k["AB"], k["cp"]["W"]]
+        a2 = do("s", ad, act(XWs[:, 256:384], LWs[:, 0:704].indirect(lo[:, 32:40]), AF.Copy))
+        a1 = do("v", ad, cp(XW[:, 256:384].bitcast(U32), LW[:, 0:704].bitcast(U32).indirect(lo[:, 32:40])))
+        dc = [do("p", [a1, a2], mm(T.pC[:, 512 * b:512 * b + 128], T.qE[:, 128 * b:128 * b + 128], T.sE[:, 128 * b:128 * b + 128],
+                                   XW[:, 256:384], XWs[:, 256:384], False, True)) for b in range(4)]
+        xd = [k["pl"], k["cp"]["X"], a1, a2]
+        x1 = do("v", xd, cp(oq[:, o + 256:o + 512].bitcast(U32), XW[:, 0:384].bitcast(U32).indirect(lo[:, 80:96])))
+        x2 = do("s", xd, act(os_[:, o + 256:o + 512], XWs[:, 0:384].indirect(lo[:, 80:96]), AF.Copy))
+        nw = []
+        for b in range(4):
+            i, h = T.pC[:, 512 * b + 64:512 * b + 128], NEW[:, b:256:4]
+            nw.append(do("v", [dc[b]], ts(h, i, 0.5, None, A.mult)) if b % 2 else do("s", [dc[b], st["prev"]], act(h, i, AF.Copy, scale=0.5)))
+        qn = do("v", [nw, K["NEW"]], quant(LN[:, 256:384], LNs[:, 256:384], NEW[:]))
+        return qn, nw, [x1, x2]
+
+    def renew_live(t, k, qn, oq, os_, o):
+        LN, LNs, lo = B("LN", t), B("LNs", t), B("lo16", t)
+        ld = [qn, k["pl"], k["cp"]["L"]]
+        l2 = do("s", ld, act(os_[:, o:o + 256], LNs[:, 0:384].indirect(lo[:, 64:80]), AF.Copy))
+        l1 = do("v", ld, cp(oq[:, o:o + 256].bitcast(U32), LN[:, 0:384].bitcast(U32).indirect(lo[:, 64:80])))
+        return [l1, l2]
+
+    def numbers(t, k):
+        LP, fo, wl = B("landP", t), B("fo", t), B("wl", t)
+        aP = ("aP%d" % t, arrive)
+        a = [do("v", [aP], red(fo[:, j:j + 1], LP[:, j:6:2])) for j in range(2)]
+        b = do("v", [a, k["w"]], tt(fo[:, 2:4], fo[:, 0:2], wl[:, 4:6], A.add))
+        for c in range(4):
+            dma("y", [b], T.lw[t:t + 1, 16 * c:16 * c + 16], fo[32 * c:32 * c + 16, 2:3])
+            dma("y", [b], T.sw[t:t + 1, 16 * c:16 * c + 16], fo[32 * c:32 * c + 16, 3:4])
+
+    ks = [{"sc": {}, "cp": {}} for t in range(ROUNDS)]
+    k = ks[0]
+    k["lt"], k["xt"], k["first"] = q_l, q_x, 0
+    for ty in range(2):
+        score(0, ty, (q_l, q_x)[ty], k)
+        copies(0, ty, (q_l, q_x)[ty], k["cp"])
+    for t in range(ROUNDS):
+        k = ks[t]
+        last = t + 1 == ROUNDS
+        order_and_send(t, k)
+        if t == 0:
+            consts_s()
+        prepare(t, k)
+        if t == 0:
+            consts_v()
+            rows()
+        else:
+            consts_2()
+            numbers(0, ks[0])
+        merge_and_send(t, k)
+        lists(t, k)
+        oq, os_, o = (T.FN, T.FNs, 0) if last else (B("SW", t + 1), B("SWs", t + 1), LB)
+        qn, nw, xt = renew(t, k, oq, os_, o)
+        if last:
+            lt = renew_live(t, k, qn, oq, os_, o)
+            dma("y", xt, T.oc[:, 1024:2048], T.FN[:, 256:512].bitcast(U8))
+            for q in range(4):
+                dma("y", xt, T.osc[4 * q:4 * q + 4, 256:512], T.FNs[32 * q:32 * q + 4, 256:512])
+            my = do("p", [lt, K["qW"], k["sc"][0][1]], mm(T.pA[:, 0:256], T.qW[:], T.sW[:], T.FN[:, 0:256], T.FNs[:, 0:256]))
+            dma("y", lt, T.oc[:, 0:1024], T.FN[:, 0:256].bitcast(U8))
+            for q in range(4):
+                dma("y", lt, T.osc[4 * q:4 * q + 4, 0:256], T.FNs[32 * q:32 * q + 4, 0:256])
+            yc = do("s", [my], act(T.yt[:], T.pA[:, 0:256], AF.Copy))
+            dma("s", [yc], T.y[:], T.yt[:])
+            numbers(t, k)
+        else:
+            n = ks[t + 1]
+            n["xt"], n["first"] = xt, 1
+            st["prev"] = [xt, nw, k["w"]]
+            copies(t + 1, 1, xt, n["cp"])
+            n["lt"] = lt = renew_live(t, k, qn, oq, os_, o)
+            score(t + 1, 1, xt, n)
+            copies(t + 1, 0, lt, n["cp"])
+            score(t + 1, 0, lt, n)
+            st["prev"] = [lt, xt, nw, k["w"]]
+    for s, n in cnt.items():
+        if top.get(s, 0) < n:
+            g.wait_ge(T.sem[s], n)

@@ -3,9 +3,12 @@ from concourse.mybir import dt, AluOpType as A, AxisListType, ActivationFunction
 
 F8 = "float8_e4m3fn_x4"
 TINY = 2.0 ** -118
-R16, R64 = 1.5 * 2.0 ** 27, 1.5 * 2.0 ** 29
+LIFT = 2.0 ** -100
+TOP = 2.0 ** 24
+R64 = 1.5 * 2.0 ** 29
 ROUNDS = 2
 LB, XB = 192, 448
+REMA, LAL, LBL, HPL, NUML, COLL, SEND, COLD, NUMD, HPD, LBD, LAD, REMB, FL1, FL2, ULL, ULD = range(17)
 
 SCRATCH = {
     "pA": ("psum", [128, 512], "float32"), "pB": ("psum", [128, 512], "float32"), "pC": ("psum", [128, 2048], "float32"),
@@ -14,33 +17,31 @@ SCRATCH = {
 for _n, _w, _d in (
         ("t_lv", 1024, "bfloat16"), ("t_dm", 1024, "bfloat16"), ("t_nz", 1024, "bfloat16"), ("t_w", 512, "bfloat16"),
         ("u0", 4, "bfloat16"), ("z0", 4, "bfloat16"), ("uz", 1024, "bfloat16"), ("qU", 256, F8), ("sU", 256, "uint8"),
-        ("qW", 128, F8), ("sW", 128, "uint8"), ("ones", 516, "bfloat16"), ("zer", 128, "bfloat16"),
+        ("qW", 128, F8), ("sW", 128, "uint8"), ("ones", 516, "bfloat16"), ("zer", 128, "bfloat16"), ("MK", 66, "bfloat16"),
         ("SS", 1024, "bfloat16"), ("SI", 1024, "bfloat16"), ("EM", 516, "bfloat16"), ("qS", 256, F8), ("sS", 256, "uint8"),
         ("qI", 256, F8), ("sI", 256, "uint8"), ("qE", 512, F8), ("sE", 512, "uint8"), ("NZ", 256, F8), ("NZs", 256, "uint8"),
-        ("pI", 1, "int32"), ("ii", 8, "int32"), ("fc", 8, "float32"), ("cc", 16, "float32"),
+        ("ii", 10, "int32"), ("fc", 32, "float32"), ("cf", 96, "float32"), ("cl", 32, "uint16"),
         ("tin", 256, "bfloat16"), ("Mneg", 256, "bfloat16"), ("Mtri", 256, "bfloat16"), ("Kn", 128, "bfloat16"), ("RC", 128, "bfloat16"),
-        ("sel", 4, "float32"), ("io8", 8, "float32"), ("dmp", 4, "float32"), ("io32", 32, "float32"), ("DG", 32, "bfloat16"),
-        ("sgt", 32, "float32"), ("VO", 64, "bfloat16"), ("OE", 8, "float32"), ("urow", 512, "bfloat16"),
-        ("yt", 256, "float32"), ("FN", 512, F8), ("FNs", 512, "uint8")):
+        ("dmp", 4, "float32"), ("DG", 64, "bfloat16"), ("DT", 16, "float32"), ("MS", 192, "float32"), ("IOTA", 512, "bfloat16"),
+        ("sgt", 32, "float32"), ("VO", 64, "bfloat16"), ("urow", 512, "bfloat16"),
+        ("yt", 256, "float32"), ("FN", 512, F8), ("FNs", 512, "uint8"),
+        ("qH", 256, F8), ("sH", 256, "uint8"), ("H", 1024, "bfloat16"), ("qG", 128, F8), ("sG", 128, "uint8"),
+        ("NEW", 512, "bfloat16"), ("VT", 192, "bfloat16"), ("sC", 4, "float32"), ("Vc", 512, "float32"), ("yd", 512, "float32"),
+        ("yo", 512, "float32"), ("DD", 1024, "bfloat16"), ("rk", 136, "float32"), ("trA", 256, "float32"), ("G", 192, "float32"),
+        ("trG", 192, "float32"), ("own", 8, "float32"), ("LM", 24, "float32"), ("XR", 832, "float32"), ("R", 1088, "float32"),
+        ("Dc", 2080, "bfloat16"), ("cs", 432, "float32"), ("sm", 48, "float32"), ("Mx", 256, "float32"), ("trU", 512, "bfloat16"),
+        ("so", 8, "uint16"), ("fm", 16, "bfloat16"), ("LF", 16, "bfloat16"), ("wl", 4, "float32"), ("wu", 2, "uint16"),
+        ("LP", 6, "uint16"), ("LQ", 16, "float32"), ("fo", 64, "float32"), ("F0", 2560, "bfloat16"), ("F1", 5248, "bfloat16")):
     SCRATCH[_n] = ("sbuf", [128, _w], _d)
-ONCE = ("yd", "yo", "DD", "Dc", "tr2", "trU", "qH", "sH", "H", "Gs", "sC", "Vc", "rk", "trA", "wk",
-        "VT", "XR", "R", "pw", "ow", "ix", "own", "NEW", "lo16", "qF", "sF", "qG", "sG")
 for _n, _w, _d in (
         ("SW", 704, F8), ("SWs", 704, "uint8"), ("LW", 704, F8), ("LWs", 704, "uint8"), ("XW", 384, F8), ("XWs", 384, "uint8"),
         ("LN", 384, F8), ("LNs", 384, "uint8"), ("PS", 64, F8), ("PSs", 64, "uint8"), ("NP", 128, F8), ("NPs", 128, "uint8"),
-        ("qH", 128, F8), ("sH", 128, "uint8"), ("qF", 128, F8), ("sF", 128, "uint8"), ("qG", 128, F8), ("sG", 128, "uint8"),
-        ("H", 512, "bfloat16"), ("F", 2560, "bfloat16"), ("NEW", 512, "bfloat16"), ("VT", 96, "bfloat16"),
-        ("sC", 4, "float32"), ("Vc", 512, "float32"), ("yd", 512, "float32"), ("yo", 512, "float32"), ("DD", 1024, "bfloat16"),
-        ("rk", 4, "float32"), ("trA", 128, "float32"), ("Gs", 64, "float32"), ("trG", 64, "float32"), ("dg", 4, "float32"), ("wk", 5, "float32"),
-        ("own", 2, "float32"), ("landM", 6, "float32"), ("landP", 6, "float32"), ("XR", 256, "float32"), ("R", 256, "float32"),
-        ("Dc", 1040, "bfloat16"), ("cn", 4, "float32"), ("pw", 8, "float32"), ("ow", 16, "float32"),
-        ("tr2", 256, "float32"), ("ix", 40, "float32"), ("UL", 704, "bfloat16"),
-        ("trU", 512, "bfloat16"), ("lo16", 128, "uint16"), ("wl", 8, "float32"), ("fo", 4, "float32")):
-    for _t in range(1 if _n in ONCE else ROUNDS):
+        ("qF", 128, F8), ("sF", 128, "uint8"), ("tr2", 256, "float32"), ("ix", 32, "float32"), ("UL", 704, "bfloat16"),
+        ("lo", 128, "uint16")):
+    for _t in range(ROUNDS):
         SCRATCH[_n + str(_t)] = ("sbuf", [128, _w], _d)
 
-SEMAPHORES = ["v", "s", "p", "gc", "ls"] + ["d%d" % k for k in range(80)] + \
-    [n + str(t) for n in ("aM", "aP", "aC") for t in range(ROUNDS)]
+SEMAPHORES = ["v", "s", "p", "gc", "ls", "out", "aM0", "aM1", "aM2", "aC0", "aC1", "aS0", "aS1", "aF", "aP"] + ["d%d" % k for k in range(60)]
 
 
 def rank_program(g, core, T, topo):
@@ -48,37 +49,67 @@ def rank_program(g, core, T, topo):
     if rank is None:
         return
     cores = list(T.cores)
-    others = [q for q in range(4) if q != rank]
+    others = [rank ^ d for d in (3, 1, 2)]
     Q = {"v": g.vector, "s": g.scalar, "p": g.tensor, "gc": g, "y": g.sync}
-    cnt, seen, top, nd = {}, {}, {}, [0]
+    cnt, top, nd = {}, {}, [0]
+    know = {q: {} for q in Q}
+    behind = {}
+
+    def flat(deps, out):
+        for d in deps:
+            if isinstance(d, list):
+                flat(d, out)
+            elif d is not None:
+                out[d[0]] = max(out.get(d[0], 0), d[1])
+        return out
 
     def need(qn, deps):
-        for d in deps:
-            if d is None:
+        want = flat(deps, {})
+        for s, n in want.items():
+            if know[qn].get(s, 0) >= n or any(behind.get(o, {}).get(s, 0) >= n for o in want.items() if o[0] != s):
                 continue
-            if isinstance(d, list):
-                need(qn, d)
-            elif seen.get((qn, d[0]), 0) < d[1]:
-                Q[qn].wait_ge(T.sem[d[0]], d[1])
-                seen[(qn, d[0])] = d[1]
-                top[d[0]] = max(top.get(d[0], 0), d[1])
+            Q[qn].wait_ge(T.sem[s], n)
+            top[s] = max(top.get(s, 0), n)
+        for s, n in want.items():
+            for a, b in list(behind.get((s, n), {}).items()) + [(s, n)]:
+                know[qn][a] = max(know[qn].get(a, 0), b)
+
+    def token(qn, s, n, step):
+        cnt[s] = n
+        k = dict(behind.get((s, n - step), {}))
+        for a, b in know[qn].items():
+            k[a] = max(k.get(a, 0), b)
+        behind[(s, n)] = k
+        return (s, n)
 
     def do(qn, deps, f):
         need(qn, deps)
         f(Q[qn]).then_inc(T.sem[qn], 1)
-        cnt[qn] = cnt.get(qn, 0) + 1
-        return (qn, cnt[qn])
+        return token(qn, qn, cnt.get(qn, 0) + 1, 1)
 
-    def dma(qn, deps, out, in_):
+    side = [False]
+
+    def gp(deps, f, upper=False):
+        if upper != side[0]:
+            deps = [deps, ("gc", cnt["gc"])]
+            side[0] = upper
+        return do("gc", deps, f)
+
+    def dma(qn, deps, out, in_, s=None):
         need(qn, deps)
+        if s is None:
+            s = "d%d" % nd[0]
+            nd[0] += 1
+        Q[qn].dma_start(out, in_).then_inc(T.sem[s], 16)
+        return token(qn, s, cnt.get(s, 0) + 16, 16)
+
+    def group(qn, deps, pairs):
         s = "d%d" % nd[0]
         nd[0] += 1
-        Q[qn].dma_start(out, in_).then_inc(T.sem[s], 16)
-        cnt[s] = 16
-        return (s, 16)
+        return [dma(qn, deps, o, i, s) for o, i in pairs][-1]
 
     def B(n, t):
-        return T[n + ("0" if n in ONCE else str(t))]
+        return T[n + str(t)]
 
     dst = [cores[q] for q in others]
     far = [c for c in dst if topo.chip(c) != topo.chip(core)]
@@ -90,19 +121,19 @@ def rank_program(g, core, T, topo):
     for c in dst:
         if c not in eng:
             eng[c] = [e for e in topo.engines(core, c) if e not in fe][::len(far)]
-    arrive = sum(len(e) for e in eng.values())
+    each = len(eng[dst[0]])
 
-    def send(deps, sem, view, land):
+    def send(deps, sem, view, land, to=(0, 1, 2)):
         need("gc", deps)
         tr = []
-        for q, c in zip(others, dst):
-            rid, pid, _ = topo.addr(c)
-            s = [x for x in range(4) if x != q].index(rank)
-            tr.append(RemoteDMATransfer(dst_ids=[DstId(rid=rid, pnc=pid)], dma_engine_mask=sum(1 << e for e in eng[c]),
-                                        remote_sem=T.sem[sem], src=view, dst=land(s)))
+        for s in to:
+            rid, pid, _ = topo.addr(dst[s])
+            tr.append(RemoteDMATransfer(dst_ids=[DstId(rid=rid, pnc=pid)], dma_engine_mask=sum(1 << e for e in eng[dst[s]]),
+                                        remote_sem=T.sem[sem], src=view(s), dst=land(s)))
         g.remote_dma_fused(tr, local_sem=T.sem["ls"])
-        cnt["ls"] = cnt.get("ls", 0) + arrive
-        cnt[sem] = cnt.get(sem, 0) + arrive
+        cnt["ls"] = cnt.get("ls", 0) + each * len(to)
+        cnt[sem] = cnt.get(sem, 0) + each * len(to)
+        return (sem, cnt[sem])
 
     def ts(o, i, s1, s2, *ops):
         if len(ops) == 1:
@@ -121,6 +152,9 @@ def rank_program(g, core, T, topo):
     def red(o, i):
         return lambda q: q.tensor_reduce(o, i, AxisListType.X, A.add)
 
+    def scan(o, a, b, first):
+        return lambda q: q.tensor_tensor_scan(o, a, b, first, A.add, A.add)
+
     def trn(o, i):
         return lambda q: q.transpose(o, i)
 
@@ -137,47 +171,54 @@ def rank_program(g, core, T, topo):
         return lambda q: q.matmul_mx(o, a, sa, b, sb, st, sp)
 
     U8, U32 = dt.uint8, dt.uint32
-
-    def after(p0):
-        return ("gc", cnt["gc"]) if p0 else None
+    SW0, SWs0 = B("SW", 0), B("SWs", 0)
+    K = {}
+    F_ = lambda c: T.fc[:, c:c + 1]
+    C_ = lambda c: T.fc[:, 10 + c:11 + c]
+    SG, M1, M0, SM1, SM0, AQ, H1, EV, OD, TM, CM, E4, TM1, TM0, SG4, EX0, EX1, EX2, ST = range(19)
+    io64, io8, OE, OE2, rep, vtb = T.cf[:, 0:64], T.cf[:, 64:72], T.cf[:, 72:78], T.cf[:, 78:80], T.cf[:, 80:92], T.cf[:, 92:96]
+    REP, VTL, EXL = T.cl[:, 0:12], T.cl[:, 12:16], T.cl[:, 16:17]
+    VT, own, XR, R, Dc, cs, sm, Mx = T.VT, T.own, T.XR, T.R, T.Dc, T.cs, T.sm, T.Mx
+    so, G, trA, trG, LM = T.so, T.G, T.trA, T.trG, T.LM
+    sC, Vc, yd, DD, rk, H = T.sC, T.Vc, T.yd, T.DD, T.rk, T.H
 
     d_u = dma("s", [], T.u0[:], T.u[:, 0:4])
     d_z = dma("s", [], T.z0[:], T.z[:, 0:4])
     d_lv = dma("y", [], T.t_lv[:], T.lv[:])
     d_dm = dma("y", [], T.t_dm[:], T.dm[:])
-    d_nz = dma("y", [], T.t_nz[:], T.nz[:])
-    d_w = dma("y", [], T.t_w[:], T.w[:])
 
-    K = {}
-    i_p = do("gc", [], lambda q: q.iota(T.pI[:], [[0, 1]], 0, 1))
-    v_zer = do("v", [], fill(T.zer[:], 0.0))
+    i_p = gp([], lambda q: q.iota(T.ii[:, 9:10], [[0, 1]], 0, 1))
     v_tin = do("v", [], fill(T.tin[:], TINY))
+    v_zer = do("v", [], fill(T.zer[:], 0.0))
+    v_si = [do("v", [], fill(T.SI[:, o:o + 128], 0.0)) for o in (0, 512)]
+    v_mk = do("v", [], fill(T.MK[:], 1.0))
     bits = []
-    for c, m in enumerate((15, 32, 64, 63, 48, 112, 16)):
-        bits.append(do("v", [i_p], ts(T.ii[:, c:c + 1], T.pI[:, 0:1], m, None, A.bitwise_and)))
-    v_fc = do("v", bits, cp(T.fc[:, 0:7], T.ii[:, 0:7]))
+    for c, m in enumerate((15, 32, 64, 63, 48, 112, 16, 3, 12)):
+        bits.append(do("v", [i_p], ts(T.ii[:, c:c + 1], T.ii[:, 9:10], m, None, A.bitwise_and)))
     v_one = do("v", [], fill(T.ones[:], 1.0))
-    v_ss = do("v", [], fill(T.SS[:], 0.0))
-    v_si = do("v", [], fill(T.SI[:], 0.0))
-    i_mn = do("gc", [v_tin], lambda q: q.affine_select(T.Mneg[:], T.tin[:], [[0, 2], [1, 128]], A.is_ge, -TINY, 0, -1))
-    i_mt = do("gc", [v_tin], lambda q: q.affine_select(T.Mtri[:], T.tin[:], [[0, 2], [-1, 128]], A.is_gt, -TINY, 0, 1))
-    i_kn = do("gc", [], iota(T.Kn[:], [[16, 4], [0, 2], [1, 16]]))
-    K["io32"] = do("gc", [], iota(T.io32[:], [[0, 2], [1, 16]]))
-    K["io8"] = do("gc", [], iota(T.io8[:], [[16, 8]]))
-    K["OE"] = [do("gc", [], iota(T.OE[:, 0:6], [[1, 3], [64, 2]], 542)), do("gc", [], iota(T.OE[:, 6:8], [[64, 2]], 32))]
-    K["EM"] = do("gc", [v_one], lambda q: q.affine_select(T.EM[:], T.ones[:], [[1, 516]], A.is_equal, 0.0, -3, -4))
-    K["SI"] = [v_si]
-    for p0, p1, at, end, step, c in ((0, 128, 0, 512, 32, 1), (0, 128, 1, 512, 32, 1), (0, 128, 2, 512, 32, 1), (0, 64, 4, 512, 32, 1), (0, 64, 5, 512, 64, 2),
-                                     (0, 64, 37, 512, 64, 1), (0, 64, 6, 512, 64, 1), (0, 64, 38, 512, 128, 1), (0, 1, 15, 512, 32, 1), (0, 64, 526, 1024, 128, 1),
-                                     (64, 128, 8, 512, 32, 1), (64, 128, 9, 512, 64, 2), (64, 128, 41, 512, 64, 1), (64, 128, 10, 512, 32, 1),
-                                     (64, 128, 558, 1024, 128, 1), (64, 65, 15, 512, 32, 1)):
-        K["SI"].append(do("gc", [v_si, after(p0)], iota(T.SI[p0:p1, at:end:step], [[0, len(range(at, end, step))]], c)))
-    K["177"] = [do("gc", [K["SI"]], iota(B("Dc", 0)[:, 208 * j + 193:208 * j + 194], [[0, 1]], 177)) for j in range(2)]
-    F_ = lambda c: T.fc[:, c:c + 1]
-    C_ = lambda c: T.cc[:, c:c + 1]
-    SG, M1, M0, SM1, SM0, AQ, CD, H1, EV, OD, OB = range(11)
+    v_fc = do("v", bits, cp(T.fc[:, 0:9], T.ii[:, 0:9]))
+    v_mk = do("v", [v_mk], fill(T.MK[:, 2:66:32], 0.0))
+    z_f = do("v", [], fill(T.F0[:, 0:1024], 0.0))
+    v_ss = [do("s", [v_tin], act(T.SS[:, 256 * j:256 * j + 256], T.tin[:], AF.Copy, scale=0.0)) for j in range(4)]
+    i_mn = gp([v_tin], lambda q: q.affine_select(T.Mneg[:], T.tin[:], [[0, 2], [1, 128]], A.is_ge, -TINY, 0, -1))
+    i_kn = gp([], iota(T.Kn[:], [[16, 4], [0, 2], [1, 16]]))
+    K["io"] = [gp([], iota(io64, [[0, 4], [1, 16]])), gp([], iota(rep, [[1, 6], [0, 2]])),
+               gp([], iota(vtb, [[-1, 2], [0, 2]], 2)), gp([], iota(OE, [[-1, 3], [64, 2]], 544))]
+    si = []
+    L_, D_, N_ = (0, 64), (64, 128), (0, 128)
+    for (p0, p1), r0, r1, e, c, step in (
+            (N_, FL1, FL2, 2, 1, 1), (N_, REMA, LBL, 3, 1, 0), (N_, LBD, FL1, 3, 1, 0),
+            (L_, HPL, SEND, 0, 1, 0), (L_, HPL, SEND, 1, 1, 0), (L_, COLL, SEND, 2, 3, 0), (L_, LAL, LBL, 2, 3, 1), (L_, NUML, NUML, 2, 4 * rank, 0),
+            (L_, REMA, LBL, 514, 1, 0), (L_, ULL, None, 0, 1, 1),
+            (D_, SEND, HPD, 0, 1, 0), (D_, SEND, HPD, 1, 1, 0), (D_, SEND, COLD, 2, 7, 0), (D_, LBD, LAD, 2, 4, -1), (D_, NUMD, NUMD, 2, 4 * rank, 0),
+            (D_, LBD, REMB, 514, 1, 0), (D_, ULD, None, 0, 1, 1)):
+        if r1 is None:
+            si.append(gp([v_si], iota(T.SI[p0:p1, 4 * r0:4 * r0 + 3], [[step, 3]], c), p0 > 0))
+        elif c:
+            si.append(gp([v_si], iota(T.SI[p0:p1, 4 * r0 + e:4 * r1 + e + 1:4], [[step, r1 - r0 + 1]], c), p0 > 0))
+    K["EM"] = gp([v_one], lambda q: q.affine_select(T.EM[:], T.ones[:], [[1, 516]], A.is_equal, 0.0, -3, -4))
+    K["io2"] = [gp([], iota(io8, [[16, 8]])), gp([], iota(OE2, [[64, 2]], 32))]
 
-    SW0, SWs0 = B("SW", 0), B("SWs", 0)
     uz, cst = [], []
     for c, src, a, b in ((H1, 5, 1.0, 128.0), (AQ, 2, 4.0, 0.0), (SG, 2, -1 / 32, 1.0)):
         cst.append(do("s", [v_fc], act(C_(c), F_(src), scale=a, bias=b)))
@@ -186,299 +227,386 @@ def rank_program(g, core, T, topo):
     for b in range(4):
         uz.append(do("s", [d_z, v_zer], act(T.uz[:, 512 + b:1024:4], T.zer[:], bias=T.z0[:, b:b + 1])))
     q_u = [do("v", uz[0:4], quant(T.qU[:, 0:128], T.sU[:, 0:128], T.uz[:, 0:512]))]
+    K["DG"] = do("v", [K["io"], v_fc], ts(T.DG[:], io64, F_(0), None, A.is_equal))
+    K["cl"] = [do("v", [K["io"]], cp(REP, rep)), do("v", [K["io"], v_fc], ts(VTL, vtb, F_(4), F_(4), A.add, A.add))]
     q_l = do("v", [d_lv], quant(SW0[:, LB:XB], SWs0[:, LB:XB], T.t_lv[:]))
     q_u.append(do("v", uz[4:8], quant(T.qU[:, 128:256], T.sU[:, 128:256], T.uz[:, 512:1024])))
-    q_x = do("v", [d_dm], quant(SW0[:, XB:704], SWs0[:, XB:704], T.t_dm[:]))
     sst = []
     for b in range(4):
         t, h = divmod(b, 2)
         hi = C_(H1) if h else F_(5)
-        sst.append(do("s", [v_ss, v_one, v_fc], act(T.SS[:, 256 * t + b:256 * t + 256:4], T.ones[:, 0:64], AF.Copy, scale=F_(0))))
-        sst.append(do("s", [cst], act(T.SS[:, 512 + 256 * t + b:768 + 256 * t:4], T.ones[:, 0:64], AF.Copy, scale=hi)))
-    K["DG"] = do("v", [K["io32"], v_fc], ts(T.DG[:], T.io32[:], F_(0), None, A.is_equal))
-    K["sel"] = do("v", [K["io8"]], ts(T.sel[:], T.io8[:, 0:4], F_(4), None, A.is_equal))
+        sst.append(do("s", [v_ss, v_mk, v_fc], act(T.SS[:, 256 * t + b:256 * t + 256:4], T.MK[:, 0:64], AF.Copy, scale=F_(0))))
+        sst.append(do("s", [cst], act(T.SS[:, 512 + 256 * t + b:768 + 256 * t:4], T.MK[:, 1:65], AF.Copy, scale=hi)))
+    i_mt = do("s", [i_mn], act(T.Mtri[:], T.Mneg[:], AF.Copy, scale=-1.0))
     v_qs = do("v", sst, quant(T.qS[:], T.sS[:], T.SS[:]))
-
-    def consts_s():
-        for c, src, a, b in ((M1, 1, 1 / 32, 0.0), (M0, 1, -1 / 32, 1.0), (CD, 2, 4.0, float(LB)),
-                             (EV, 6, -1 / 16, 1.0), (OD, 6, 1 / 16, 0.0), (OB, 6, -16.0, 0.0)):
-            cst.append(do("s", [v_fc], act(C_(c), F_(src), scale=a, bias=b)))
-        cst.append(do("s", [cst], act(C_(SM1), C_(M1), scale=C_(SG))))
-        cst.append(do("s", [], act(C_(SM0), C_(M0), scale=C_(SG))))
-        K["sgt"] = do("s", [v_one], act(T.sgt[:], T.ones[:, 0:32], AF.Copy, scale=C_(SG)))
-        Dc = B("Dc", 0)
-        K["Dc"] = K["177"] + [do("s", [], act(Dc[:, 816:817], F_(3), scale=4.0, bias=-30.0))]
-        for j in range(2):
-            K["Dc"].append(do("s", [], act(Dc[:, 208 * j + 192:208 * j + 193], F_(3), scale=2.0)))
-        K["wk"] = do("v", [], fill(B("wk", 0)[:, 4:5], -7.5))
-        K["VTc"] = do("v", [K["DG"], cst], ts(B("VT", 0)[:, 64:96], T.DG[:], C_(CD), None, A.mult))
-
-    def slots(t):
-        F = B("F", t)
-        z = do("v", [], fill(F[:, 0:1024], 0.0))
-        return [z, do("gc", [z], iota(F[0:64, 515:1024:4], [[0, 4], [0, 2], [1, 16]])),
-                do("gc", [z, after(64)], iota(F[64:128, 515:1024:4], [[16, 4], [0, 2], [0, 16]]))]
-
-    def consts_v():
-        K["F"] = [slots(0)]
-        K["VO"] = [do("v", [K["DG"]], ts(T.VO[:, 32 * s:32 * s + 32], T.DG[:], 64.0 * (s + 1), None, A.mult)) for s in range(2)]
-        K["nz"] = do("v", [d_nz], quant(T.NZ[:], T.NZs[:], T.t_nz[:]))
-        K["dmp"] = do("v", [K["io8"]], ts(T.dmp[:], T.io8[:, 0:8:2], F_(0), None, A.add))
-        K["qE"] = [do("v", [K["EM"]], quant(T.qE[:, 128 * b:128 * b + 128], T.sE[:, 128 * b:128 * b + 128], T.EM[:, 3 - b:515 - b])) for b in range(4)]
-        K["np"] = [do("v", [d_nz], quant(B("NP", 0)[:], B("NPs", 0)[:], T.t_nz[:, 0:512]))]
-        K["NEW"] = do("v", [], fill(B("NEW", 0)[:, 256:512], 0.0))
-        K["qI"] = do("v", K["SI"], quant(T.qI[:], T.sI[:], T.SI[:]))
-
-    def rows():
-        K["RC"] = do("gc", K["F"][0], iota(T.RC[:], [[16, 4], [0, 2], [1, 16]], 128))
-        K["ur"] = do("gc", [], iota(T.urow[:], [[16, 16], [0, 2], [1, 16]], -128))
-        for t in range(ROUNDS):
-            K["U%d" % t] = dma("y", [K["ur"]], B("UL", t)[:, 192:704], T.urow[:])
-
-    def consts_2():
-        K["F"].append(slots(1))
-        K["qW"] = do("v", [d_w], quant(T.qW[:], T.sW[:], T.t_w[:]))
-        K["np"].append(do("v", [d_nz], quant(B("NP", 1)[:], B("NPs", 1)[:], T.t_nz[:, 0:512])))
-
-    st = {"prev": []}
+    q_x = do("v", [d_dm], quant(SW0[:, XB:704], SWs0[:, XB:704], T.t_dm[:]))
+    d_nz = dma("y", [d_dm], T.t_nz[:], T.nz[:])
+    d_w = dma("y", [], T.t_w[:], T.w[:])
+    d_si = group("y", si, [(T.SI[:, o + 128 * j:o + 128 * j + 128], T.SI[:, o:o + 128]) for o in (0, 512) for j in (1, 2, 3)])
 
     def copies(t, x, dep, r):
         SW, SWs = B("SW", t), B("SWs", t)
         c0 = XB if x else LB
-        for dn, o, key in ((("XW", 0, "X"), ("LW", XB, "W")) if x else (("LN", 0, "L"), ("LW", LB, "W"))):
-            r.setdefault(key, []).append(dma("y", [dep], B(dn, t)[:, o:o + 256].bitcast(U8), SW[:, c0:c0 + 256].bitcast(U8)))
-            r[key].append(dma("y", [dep], B(dn + "s", t)[:, o:o + 256], SWs[:, c0:c0 + 256]))
+        for dn, o, key in ((("LW", XB, "W"), ("XW", 0, "X")) if x else (("LW", LB, "W"), ("LN", 0, "L"))):
+            r.setdefault(key, []).append(group("y", [dep], [(B(dn, t)[:, o:o + 256].bitcast(U8), SW[:, c0:c0 + 256].bitcast(U8)),
+                                                            (B(dn + "s", t)[:, o:o + 256], SWs[:, c0:c0 + 256])]))
 
-    def score(t, ty, tk, k):
-        SW, SWs, sC, Vc, yd = (B(n, t) for n in ("SW", "SWs", "sC", "Vc", "yd"))
-        pr, w = st["prev"], LB + 256 * ty
+    sco = []
+    for ty in range(2):
+        w = LB + 256 * ty
         qu, su = T.qU[:, 128 * ty:128 * ty + 128], T.sU[:, 128 * ty:128 * ty + 128]
         pX, pY = ((T.pA, T.pC), (T.pB, T.pD))[ty]
-        r = do("p", [q_u[ty], tk, pr], mm(pX[:, 0:256], qu, su, SW[:, w:w + 256], SWs[:, w:w + 256]))
+        r = do("p", [q_u[ty], (q_l, q_x)[ty]], mm(pX[:, 0:256], qu, su, SW0[:, w:w + 256], SWs0[:, w:w + 256]))
         for h in range(2):
-            c = do("p", [], mm(pY[:, 512 * h:512 * h + 128], SW[:, w + 128 * h:w + 128 * h + 128],
-                               SWs[:, w + 128 * h:w + 128 * h + 128], qu, su))
-        ra = do("s", [r, pr], act(Vc[:, 256 * ty:256 * ty + 256], pX[:, 0:256], AF.Abs))
-        ca = do("s", [c], act(sC[:, 2 * ty:2 * ty + 2], pY[:, 0:1024:512], AF.Abs))
+            c = do("p", [], mm(pY[:, 512 * h:512 * h + 128], SW0[:, w + 128 * h:w + 128 * h + 128],
+                               SWs0[:, w + 128 * h:w + 128 * h + 128], qu, su))
+        ra = do("s", [r], act(Vc[:, 256 * ty:256 * ty + 256], pX[:, 0:256], AF.Abs, bias=LIFT))
+        ca = do("s", [c], act(sC[:, 2 * ty:2 * ty + 2], pY[:, 0:1024:512], AF.Abs, bias=LIFT))
         ys = [do("s", [ca, ra], act(yd[:, 256 * ty + 128 * h:256 * ty + 128 * h + 128], Vc[:, 256 * ty + 128 * h:256 * ty + 128 * h + 128],
                                     bias=sC[:, 2 * ty + h:2 * ty + h + 1], scale=-1.0)) for h in range(2)]
-        k["sc"][ty] = (ca, ra, ys)
+        sco.append((ca, ra, ys))
+    cps = [{}, {}]
+    copies(0, 0, q_l, cps[0])
+    copies(0, 1, q_x, cps[0])
+    K["np"] = group("y", [q_l], [p for t in range(ROUNDS) for p in ((B("NP", t)[:, 0:64].bitcast(U8), SW0[:, LB:LB + 64].bitcast(U8)),
+                                                                    (B("NPs", t)[:, 0:64], SWs0[:, LB:LB + 64]))])
 
-    def ahead(t, ty, k):
-        sC, Vc, yd, DD = (B(n, t) for n in ("sC", "Vc", "yd", "DD"))
-        ca, ra, ys = k["sc"][ty]
+    def ahead(ty):
+        ca, ra, ys = sco[ty]
         o = 512 * ty
         f0, f1, f2 = ((A.is_lt, A.is_le, A.is_gt), (A.is_gt, A.is_ge, A.is_lt))[ty]
-        a = do("v", [ca, ra, st["prev"]], ts(DD[:, o:o + 128], Vc[:, 256 * ty + 128:256 * ty + 256], sC[:, 2 * ty:2 * ty + 1], None, f0))
+        a = do("v", [ca, ra], ts(DD[:, o:o + 128], Vc[:, 256 * ty + 128:256 * ty + 256], sC[:, 2 * ty:2 * ty + 1], None, f0))
         b = do("v", [ca, ra], ts(DD[:, o + 384:o + 512], Vc[:, 256 * ty:256 * ty + 128], sC[:, 2 * ty + 1:2 * ty + 2], None, f1))
         d = do("v", [ys, i_mn, i_mt], tt(DD[:, o + 128:o + 384], yd[:, 256 * ty:256 * ty + 256], (T.Mneg, T.Mtri)[ty][:], f2))
         return [a, b, d]
 
-    def order_and_send(t, k):
-        Vc, DD, rk, H = (B(n, t) for n in ("Vc", "DD", "rk", "H"))
-        pr, r = st["prev"], {}
+    rr = {}
+    rcol = [[rk[:, c:c + 1] for c in (132, 133, 134, 131)], [rk[:, c:c + 1] for c in (1, 2, 3, 0)]]
 
-        def hot(b):
-            return do("v", [r[b], i_kn, pr], ts(H[:, b:512:4], T.Kn[:], rk[:, b:b + 1], None, A.is_equal))
+    def total(b, dd):
+        rr[b] = do("s", dd, act(DD[:, 256 * b:256 * b + 256], DD[:, 256 * b:256 * b + 256], accum_out=rcol[0][b]))
 
-        def total(b, dd):
-            r[b] = do("s", dd, act(DD[:, 256 * b:256 * b + 256], DD[:, 256 * b:256 * b + 256], accum_out=rk[:, b:b + 1]))
+    dd = ahead(0)
+    total(0, dd)
+    total(1, dd)
+    dd = ahead(1)
+    total(2, dd)
+    rr[3] = do("v", dd, scan(rk[:, 4:132], DD[:, 768:896], DD[:, 896:1024], 0.0))
+    rk2 = do("s", [list(rr.values())], act(rk[:, 0:4], rk[:, 131:135], bias=-64.0))
+    srt = [{}, {}]
 
-        f, l = k["first"], 1 - k["first"]
-        dd = ahead(t, f, k)
-        total(2 * f, dd)
-        total(2 * f + 1, dd)
-        dd = ahead(t, l, k)
-        total(2 * l, dd)
-        r[2 * l + 1] = do("v", dd, red(rk[:, 2 * l + 1:2 * l + 2], DD[:, 512 * l + 256:512 * l + 512]))
-        hs = [hot(b) for b in (2 * f, 2 * f + 1, 2 * l + 1, 2 * l)]
-        qh = do("v", hs, quant(B("qH", t)[:], B("sH", t)[:], H[:]))
-        do("p", [qh, v_qs, pr], mm(T.pD[:, 0:128], T.qS[:, 0:128], T.sS[:, 0:128], B("qH", t)[:], B("sH", t)[:], True, False))
-        m = do("p", [], mm(T.pD[:, 0:128], T.qS[:, 128:256], T.sS[:, 128:256], B("qH", t)[:], B("sH", t)[:], False, True))
-        trA, lo, G, trG = B("trA", t), B("lo16", t), B("Gs", t), B("trG", t)
-        k["trA"] = a = do("v", [m], trn(trA[:], T.pD[:, 0:128]))
-        of = do("v", [a, cst[1]], ts(lo[:, 0:4], trA[:, 0:128:32], C_(AQ), None, A.add))
-        gs = do("v", [of, k["sc"][0][1], k["sc"][1][1], pr], cp(G[:], Vc[:, 0:512].indirect(lo[:, 0:4])))
-        k["M"] = tg = do("v", [gs], trn(trG[:], G[:]))
-        send([tg], "aM%d" % t, trG[:, 31:33], lambda s: B("landM", t)[:, 2 * s:2 * s + 2])
+    def hot(j, dep):
+        hs = [do("v", [dep(b), i_kn], ts(H[:, 512 * j + b:512 * j + 512:4], T.Kn[:], rcol[j][b], None, A.is_equal)) for b in (0, 1, 3, 2)]
+        qH, sH = T.qH[:, 128 * j:128 * j + 128], T.sH[:, 128 * j:128 * j + 128]
+        qh = do("v", hs, quant(qH, sH, H[:, 512 * j:512 * j + 512]))
+        pX = (T.pD, T.pA)[j]
+        do("p", [qh, v_qs], mm(pX[:, 0:128], T.qS[:, 0:128], T.sS[:, 0:128], qH, sH, True, False))
+        srt[j]["m"] = do("p", [], mm(pX[:, 0:128], T.qS[:, 128:256], T.sS[:, 128:256], qH, sH, False, True))
 
-    def prepare(t, k):
-        own, wk, dg, VT, trA, trG, XR = (B(n, t) for n in ("own", "wk", "dg", "VT", "trA", "trG", "XR"))
-        w = do("v", [k["trA"], K["sel"]], tt(wk[:, 0:4], trA[:, 0:128:32], T.sel[:], A.mult))
-        a = do("v", [k["M"], cst], ts(own[:, 1:2], trG[:, 32:33], C_(SM1), None, A.mult))
-        pl = do("v", [w, K["wk"]], red(dg[:, 0:1], wk[:]))
-        k["s"] = do("v", [a], ts(own[:, 0:1], trG[:, 31:32], C_(SM0), own[:, 1:2], A.mult, A.add))
-        hi = do("v", [pl], ts(dg[:, 1:2], dg[:, 0:1], R16, R16, A.add, A.subtract))
-        xo = [do("s", [k["M"], K["sgt"]], act(XR[:, 192 + 32 * j:224 + 32 * j], T.sgt[:], AF.Copy, scale=trG[:, 31 + j:32 + j])) for j in range(2)]
-        v1 = do("v", [hi], ts(VT[:, 32:64], T.DG[:], dg[:, 1:2], None, A.mult))
-        lo_ = do("v", [hi], ts(dg[:, 2:3], dg[:, 0:1], dg[:, 1:2], 7.5, A.subtract, A.add))
-        k["Ro"] = do("v", xo, trn(B("R", t)[:, 192:256], XR[:, 192:256]))
-        v0 = do("v", [lo_], ts(VT[:, 0:32], T.DG[:], dg[:, 2:3], None, A.mult))
-        k["VT"] = [v0, v1, K["VTc"]]
+    def sorted_(j):
+        k = srt[j]
+        k["trA"] = a = do("v", [k["m"]], trn(trA[:, 128 * j:128 * j + 128], (T.pD, T.pA)[j][:, 0:128]))
+        k["of"] = of = do("v", [a, cst[1]], ts(so[:, 4 * j:4 * j + 4], trA[:, 128 * j:128 * j + 128:32], C_(AQ), None, A.add))
+        k["G"] = gs = do("v", [of], cp(G[:, 64 * j:64 * j + 64], Vc[:, 0:512].indirect(so[:, 4 * j:4 * j + 4])))
+        k["M"] = tg = do("v", [gs], trn(trG[:, 64 * j:64 * j + 64], G[:, 64 * j:64 * j + 64]))
+        k["a"] = send([tg], "aM%d" % j, lambda s: trG[:, 64 * j + 31:64 * j + 33], lambda s: LM[:, 8 * j + 2 * s:8 * j + 2 * s + 2])
 
-    def before(s, q, t, deps, at, x_of, neg=None):
-        R, Dc, out, seg = B("R", t), B("Dc", t), [], []
+    hot(0, lambda b: rr[b])
+    K["MS"] = []
+    for s in range(3):
+        low = others[s] < rank
+        if s and low == (others[s - 1] < rank):
+            continue
+        e = s + 1
+        while e < 3 and (others[e] < rank) == low:
+            e += 1
+        K["MS"].append(do("v", [], fill(T.MS[0:64, 64 * s:64 * e], TOP - 1 if low else TOP)))
+        K["MS"].append(do("v", [], fill(T.MS[64:128, 64 * s:64 * e], -TOP if low else 1 - TOP)))
+    for c, src, a, b in ((M1, 1, 1 / 32, 0.0), (M0, 1, -1 / 32, 1.0), (ST, 2, -TOP / 32, TOP), (E4, 3, 4.0, -30.0), (EV, 6, -1 / 16, 1.0), (OD, 6, 1 / 16, 0.0),
+                         (SG4, 2, -1 / 128, 0.25), (EX0, 2, REMB / 64, 0.0)):
+        cst.append(do("s", [v_fc], act(C_(c), F_(src), scale=a, bias=b)))
+    c1 = [do("s", [cst], act(C_(TM), F_(2), scale=1 / 64, bias=C_(ST)))]
+    for c, a, b in ((SM1, M1, SG), (SM0, M0, SG)):
+        c1.append(do("s", [], act(C_(c), C_(a), scale=C_(b))))
+    ex = do("s", [], act(C_(EX1), F_(7), scale=32.0, bias=C_(EX0)))
+    K["sgt"] = do("s", [v_one], act(T.sgt[:], T.ones[:, 0:32], AF.Copy, scale=C_(SG)))
+    K["mark"] = [do("s", [K["DG"]], act(VT[:, 96 * j:96 * j + 32], T.DG[:, 0:32], AF.Copy, scale=64.0)) for j in range(2)]
+    for c, a, b in ((TM1, M1, TM), (TM0, M0, TM)):
+        cst.append(do("s", [c1], act(C_(c), C_(a), scale=C_(b))))
+    cst.append(do("s", [], act(C_(CM), C_(TM), bias=-1.0)))
+    ex = do("s", [ex], act(C_(EX2), F_(8), scale=C_(SG4), bias=C_(EX1)))
+    sorted_(0)
+
+    K["177"] = [gp([], iota(Dc[:, 208 * j + 193:208 * j + 194], [[0, 1]], 177)) for j in range(2)]
+    K["F"] = [gp([z_f], iota(T.F0[0:1, 515:1024:4], [[0, 4], [0, 2], [1, 16]])),
+              gp([z_f], iota(T.F0[64:65, 515:1024:4], [[16, 4], [0, 2], [0, 16]]), True)]
+    d_f1 = dma("y", K["F"], T.F1[:, 512:1024], T.F0[:, 512:1024])
+    K["qE"] = []
+
+    def unpack(b):
+        K["qE"].append(do("v", [K["EM"]], quant(T.qE[:, 128 * b:128 * b + 128], T.sE[:, 128 * b:128 * b + 128], T.EM[:, 3 - b:515 - b])))
+
+    def digits(j):
+        return do("v", [srt[j]["trA"], K["cl"], K["DG"]], tt(VT[:, 96 * j + 32:96 * j + 96], trA[:, 128 * j:128 * j + 128].indirect(VTL), T.DG[:], A.mult))
+
+    def mine(j, o):
+        a = do("s", [srt[j]["M"], cst], act(own[:, o + 1:o + 2], trG[:, 64 * j + 32:64 * j + 33], scale=C_(TM1)))
+        return do("s", [a], act(own[:, o:o + 1], trG[:, 64 * j + 31:64 * j + 32], scale=C_(TM0), bias=own[:, o + 1:o + 2]))
+
+    s_a = mine(0, 0)
+    xo = [do("s", [K["sgt"]], act(XR[:, 192 + 32 * j:224 + 32 * j], T.sgt[:], AF.Copy, scale=trG[:, 31 + j:32 + j])) for j in range(2)]
+    K["VO"] = [do("s", [K["DG"]], act(T.VO[:, 32 * s:32 * s + 32], T.DG[:, 0:32], AF.Copy, scale=64.0 * (s + 1))) for s in range(2)]
+    K["Dc"] = K["177"] + [do("s", [], act(Dc[:, 208 * j + 192:208 * j + 193], F_(3), scale=2.0)) for j in range(2)]
+    K["DT"] = do("s", [cst], act(T.DT[:], T.DG[:, 0:16], AF.Copy, scale=C_(TM)))
+    K["NEW"] = do("s", [v_one], act(T.NEW[:, 0:256], T.ones[:, 0:256], AF.Copy, scale=0.0))
+    K["dmp"] = do("s", [K["io2"]], act(T.dmp[:], T.cf[:, 64:72:2], bias=F_(0)))
+    hot(1, lambda b: rk2)
+    vt = [digits(0)]
+    unpack(0)
+    K["qI"] = do("v", [d_si], quant(T.qI[:], T.sI[:], T.SI[:]))
+    sorted_(1)
+    vt.append(digits(1))
+    exl = do("v", [ex], cp(EXL, C_(EX2)))
+    for b in range(1, 4):
+        unpack(b)
+    t_b = mine(1, 2)
+    p2 = [do("s", [vt[j]], act(Mx[:, 64 * j:64 * j + 64], VT[:, 96 * j + 32:96 * j + 96], accum_out=own[:, 4 + j:5 + j])) for j in range(2)]
+    K["RC"] = gp([], iota(T.RC[:], [[16, 4], [0, 2], [1, 16]], 192))
+    K["ur"] = gp([], iota(T.urow[:], [[16, 16], [0, 2], [1, 16]], -128))
+    K["IOTA"] = gp([], iota(T.IOTA[:], [[0, 2], [2, 256]]))
+    K["U"] = [dma("y", [K["ur"]], B("UL", t)[:, 192:704], T.urow[:]) for t in range(ROUNDS)]
+
+    def signs(q, deps, at, x_of, o):
+        out, seg = [], []
         for x in x_of:
-            op = A.is_le if (others + [rank])[x] < q else A.is_lt
-            if seg and seg[-1][1] == 64 * x and seg[-1][2] == op:
+            tie = (others + [rank])[x] < q
+            if seg and seg[-1][1] == 64 * x and seg[-1][2] == tie:
                 seg[-1][1] += 64
             else:
-                seg.append([64 * x, 64 * x + 64, op])
-        for (c0, c1, op) in seg:
-            if neg is None:
-                out.append(do("v", deps, ts(Dc[:, at:at + c1 - c0], R[:, c0:c1], s, 4.0, op, A.mult)))
-            else:
-                out.append(do("s", deps, act(Dc[:, at:at + c1 - c0], neg[0][:, neg[1] + c0:neg[1] + c1], AF.Sign, bias=TINY if op == A.is_le else -TINY)))
+                seg.append([64 * x, 64 * x + 64, tie])
+        for (c0, c1, tie) in seg:
+            out.append(do("s", deps, act(Dc[:, at:at + c1 - c0], T.yo[:, o + c0:o + c1], AF.Sign, bias=TINY if tie else -TINY)))
             at += c1 - c0
         return out
 
-    def merge_and_send(t, k):
-        LM, XR, R, Dc, cn, pw, lo, own, F, ow, yo = (B(n, t) for n in ("landM", "XR", "R", "Dc", "cn", "pw", "lo16", "own", "F", "ow", "yo"))
-        aM = ("aM%d" % t, arrive)
-        xs = []
-        for j in range(6):
-            if j % 2 == 0:
-                xs.append(do("v", [aM, cst], ts(XR[:, 32 * j:32 * j + 32], T.ones[:, 0:32], LM[:, j:j + 1], C_(SG), A.mult, A.mult)))
-            else:
-                xs.append(do("s", [aM, K["sgt"]], act(XR[:, 32 * j:32 * j + 32], T.sgt[:], AF.Copy, scale=LM[:, j:j + 1])))
-        k["R"] = do("v", xs, trn(R[:, 0:192], XR[:, 0:192]))
-        d = before(own[:, 0:1], rank, t, [k["R"], k["s"], st["prev"]], 624, range(3))
-        k["cn"] = c = do("v", [d, K["Dc"]], red(cn[:, 3:4], Dc[:, 624:817]))
-        fl = do("v", [c], ts(pw[:, 0:1], cn[:, 3:4], R64, R64, A.add, A.subtract))
-        of = do("v", [fl, K["OE"]], ts(lo[:, 4:10], T.OE[:, 0:6], pw[:, 0:1], cn[:, 3:4], A.add, A.add))
-        sc = do("v", [of, k["VT"], K["F"][t]], cp(F[:, 0:2560].indirect(lo[:, 4:10]), B("VT", t)[:]))
-        k["qF"] = do("v", [sc], quant(B("qF", t)[:], B("sF", t)[:], F[:, 512:1024]))
-        m = do("p", [k["qF"], K["qI"], st["prev"]], mm(T.pD[:, 512:640], T.qI[:, 0:128], T.sI[:, 0:128], B("qF", t)[:], B("sF", t)[:]))
-        k["own2"] = do("p", [k["sc"][1][1]], mm(T.pB[:, 0:128], B("qF", t)[:], B("sF", t)[:], T.qI[:, 0:128], T.sI[:, 0:128]))
-        o2 = [do("s", [aM, cst], act(ow[:, s:s + 1], LM[:, 2 * s:2 * s + 1], scale=C_(SM0))) for s in range(2)]
-        for s in range(2):
-            o2[s] = do("s", [o2[s]], act(ow[:, 8 + s:9 + s], LM[:, 2 * s + 1:2 * s + 2], scale=C_(SM1), bias=ow[:, s:s + 1]))
-        ys = [do("s", [o2[s], k["R"], k["Ro"]], act(yo[:, 256 * s + 64 - 64 * s:256 * s + 256], R[:, 64 - 64 * s:256], bias=ow[:, 8 + s:9 + s], scale=-1.0)) for s in range(2)]
-        sg = [before(None, others[s], t, [ys[s], st["prev"]], 208 * s, [x for x in range(4) if x != s], (yo, 256 * s)) for s in range(2)]
-        k["c2"] = [do("s", [sg[s], K["Dc"]], act(Dc[:, 416 + 416 * s:610 + 416 * s], Dc[:, 208 * s:208 * s + 194], scale=2.0, accum_out=cn[:, s:s + 1])) for s in range(2)]
-        a = do("v", [m], trn(B("tr2", t)[:, 0:128], T.pD[:, 512:640]))
-        of = do("v", [a], ts(lo[:, 10:14], B("tr2", t)[:, 0:128:32], float(LB), 703.0, A.max, A.min))
-        k["tr2"] = a
+    ks = [{}, {}]
+
+    def slots(t, of, n, deps, gaps):
+        k, lo, tr2 = ks[t], B("lo", t), B("tr2", t)
+        F, qF, sF = T["F%d" % t], B("qF", t), B("sF", t)
+        sc = do("v", [of, vt, K["mark"], K["F"], d_f1], cp(F[:, 0:F.shape[1]].indirect(lo[:, 0:6 * n]), VT[:, 0:96 * n]))
+        k["qF"] = do("v", [sc], quant(qF[:], sF[:], F[:, 512:1024]))
+        m = do("p", [k["qF"], K["qI"], deps], mm(T.pD[:, 512:640], T.qI[:, 0:128], T.sI[:, 0:128], qF[:], sF[:]))
+        k["own2"] = do("p", [], mm(T.pB[:, 0:128], qF[:], sF[:], T.qI[:, 0:128], T.sI[:, 0:128]))
+        gaps[0]()
+        k["tr2"] = a = do("v", [m], trn(tr2[:, 0:128], T.pD[:, 512:640]))
+        of = do("v", [a], ts(lo[:, 12:16], tr2[:, SEND:128:32], float(LB), 703.0, A.max, A.min))
+        gaps[1]()
         pd = [of, k["lt"], k["xt"]]
-        ps = do("v", pd, cp(B("PS", t)[:].bitcast(U32), B("SW", t)[:, 0:704].bitcast(U32).indirect(lo[:, 10:14])))
-        pss = do("s", pd, act(B("PSs", t)[:], B("SWs", t)[:, 0:704].indirect(lo[:, 10:14]), AF.Copy))
+        ps = do("v", pd, cp(B("PS", t)[:].bitcast(U32), B("SW", t)[:, 0:704].bitcast(U32).indirect(lo[:, 12:16])))
+        pss = do("s", pd, act(B("PSs", t)[:], B("SWs", t)[:, 0:704].indirect(lo[:, 12:16]), AF.Copy))
         LW, LWs = B("LW", t), B("LWs", t)
-        o = (64, 128, 0)
-        send([ps], "aC%d" % t, B("PS", t)[:, 0:64].bitcast(U8), lambda s: LW[:, o[s]:o[s] + 64].bitcast(U8))
-        send([pss], "aC%d" % t, B("PSs", t)[:, 0:64], lambda s: LWs[:, o[s]:o[s] + 64])
+        k["aC"] = send([ps], "aC%d" % t, lambda s: B("PS", t)[:, 0:64].bitcast(U8), lambda s: LW[:, 64 * s:64 * s + 64].bitcast(U8))
+        k["aS"] = send([pss], "aS%d" % t, lambda s: B("PSs", t)[:, 0:64], lambda s: LWs[:, 64 * s:64 * s + 64])
 
-    def lists(t, k):
-        cn, pw, lo, F, ix, tr2, wl, UL, trU = (B(n, t) for n in ("cn", "pw", "lo16", "F", "ix", "tr2", "wl", "UL", "trU"))
-        tok = k["tr2"]
-        row = lambda r, g=0: tr2[:, 128 * g + r:128 * g + 128:32]
-        nl = do("v", [tok], cp(lo[:, 24:28], row(25)))
-        e = [do("s", [tok, cst], act(ix[:, 0:4], row(1), AF.Copy, scale=C_(EV))),
-             do("s", [tok, cst], act(ix[:, 4:8], row(2), scale=C_(OD), bias=C_(OB)))]
-        fl = do("v", k["c2"], ts(pw[:, 2:4], cn[:, 0:2], R64, R64, A.add, A.subtract))
-        nd_ = [nl, K["nz"], K["np"][t], st["prev"]]
-        k["np"] = [do("s", nd_, act(B("NPs", t)[:, 64:128], T.NZs[:, 0:256].indirect(lo[:, 24:28]), AF.Copy))]
-        of = [do("v", [fl, K["OE"]], ts(lo[:, 16 + 2 * s:18 + 2 * s], T.OE[:, 6:8], pw[:, 2 + s:3 + s], cn[:, s:s + 1], A.add, A.add)) for s in range(2)]
-        u1 = do("v", e, tt(ix[:, 8:12], ix[:, 0:4], ix[:, 4:8], A.max))
-        sc = do("v", [of, K["VO"], k["qF"]], cp(F[:, 0:2560].indirect(lo[:, 16:20]), T.VO[:]))
+    def row(t, r, h=0):
+        return B("tr2", t)[:, 128 * h + r:128 * h + 128:32]
+
+    def noise_list(t):
+        ks[t]["nl"] = do("v", [ks[t]["tr2"]], cp(B("lo", t)[:, 24:28], row(t, HPL)))
+
+    def noise(t, deps):
+        k, lo = ks[t], B("lo", t)
+        nd_ = [k["nl"], K["nz"], K["np"]]
+        a = do("s", nd_, act(B("NPs", t)[:, 64:128], T.NZs[:, 0:256].indirect(lo[:, 24:28]), AF.Copy))
+        b = do("v", nd_, cp(B("NP", t)[:, 64:128].bitcast(U32), T.NZ[:, 0:256].bitcast(U32).indirect(lo[:, 24:28])))
+        k["dn"] = [do("p", [a, b, K["qE"], deps], mm(T.pC[:, 512 * j:512 * j + 128], T.qE[:, 128 * j:128 * j + 128], T.sE[:, 128 * j:128 * j + 128],
+                                                     B("NP", t)[:], B("NPs", t)[:], True, False)) for j in range(4)]
+
+    def places(t, deps):
+        k, ix, lo, UL = ks[t], B("ix", t), B("lo", t), B("UL", t)
+        e = do("s", [k["tr2"], cst], act(ix[:, 0:4], row(t, ULL), AF.Copy, scale=C_(EV)))
+        e2 = do("s", [], act(ix[:, 4:8], row(t, ULD), AF.Copy, scale=C_(OD)))
+        yield
+        u1 = do("v", [e, e2], tt(ix[:, 8:12], ix[:, 0:4], ix[:, 4:8], A.max))
+        yield
         u2 = do("v", [u1, K["dmp"]], tt(ix[:, 12:16], ix[:, 8:12], T.dmp[:], A.max))
-        qg = do("v", [sc], quant(B("qG", t)[:], B("sG", t)[:], F[:, 0:512]))
-        do("p", [k["qF"], k["trA"]], mm(T.pD[:, 0:128], T.qI[:, 0:128], T.sI[:, 0:128], B("qF", t)[:], B("sF", t)[:], True, False))
-        mo = do("p", [qg], mm(T.pD[:, 0:128], T.qI[:, 128:256], T.sI[:, 128:256], B("qG", t)[:], B("sG", t)[:], False, True))
+        yield
         uo = [do("v", [u2], ts(lo[:, 48 + h:56:2], ix[:, 12:16], 16.0 * h, None, A.add)) for h in range(2)]
-        k["np"].append(do("v", nd_, cp(B("NP", t)[:, 64:128].bitcast(U32), T.NZ[:, 0:256].bitcast(U32).indirect(lo[:, 24:28]))))
-        k["dn"] = [do("p", [k["np"], K["qE"], st["prev"]], mm(T.pC[:, 512 * b:512 * b + 128], T.qE[:, 128 * b:128 * b + 128], T.sE[:, 128 * b:128 * b + 128],
-                                                              B("NP", t)[:], B("NPs", t)[:], True, False)) for b in range(4)]
-        w1 = do("s", [k["own2"]], act(wl[:, 0:2], T.pB[:, 9:11], AF.Sign))
-        k["w"] = []
-        for j in range(2):
-            w2 = do("s", [w1], act(wl[:, 2 + j:3 + j], wl[:, j:j + 1], AF.Copy, scale=256.0 * rank - (LB, XB)[j]))
-            k["w"].append(do("s", [w2], act(wl[:, 4 + j:5 + j], T.pB[:, 9 + j:10 + j], bias=wl[:, 2 + j:3 + j])))
-        send([k["w"]], "aP%d" % t, wl[:, 4:6], lambda s: B("landP", t)[:, 2 * s:2 * s + 2])
-        us = do("v", [uo, K["RC"], K["U%d" % t]], cp(UL[:, 0:704].indirect(lo[:, 48:56]), T.RC[:]))
-        a = do("v", [mo], trn(tr2[:, 128:256], T.pD[:, 0:128]))
-        m = [do("v", [a], tt(ix[:, 16 + 4 * j:20 + 4 * j], row(9 + j), row(3 + 8 * j, 1), A.max)) for j in range(2)]
-        k["AB"] = do("v", m, cp(lo[:, 32:40], ix[:, 16:24]))
-        a = do("v", [us], trn(trU[:], UL[:, 192:704]))
-        k["pl"] = [do("v", [a], ts(lo[:, 64 + 16 * x:80 + 16 * x], trU[:, 16 * x:512:32], 128.0, None, A.add)) for x in range(2)]
+        yield
+        us = do("v", [uo, K["RC"], K["U"][t]], cp(UL[:, 0:704].indirect(lo[:, 48:56]), T.RC[:]))
+        yield
+        a = do("v", [us, deps], trn(T.trU[:], UL[:, 192:704]))
+        yield
+        k["pl"] = [do("v", [a], ts(lo[:, 64 + 16 * x:80 + 16 * x], T.trU[:, 16 * x:512:32], 128.0, None, A.add)) for x in range(2)]
+        yield
 
-    def renew(t, k, oq, os_, o):
-        LW, LWs, XW, XWs, LN, LNs, NEW, lo = (B(n, t) for n in ("LW", "LWs", "XW", "XWs", "LN", "LNs", "NEW", "lo16"))
-        ad = [("aC%d" % t, 2 * arrive), k["AB"], k["cp"]["W"]]
-        a2 = do("s", ad, act(XWs[:, 256:384], LWs[:, 0:704].indirect(lo[:, 32:40]), AF.Copy))
-        a1 = do("v", ad, cp(XW[:, 256:384].bitcast(U32), LW[:, 0:704].bitcast(U32).indirect(lo[:, 32:40])))
-        dc = [do("p", [a1, a2], mm(T.pC[:, 512 * b:512 * b + 128], T.qE[:, 128 * b:128 * b + 128], T.sE[:, 128 * b:128 * b + 128],
-                                   XW[:, 256:384], XWs[:, 256:384], False, True)) for b in range(4)]
-        xd = [k["pl"], k["cp"]["X"], a1, a2]
-        x1 = do("v", xd, cp(oq[:, o + 256:o + 512].bitcast(U32), XW[:, 0:384].bitcast(U32).indirect(lo[:, 80:96])))
-        x2 = do("s", xd, act(os_[:, o + 256:o + 512], XWs[:, 0:384].indirect(lo[:, 80:96]), AF.Copy))
-        nw = []
-        for b in range(4):
-            i, h = T.pC[:, 512 * b + 64:512 * b + 128], NEW[:, b:256:4]
-            nw.append(do("v", [dc[b]], ts(h, i, 0.5, None, A.mult)) if b % 2 else do("s", [dc[b], st["prev"]], act(h, i, AF.Copy, scale=0.5)))
-        qn = do("v", [nw, K["NEW"]], quant(LN[:, 256:384], LNs[:, 256:384], NEW[:]))
-        return qn, nw, [x1, x2]
+    def arrived(t):
+        k, lo = ks[t], B("lo", t)
+        LW, LWs, XW, XWs = (B(n, t) for n in ("LW", "LWs", "XW", "XWs"))
+        ad = [k["AB"], cps[t]["W"]]
+        b2 = do("s", [ad, k["aS"]], act(XWs[:, 256:320], LWs[:, 0:704].indirect(lo[:, 36:40]), AF.Copy))
+        b1 = do("v", [ad, k["aC"]], cp(XW[:, 256:320].bitcast(U32), LW[:, 0:704].bitcast(U32).indirect(lo[:, 36:40])))
+        k["dc"] = [do("p", [b1, b2, cps[t]["X"]], mm(T.pC[:, 512 * b:512 * b + 128], T.qE[:, 128 * b:128 * b + 128], T.sE[:, 128 * b:128 * b + 128],
+                                                     XW[:, 192:320], XWs[:, 192:320], False, True)) for b in range(4)]
+        a1 = do("v", [], cp(XW[:, 320:384].bitcast(U32), LW[:, 0:704].bitcast(U32).indirect(lo[:, 32:36])))
+        a2 = do("s", [], act(XWs[:, 320:384], LWs[:, 0:704].indirect(lo[:, 32:36]), AF.Copy))
+        k["A"] = {"v": a1, "s": a2}
 
-    def renew_live(t, k, qn, oq, os_, o):
-        LN, LNs, lo = B("LN", t), B("LNs", t), B("lo16", t)
-        ld = [qn, k["pl"], k["cp"]["L"]]
-        l2 = do("s", ld, act(os_[:, o:o + 256], LNs[:, 0:384].indirect(lo[:, 64:80]), AF.Copy))
-        l1 = do("v", ld, cp(oq[:, o:o + 256].bitcast(U32), LN[:, 0:384].bitcast(U32).indirect(lo[:, 64:80])))
-        return [l1, l2]
+    def renew(t, deps):
+        k, NEW = ks[t], T.NEW
+        k["nw"] = [do("v", [k["dc"][b], deps], ts(NEW[:, 256 + b:512:4], T.pC[:, 512 * b + 64:512 * b + 128], 0.5, None, A.mult)) for b in range(4)]
+        k["qn"] = do("v", [k["nw"], K["NEW"]], quant(B("LN", t)[:, 256:384], B("LNs", t)[:, 256:384], NEW[:]))
 
-    def numbers(t, k):
-        LP, fo, wl = B("landP", t), B("fo", t), B("wl", t)
-        aP = ("aP%d" % t, arrive)
-        a = [do("v", [aP], red(fo[:, j:j + 1], LP[:, j:6:2])) for j in range(2)]
-        b = do("v", [a, k["w"]], tt(fo[:, 2:4], fo[:, 0:2], wl[:, 4:6], A.add))
-        for c in range(4):
-            dma("y", [b], T.lw[t:t + 1, 16 * c:16 * c + 16], fo[32 * c:32 * c + 16, 2:3])
-            dma("y", [b], T.sw[t:t + 1, 16 * c:16 * c + 16], fo[32 * c:32 * c + 16, 3:4])
+    def held(t, x, oq, os_, o, qs="vs", c0=0, c1=16):
+        k, lo = ks[t], B("lo", t)
+        W, Ws = (B("XW", t), B("XWs", t)) if x else (B("LN", t), B("LNs", t))
+        ld = lambda q: [k["pl"], [k["A"][q], cps[t]["X"]] if x else [k["qn"], cps[t]["L"]]]
+        li, r = lo[:, 64 + 16 * x + c0:64 + 16 * x + c1], []
+        if "s" in qs:
+            r.append(do("s", ld("s"), act(os_[:, o + 16 * c0:o + 16 * c1], Ws[:, 0:384].indirect(li), AF.Copy)))
+        if "v" in qs:
+            r.append(do("v", ld("v"), cp(oq[:, o + 16 * c0:o + 16 * c1].bitcast(U32), W[:, 0:384].bitcast(U32).indirect(li))))
+        return r
 
-    ks = [{"sc": {}, "cp": {}} for t in range(ROUNDS)]
-    k = ks[0]
-    k["lt"], k["xt"], k["first"] = q_l, q_x, 0
-    for ty in range(2):
-        score(0, ty, (q_l, q_x)[ty], k)
-        copies(0, ty, (q_l, q_x)[ty], k["cp"])
+    k, lo, ix = ks[0], B("lo", 0), B("ix", 0)
+    k["lt"], k["xt"] = q_l, q_x
+    XO, RW = 256, 768
+    aM = srt[0]["a"]
+    a = do("v", [aM, K["cl"], K["MS"]], tt(XR[:, 256:448], LM[:, 0:6].indirect(REP), T.MS[:], A.mult))
+    x1 = do("v", [a], trn(R[:, XO:XO + 192], XR[:, 256:448]))
+    raw = [do("s", [aM, K["sgt"]], act(XR[:, 32 * j:32 * j + 32], T.sgt[:], AF.Copy, scale=LM[:, j:j + 1])) for j in range(6)]
+    d = do("v", [x1, s_a], ts(Dc[:, 624:816], R[:, XO:XO + 192], own[:, 0:1], 4.0, A.is_lt, A.mult))
+    Rt = do("v", [raw, xo], trn(R[:, 0:256], XR[:, 0:256]))
+    c1 = do("v", [d], scan(cs[:, 0:96], Dc[:, 624:720], Dc[:, 720:816], C_(E4)))
+    cn = cs[:, 95:96]
+    fl = do("v", [c1], ts(sm[:, 0:1], cn, R64, R64, A.add, A.subtract))
+    of = do("v", [fl, K["io"]], ts(lo[:, 0:6], OE, sm[:, 0:1], cn, A.add, A.add))
+    o2 = [do("s", [aM, cst], act(sm[:, 8 + s:9 + s], LM[:, 2 * s + 2:2 * s + 3], scale=C_(SM0))) for s in range(2)]
+    for s in range(2):
+        o2[s] = do("s", [o2[s]], act(sm[:, 10 + s:11 + s], LM[:, 2 * s + 3:2 * s + 4], scale=C_(SM1), bias=sm[:, 8 + s:9 + s]))
+    ys = [do("s", [o2[s], Rt], act(T.yo[:, 256 * s:256 * s + 256], R[:, 0:256], bias=sm[:, 10 + s:11 + s], scale=-1.0)) for s in range(2)]
+    sg = [signs(others[s + 1], [ys[s]], 208 * s, [x for x in range(4) if x != s + 1], 256 * s) for s in range(2)]
+    c2 = [do("s", [sg[s], K["Dc"]], act(Dc[:, 416 + 416 * s:610 + 416 * s], Dc[:, 208 * s:208 * s + 194], scale=2.0, accum_out=sm[:, 4 + s:5 + s])) for s in range(2)]
+    k1 = do("s", [c1], act(sm[:, 16:17], cn, scale=0.25, bias=135.5))
+
+    def gap0():
+        K["nz"] = do("v", [d_nz], quant(T.NZ[:], T.NZs[:], T.t_nz[:]))
+
+    slots(0, of, 1, [srt[1]["trA"]], [gap0, lambda: noise_list(0)])
+    pla = places(0, [])
+    next(pla)
+    fl = do("v", c2, ts(sm[:, 2:4], sm[:, 4:6], R64, R64, A.add, A.subtract))
+    noise(0, [])
+    of = [do("v", [fl, K["io2"]], ts(lo[:, 16 + 2 * s:18 + 2 * s], OE2, sm[:, 2 + s:3 + s], sm[:, 4 + s:5 + s], A.add, A.add)) for s in range(2)]
+    next(pla)
+    sc = do("v", [of, K["VO"], k["qF"]], cp(T.F0[:, 0:2560].indirect(lo[:, 16:20]), T.VO[:]))
+    next(pla)
+    qg = do("v", [sc], quant(T.qG[:], T.sG[:], T.F0[:, 0:512]))
+    do("p", [k["qF"], srt[0]["trA"]], mm(T.pD[:, 0:128], T.qI[:, 0:128], T.sI[:, 0:128], B("qF", 0)[:], B("sF", 0)[:], True, False))
+    mo = do("p", [qg], mm(T.pD[:, 0:128], T.qI[:, 128:256], T.sI[:, 128:256], T.qG[:], T.sG[:], False, True))
+    w0 = do("s", [k["own2"], cst], act(T.wl[:, 0:2], T.pB[:, NUML:NUMD + 1:NUMD - NUML], AF.Copy, scale=C_(EV)))
+    next(pla)
+    k2 = do("v", [k1], ts(sm[:, 17:18], sm[:, 16:17], 192.0, sm[:, 16:17], A.is_lt, A.mult))
+    next(pla)
+    a = do("v", [mo], trn(B("tr2", 0)[:, 128:256], T.pD[:, 0:128]))
+    k3 = do("v", [k2], ts(lo[:, 112:113], sm[:, 17:18], F_(3), None, A.max))
+    m = [do("v", [a], tt(ix[:, 16 + 4 * j:20 + 4 * j], row(0, (COLL, COLD)[j]), row(0, (REMA, REMB)[j], 1), A.max)) for j in range(2)]
+    next(pla)
+    k["AB"] = do("v", m, cp(lo[:, 32:40], ix[:, 16:24]))
+    next(pla)
+    ex2 = do("v", [a, exl], cp(lo[:, 96:112], B("tr2", 0)[:, 128:256].indirect(EXL)))
+    xp = do("v", [srt[1]["a"]], tt(XR[:, 448:640], LM[:, 8:14].indirect(REP), T.MS[:], A.mult))
+
+    arrived(0)
+    qM, sM = T.qU[:, 64:192], T.sU[:, 64:192]
+    mA = do("p", [list(k["A"].values()), srt[1]["trA"]], mm(T.pA[:, 0:128], qM, sM, B("XW", 0)[:, 256:384], B("XWs", 0)[:, 256:384]))
+    n = ks[1]
+    n["xt"] = held(0, 1, B("SW", 1), B("SWs", 1), XB)
+    copies(1, 1, n["xt"], cps[1])
+    renew(0, [])
+    sA = do("s", [mA], act(G[64:128, 128:192], T.pA[64:128, 64:128], AF.Abs, bias=LIFT))
+    mN = do("p", [k["qn"], w0], mm(T.pB[:, 0:128], qM, sM, B("LN", 0)[:, 256:384], B("LNs", 0)[:, 256:384]))
+    x2 = do("v", [xp], trn(R[:, XO + 192:XO + 384], XR[:, 448:640]))
+    mo_ = do("v", [p2, K["IOTA"], srt[1]["of"]], ts(Mx[:, 0:128], T.IOTA[:, 0:512].indirect(so[:, 0:8]), own[:, 4:5], C_(CM), A.is_ge, A.add))
+    sN = do("s", [mN], act(G[0:64, 128:192], T.pB[0:64, 64:128], AF.Abs, bias=LIFT))
+    tg = do("v", [sA, sN], trn(trG[:, 128:192], G[:, 128:192]))
+    aM = send([tg], "aM2", lambda s: trG[:, 159:161], lambda s: LM[:, 16 + 2 * s:18 + 2 * s])
+
+    a = do("s", [x1, x2, t_b], act(Dc[:, 1040:1424], R[:, XO:XO + 384], AF.Sign, scale=-1.0, bias=own[:, 2:3]))
+    a = do("s", [a], act(Dc[:, 1424:1808], Dc[:, 1040:1424], AF.Relu, scale=4.0, accum_out=sm[:, 14:15]))
+    base_b = do("s", [a], act(sm[:, 15:16], sm[:, 14:15], bias=C_(E4)))
+    a = do("v", [k3, K["DT"]], tt(cs[:, 416:432], G[:, 0:192].indirect(lo[:, 112:113]), T.DT[:], A.mult))
+    xw = do("v", [mo_, srt[1]["G"]], tt(R[:, XO + 384:XO + 512], G[:, 0:128], Mx[:, 0:128], A.mult))
+    mn = [do("v", [ex2], ts(Mx[:, 128:192], T.IOTA[:, 0:256].indirect(lo[:, 108:112]), own[:, 4:5], C_(CM), A.is_ge, A.add))]
+    t_a = do("v", [a], red(own[:, 6:7], cs[:, 416:432]))
+    mn.append(do("v", [], ts(Mx[:, 192:256], T.IOTA[:, 0:256].indirect(lo[:, 108:112]), own[:, 5:6], C_(CM), A.is_ge, A.add)))
+    d = do("v", [t_a, xw, x2, c2], ts(Dc[:, 0:512], R[:, XO:XO + 512], own[:, 6:7], 4.0, A.is_lt, A.mult))
+    xn = [do("v", [mn[0]], tt(R[:, RW + 192:RW + 256], G[:, 128:192], Mx[:, 128:192], A.mult))]
+    a = do("v", [d], scan(cs[:, 96:352], Dc[:, 0:256], Dc[:, 256:512], -286.0))
+    xn.append(do("v", [mn[1]], tt(R[:, RW + 256:RW + 320], G[:, 128:192], Mx[:, 192:256], A.mult)))
+    base_a = do("v", [a], ts(sm[:, 18:19], cs[:, 351:352], -30.0, None, A.max))
+    n["lt"] = held(0, 0, B("SW", 1), B("SWs", 1), LB, "s")
+
+    l0 = lo
+    k, lo, ix = ks[1], B("lo", 1), B("ix", 1)
+    a = do("v", [aM], tt(XR[:, 640:832], LM[:, 16:22].indirect(REP), T.MS[:], A.mult))
+    Rt = do("v", [a], trn(R[:, RW:RW + 192], XR[:, 640:832]))
+    d = [do("v", [Rt, xn, t_a, t_b], ts(Dc[:, 1808 + 64 * j:1872 + 64 * j], R[:, RW:RW + 320].indirect(l0[:, 100 + 4 * j:104 + 4 * j]),
+                                        (own[:, 6:7], own[:, 2:3])[j], 4.0, A.is_lt, A.mult)) for j in range(2)]
+    c = [do("v", [d[j], base_a, base_b], scan(cs[:, 352 + 32 * j:384 + 32 * j], Dc[:, 1808 + 64 * j:1840 + 64 * j], Dc[:, 1840 + 64 * j:1872 + 64 * j],
+                                              (sm[:, 18:19], sm[:, 15:16])[j])) for j in range(2)]
+    fl = [do("v", [c[j]], ts(sm[:, 20 + j:21 + j], cs[:, 383 + 32 * j:384 + 32 * j], R64, R64, A.add, A.subtract)) for j in range(2)]
+    of = [do("v", [fl[j]], ts(lo[:, 6 * j:6 * j + 6], OE, sm[:, 20 + j:21 + j], cs[:, 383 + 32 * j:384 + 32 * j], A.add, A.add)) for j in range(2)]
+
+    def gap0():
+        n["lt"] += held(0, 0, B("SW", 1), B("SWs", 1), LB, "v")
+        copies(1, 0, n["lt"], cps[1])
+
+    def gap1():
+        f = [do("s", [k["tr2"]], act(T.fm[:, 8 * j:8 * j + 4], row(1, (FL1, FL2)[j]), AF.Copy)) for j in range(2)]
+        k["aF"] = send(f, "aF", lambda s: T.fm[:, 8 * s - 8:8 * s - 4], lambda s: T.LF[:, 8 * s - 8:8 * s - 4], (1, 2))
+
+    slots(1, of, 2, [sN, ks[0]["tr2"]], [gap0, gap1])
+    LQ, fo = T.LQ, T.fo
+    w1 = [do("s", [k["own2"], w0], act(LQ[:, 6 + j:7 + j], T.pB[:, (NUML, NUMD)[j]:(NUML, NUMD)[j] + 1], scale=C_(OD), bias=T.wl[:, j:j + 1])) for j in range(2)]
+    pla = places(1, [ks[0]["pl"]])
+    next(pla)
+    noise_list(1)
+    wu = do("v", w1, cp(T.wu[:], LQ[:, 6:8]))
+    aP = send([wu], "aP", lambda s: T.wu[:], lambda s: T.LP[:, 2 * s:2 * s + 2])
+    noise(1, [ks[0]["nw"]])
+    next(pla)
+    K["qW"] = do("v", [d_w], quant(T.qW[:], T.sW[:], T.t_w[:]))
+    next(pla)
+    z_o = do("v", [], fill(fo[:, 0:32], 0.0))
+    next(pla)
+    next(pla)
+    a = do("v", [k["aF"]], tt(ix[:, 24:28], T.LF[:, 0:4], T.LF[:, 8:12], A.add))
+    next(pla)
+    m = [do("v", [a], tt(ix[:, 16 + 4 * j:20 + 4 * j], row(1, (COLL, COLD)[j]), ix[:, 24:28], A.max)) for j in range(2)]
+    next(pla)
+    k["AB"] = do("v", m, cp(lo[:, 32:40], ix[:, 16:24]))
+    arrived(1)
+    xt = held(1, 1, T.FN, T.FNs, 256)
+    lq = do("v", [aP], cp(LQ[:, 0:6], T.LP[:]))
+    renew(1, [ks[0]["qn"]])
+    dma("y", xt, T.oc[:, 1024:2048], T.FN[:, 256:512].bitcast(U8), "out")
+    nu = [do("s", [lq, w1, z_o], act(LQ[:, 8 + 4 * j:12 + 4 * j], LQ[:, j:8:2], accum_out=fo[:, j:j + 1])) for j in range(2)]
+    lt = [held(1, 0, T.FN, T.FNs, 0, "vs", 8 * h, 8 * h + 8) for h in range(2)]
+    a = do("v", nu, trn(fo[:, 32:64], fo[:, 0:32]))
+    my = [do("p", [lt[h], K["qW"], sA, w1], mm((T.pA, T.pB)[h][:, 0:128], T.qW[:], T.sW[:], T.FN[:, 128 * h:128 * h + 128], T.FNs[:, 128 * h:128 * h + 128]))
+          for h in range(2)]
+    dma("y", lt, T.oc[:, 0:1024], T.FN[:, 0:256].bitcast(U8), "out")
+    for q in range(4):
+        dma("y", [lt, xt], T.osc[4 * q:4 * q + 4, :], T.FNs[32 * q:32 * q + 4, 0:512], "out")
+    y0 = do("s", [my[0]], act(T.yt[:, 0:128], T.pA[:, 0:128], AF.Copy))
+    y1 = do("v", [my[1]], cp(T.yt[:, 128:256], T.pB[:, 0:128]))
+    dma("s", [y0, y1], T.y[:], T.yt[:], "out")
     for t in range(ROUNDS):
-        k = ks[t]
-        last = t + 1 == ROUNDS
-        order_and_send(t, k)
-        if t == 0:
-            consts_s()
-        prepare(t, k)
-        if t == 0:
-            consts_v()
-            rows()
-        else:
-            consts_2()
-            numbers(0, ks[0])
-        merge_and_send(t, k)
-        lists(t, k)
-        oq, os_, o = (T.FN, T.FNs, 0) if last else (B("SW", t + 1), B("SWs", t + 1), LB)
-        qn, nw, xt = renew(t, k, oq, os_, o)
-        if last:
-            lt = renew_live(t, k, qn, oq, os_, o)
-            dma("y", xt, T.oc[:, 1024:2048], T.FN[:, 256:512].bitcast(U8))
-            for q in range(4):
-                dma("y", xt, T.osc[4 * q:4 * q + 4, 256:512], T.FNs[32 * q:32 * q + 4, 256:512])
-            my = do("p", [lt, K["qW"], k["sc"][0][1]], mm(T.pA[:, 0:256], T.qW[:], T.sW[:], T.FN[:, 0:256], T.FNs[:, 0:256]))
-            dma("y", lt, T.oc[:, 0:1024], T.FN[:, 0:256].bitcast(U8))
-            for q in range(4):
-                dma("y", lt, T.osc[4 * q:4 * q + 4, 0:256], T.FNs[32 * q:32 * q + 4, 0:256])
-            yc = do("s", [my], act(T.yt[:], T.pA[:, 0:256], AF.Copy))
-            dma("s", [yc], T.y[:], T.yt[:])
-            numbers(t, k)
-        else:
-            n = ks[t + 1]
-            n["xt"], n["first"] = xt, 1
-            st["prev"] = [xt, nw, k["w"]]
-            copies(t + 1, 1, xt, n["cp"])
-            n["lt"] = lt = renew_live(t, k, qn, oq, os_, o)
-            score(t + 1, 1, xt, n)
-            copies(t + 1, 0, lt, n["cp"])
-            score(t + 1, 0, lt, n)
-            st["prev"] = [lt, xt, nw, k["w"]]
+        dma("y", [a], T.lw[t:t + 1, :], fo[0:128:32, 32 + 16 * t:48 + 16 * t], "out")
+        dma("y", [a], T.sw[t:t + 1, :], fo[1:128:32, 32 + 16 * t:48 + 16 * t], "out")
     for s, n in cnt.items():
-        if top.get(s, 0) < n:
+        if top.get(s, 0) < n and s != "out":
             g.wait_ge(T.sem[s], n)
+    g.wait_ge(T.sem["out"], cnt["out"])

@@ -7,8 +7,11 @@ LIFT = 2.0 ** -100
 TOP = 2.0 ** 24
 R64 = 1.5 * 2.0 ** 29
 ROUNDS = 2
-LB, XB = 192, 448
-REMA, LAL, LBL, HPL, NUML, COLL, SEND, COLD, NUMD, HPD, LBD, LAD, REMB, FL1, FL2, ULL, ULD = range(17)
+XB, LB, NB = 0, 256, 512
+REMA, LAL, LBL, HPL, NUML, COLL, SEND, COLD, NUMD, HPD, LBD, LAD, REMB, FL1, FL2, ULL, ULL1, ULD, ULD1 = range(19)
+_O = ("ahagaxalbvbuaoawaqajaiauakbnavanapabasboaraabibhbgbabjbfbdcoclbccaatamfqazfpbqfmfofnaybpflacdgfkbrfsdpdybecnfradfubyfifgfdftfcdderffgcgecffhfegdbbbtfvfbbsgpccgfgrdqfjgggqdzcjdtgkgigjdfghdegscgglgtaedjgvcmgmafgugxgwgagogygnfygzhdhadshbegcdhedxhfhghhhihjbzcweqcieebwhcdbethuhwcbhtdvbxcheahvfaexhkceephlcpesebhmehdhhpewdrhxdcckdwducyhyeyhzefeledejekczcqeidihoblfwiacreccxhnemibcscueoenichqdabkidinimctilgbijiviojpikisfzithrkbiuipjqifiqirixiyiziedmdkjtkclxkfjrdljajskdkeiwhsevkijbkhkgjcjvjdjwmakljulflgcvlykjjekkjfjzjgknjxjyjhjlkmkamblajijmihlclplblqkulolnlslreuldkojjltbmleiijkkplhjodnktjnkskrljkqkvlllkmfmemjmglumhdomimlliigmmkwmompkxmnmkmqmrlmkzmsmtkyezmumcmdlzmvlvnglwnmnhndmxnfnimwnamzmynsnrnjnonpnqnnnlntnknunynvnznwoanbnxobocodoeofncogneohokojoioupfomonorovfxoypgowppoqolotozphoopqplpapnoppmpcpdpeoxospbpopiprpypspxpwpkpjpvptqbpupzqeqcqaqfqdqtqiqgqhqjqvquqkqnqlqwqoqpqrqmqqqsqx")
+ORDER = [26 * (ord(_O[_i]) - 97) + ord(_O[_i + 1]) - 97 for _i in range(0, len(_O), 2)]
+ALSO = [(264, 267)]
 
 SCRATCH = {
     "pA": ("psum", [128, 512], "float32"), "pB": ("psum", [128, 512], "float32"), "pC": ("psum", [128, 2048], "float32"),
@@ -20,23 +23,23 @@ for _n, _w, _d in (
         ("qW", 128, F8), ("sW", 128, "uint8"), ("ones", 516, "bfloat16"), ("zer", 128, "bfloat16"), ("MK", 66, "bfloat16"),
         ("SS", 1024, "bfloat16"), ("SI", 1024, "bfloat16"), ("EM", 516, "bfloat16"), ("qS", 256, F8), ("sS", 256, "uint8"),
         ("qI", 256, F8), ("sI", 256, "uint8"), ("qE", 512, F8), ("sE", 512, "uint8"), ("NZ", 256, F8), ("NZs", 256, "uint8"),
-        ("ii", 10, "int32"), ("fc", 32, "float32"), ("cf", 96, "float32"), ("cl", 32, "uint16"),
+        ("ii", 12, "int32"), ("fc", 36, "float32"), ("cf", 96, "float32"), ("cl", 32, "uint16"),
         ("tin", 256, "bfloat16"), ("Mneg", 256, "bfloat16"), ("Mtri", 256, "bfloat16"), ("Kn", 128, "bfloat16"), ("RC", 128, "bfloat16"),
-        ("dmp", 4, "float32"), ("DG", 64, "bfloat16"), ("DT", 16, "float32"), ("MS", 192, "float32"), ("IOTA", 512, "bfloat16"),
-        ("sgt", 32, "float32"), ("VO", 64, "bfloat16"), ("urow", 512, "bfloat16"),
+        ("dmp", 16, "float32"), ("DG", 32, "bfloat16"), ("DT", 16, "float32"), ("yw", 384, "float32"), ("IOTA", 512, "bfloat16"),
+        ("sgt", 128, "float32"), ("Gs", 96, "float32"), ("XC", 192, "bfloat16"), ("VO", 64, "bfloat16"), ("NP", 192, F8), ("NPs", 192, "uint8"),
         ("yt", 256, "float32"), ("FN", 512, F8), ("FNs", 512, "uint8"),
         ("qH", 256, F8), ("sH", 256, "uint8"), ("H", 1024, "bfloat16"), ("qG", 128, F8), ("sG", 128, "uint8"),
-        ("NEW", 512, "bfloat16"), ("VT", 192, "bfloat16"), ("sC", 4, "float32"), ("Vc", 512, "float32"), ("yd", 512, "float32"),
+        ("NEW", 512, "bfloat16"), ("VT", 96, "bfloat16"), ("sC", 4, "float32"), ("Vc", 512, "float32"), ("yd", 512, "float32"),
         ("yo", 512, "float32"), ("DD", 1024, "bfloat16"), ("rk", 136, "float32"), ("trA", 256, "float32"), ("G", 192, "float32"),
-        ("trG", 192, "float32"), ("own", 8, "float32"), ("LM", 24, "float32"), ("XR", 832, "float32"), ("R", 1088, "float32"),
-        ("Dc", 2080, "bfloat16"), ("cs", 432, "float32"), ("sm", 48, "float32"), ("Mx", 256, "float32"), ("trU", 512, "bfloat16"),
+        ("trG", 192, "float32"), ("own", 8, "float32"), ("LM", 24, "float32"), ("XR", 576, "float32"), ("R", 832, "float32"),
+        ("Dc", 2592, "bfloat16"), ("cs", 432, "float32"), ("sm", 48, "float32"), ("Mx", 384, "float32"), ("trU", 1024, "bfloat16"),
         ("so", 8, "uint16"), ("fm", 16, "bfloat16"), ("LF", 16, "bfloat16"), ("wl", 4, "float32"), ("wu", 2, "uint16"),
         ("LP", 6, "uint16"), ("LQ", 16, "float32"), ("fo", 64, "float32"), ("F0", 2560, "bfloat16"), ("F1", 5248, "bfloat16")):
     SCRATCH[_n] = ("sbuf", [128, _w], _d)
 for _n, _w, _d in (
-        ("SW", 704, F8), ("SWs", 704, "uint8"), ("LW", 704, F8), ("LWs", 704, "uint8"), ("XW", 384, F8), ("XWs", 384, "uint8"),
-        ("LN", 384, F8), ("LNs", 384, "uint8"), ("PS", 64, F8), ("PSs", 64, "uint8"), ("NP", 128, F8), ("NPs", 128, "uint8"),
-        ("qF", 128, F8), ("sF", 128, "uint8"), ("tr2", 256, "float32"), ("ix", 32, "float32"), ("UL", 704, "bfloat16"),
+        ("SW", 640, F8), ("SWs", 640, "uint8"), ("LW", 320, F8), ("LWs", 320, "uint8"), ("XW", 448, F8), ("XWs", 448, "uint8"),
+        ("PS", 64, F8), ("PSs", 64, "uint8"),
+        ("qF", 144, F8), ("sF", 144, "uint8"), ("tr2", 256, "float32"), ("ix", 32, "float32"), ("UL", 704, "bfloat16"),
         ("lo", 128, "uint16")):
     for _t in range(ROUNDS):
         SCRATCH[_n + str(_t)] = ("sbuf", [128, _w], _d)
@@ -50,90 +53,39 @@ def rank_program(g, core, T, topo):
         return
     cores = list(T.cores)
     others = [rank ^ d for d in (3, 1, 2)]
+    low = [int(q < rank) for q in others]
     Q = {"v": g.vector, "s": g.scalar, "p": g.tensor, "gc": g, "y": g.sync}
-    cnt, top, nd = {}, {}, [0]
-    know = {q: {} for q in Q}
-    behind = {}
+    calls = []
 
     def flat(deps, out):
         for d in deps:
             if isinstance(d, list):
                 flat(d, out)
             elif d is not None:
-                out[d[0]] = max(out.get(d[0], 0), d[1])
+                out.append(d)
         return out
 
-    def need(qn, deps):
-        want = flat(deps, {})
-        for s, n in want.items():
-            if know[qn].get(s, 0) >= n or any(behind.get(o, {}).get(s, 0) >= n for o in want.items() if o[0] != s):
-                continue
-            Q[qn].wait_ge(T.sem[s], n)
-            top[s] = max(top.get(s, 0), n)
-        for s, n in want.items():
-            for a, b in list(behind.get((s, n), {}).items()) + [(s, n)]:
-                know[qn][a] = max(know[qn].get(a, 0), b)
-
-    def token(qn, s, n, step):
-        cnt[s] = n
-        k = dict(behind.get((s, n - step), {}))
-        for a, b in know[qn].items():
-            k[a] = max(k.get(a, 0), b)
-        behind[(s, n)] = k
-        return (s, n)
+    def note(kind, qn, deps, what):
+        calls.append((kind, qn, flat(deps, []), what))
+        return len(calls) - 1
 
     def do(qn, deps, f):
-        need(qn, deps)
-        f(Q[qn]).then_inc(T.sem[qn], 1)
-        return token(qn, qn, cnt.get(qn, 0) + 1, 1)
-
-    side = [False]
+        return note("do", qn, deps, f)
 
     def gp(deps, f, upper=False):
-        if upper != side[0]:
-            deps = [deps, ("gc", cnt["gc"])]
-            side[0] = upper
-        return do("gc", deps, f)
+        return note("upper" if upper else "gp", "gc", deps, f)
+
+    def group(qn, deps, pairs, s=None):
+        return note("dma", qn, deps, (pairs, s))
 
     def dma(qn, deps, out, in_, s=None):
-        need(qn, deps)
-        if s is None:
-            s = "d%d" % nd[0]
-            nd[0] += 1
-        Q[qn].dma_start(out, in_).then_inc(T.sem[s], 16)
-        return token(qn, s, cnt.get(s, 0) + 16, 16)
+        return group(qn, deps, [(out, in_)], s)
 
-    def group(qn, deps, pairs):
-        s = "d%d" % nd[0]
-        nd[0] += 1
-        return [dma(qn, deps, o, i, s) for o, i in pairs][-1]
+    def send(deps, sem, view, land, to=(0, 1, 2)):
+        return note("send", "gc", deps, (sem, view, land, to))
 
     def B(n, t):
         return T[n + str(t)]
-
-    dst = [cores[q] for q in others]
-    far = [c for c in dst if topo.chip(c) != topo.chip(core)]
-    fe = topo.engines(core, far[0])
-    eng = {}
-    for n, c in enumerate(far):
-        w = len(fe) // len(far)
-        eng[c] = fe[n * w:(n + 1) * w]
-    for c in dst:
-        if c not in eng:
-            eng[c] = [e for e in topo.engines(core, c) if e not in fe][::len(far)]
-    each = len(eng[dst[0]])
-
-    def send(deps, sem, view, land, to=(0, 1, 2)):
-        need("gc", deps)
-        tr = []
-        for s in to:
-            rid, pid, _ = topo.addr(dst[s])
-            tr.append(RemoteDMATransfer(dst_ids=[DstId(rid=rid, pnc=pid)], dma_engine_mask=sum(1 << e for e in eng[dst[s]]),
-                                        remote_sem=T.sem[sem], src=view(s), dst=land(s)))
-        g.remote_dma_fused(tr, local_sem=T.sem["ls"])
-        cnt["ls"] = cnt.get("ls", 0) + each * len(to)
-        cnt[sem] = cnt.get(sem, 0) + each * len(to)
-        return (sem, cnt[sem])
 
     def ts(o, i, s1, s2, *ops):
         if len(ops) == 1:
@@ -174,10 +126,11 @@ def rank_program(g, core, T, topo):
     SW0, SWs0 = B("SW", 0), B("SWs", 0)
     K = {}
     F_ = lambda c: T.fc[:, c:c + 1]
-    C_ = lambda c: T.fc[:, 10 + c:11 + c]
-    SG, M1, M0, SM1, SM0, AQ, H1, EV, OD, TM, CM, E4, TM1, TM0, SG4, EX0, EX1, EX2, ST = range(19)
-    io64, io8, OE, OE2, rep, vtb = T.cf[:, 0:64], T.cf[:, 64:72], T.cf[:, 72:78], T.cf[:, 78:80], T.cf[:, 80:92], T.cf[:, 92:96]
-    REP, VTL, EXL = T.cl[:, 0:12], T.cl[:, 12:16], T.cl[:, 16:17]
+    C_ = lambda c: T.fc[:, 12 + c:13 + c]
+    M1, M0, AQ, H1, EV, OD, TM, CM, E4, TM1, TM0, SG4, EX0, EX1, EX2, ST, NST, UX0, UX1, UX2, SG, SM0, SM1 = range(23)
+    io64, io8, OE, OE2, vtb = T.cf[:, 0:32], T.cf[:, 64:80], T.cf[:, 80:83], T.cf[:, 86:88], T.cf[:, 92:94]
+    VTL, EXL, UXL = T.cl[:, 12:14], T.cl[:, 16:17], T.cl[:, 18:19]
+    TRL = T.cl[:, 20:22]
     VT, own, XR, R, Dc, cs, sm, Mx = T.VT, T.own, T.XR, T.R, T.Dc, T.cs, T.sm, T.Mx
     so, G, trA, trG, LM = T.so, T.G, T.trA, T.trG, T.LM
     sC, Vc, yd, DD, rk, H = T.sC, T.Vc, T.yd, T.DD, T.rk, T.H
@@ -186,426 +139,435 @@ def rank_program(g, core, T, topo):
     d_z = dma("s", [], T.z0[:], T.z[:, 0:4])
     d_lv = dma("y", [], T.t_lv[:], T.lv[:])
     d_dm = dma("y", [], T.t_dm[:], T.dm[:])
+    d_nz = dma("y", [d_dm], T.t_nz[:], T.nz[:])
+    d_w = dma("y", [d_dm], T.t_w[:], T.w[:])
 
-    i_p = gp([], lambda q: q.iota(T.ii[:, 9:10], [[0, 1]], 0, 1))
+    i_p = gp([], lambda q: q.iota(T.ii[:, 11:12], [[0, 1]], 0, 1))
     v_tin = do("v", [], fill(T.tin[:], TINY))
     v_zer = do("v", [], fill(T.zer[:], 0.0))
     v_si = [do("v", [], fill(T.SI[:, o:o + 128], 0.0)) for o in (0, 512)]
     v_mk = do("v", [], fill(T.MK[:], 1.0))
-    bits = []
-    for c, m in enumerate((15, 32, 64, 63, 48, 112, 16, 3, 12)):
-        bits.append(do("v", [i_p], ts(T.ii[:, c:c + 1], T.ii[:, 9:10], m, None, A.bitwise_and)))
+    bits = [do("v", [i_p], ts(T.ii[:, c:c + 1], T.ii[:, 11:12], m, None, A.bitwise_and)) for c, m in enumerate((15, 32, 64, 63, 48, 112, 16, 3, 12, 6, 1))]
     v_one = do("v", [], fill(T.ones[:], 1.0))
-    v_fc = do("v", bits, cp(T.fc[:, 0:9], T.ii[:, 0:9]))
+    v_fc = do("v", bits, cp(T.fc[:, 0:11], T.ii[:, 0:11]))
     v_mk = do("v", [v_mk], fill(T.MK[:, 2:66:32], 0.0))
-    z_f = do("v", [], fill(T.F0[:, 0:1024], 0.0))
-    v_ss = [do("s", [v_tin], act(T.SS[:, 256 * j:256 * j + 256], T.tin[:], AF.Copy, scale=0.0)) for j in range(4)]
+    v_ss = [do("s", [v_tin], act(T.SS[:, o + b:o + 256:4], T.tin[:, 0:64], AF.Copy, scale=0.0)) for b in range(4) for o in (256 - 256 * (b // 2), 768 - 256 * (b // 2))]
+    z_f = [do("s", [v_tin], act(T.F0[:, o:o + 256], T.tin[:], AF.Copy, scale=0.0)) for o in (512, 768)]
+    z_g = [do("s", [v_tin], act(T.F0[:, o:o + 256], T.tin[:], AF.Copy, scale=0.0)) for o in (0, 256)]
+    K["NEW"] = do("s", [v_tin], act(T.NEW[:, 256:512], T.tin[:], AF.Copy, scale=0.0))
+    K["fo"] = do("v", [], fill(T.fo[:, 0:32], 0.0))
     i_mn = gp([v_tin], lambda q: q.affine_select(T.Mneg[:], T.tin[:], [[0, 2], [1, 128]], A.is_ge, -TINY, 0, -1))
+    i_mt = do("s", [i_mn], act(T.Mtri[:], T.Mneg[:], AF.Copy, scale=-1.0))
     i_kn = gp([], iota(T.Kn[:], [[16, 4], [0, 2], [1, 16]]))
-    K["io"] = [gp([], iota(io64, [[0, 4], [1, 16]])), gp([], iota(rep, [[1, 6], [0, 2]])),
-               gp([], iota(vtb, [[-1, 2], [0, 2]], 2)), gp([], iota(OE, [[-1, 3], [64, 2]], 544))]
+    i_64, i_vt, i_oe = gp([], iota(io64, [[0, 2], [1, 16]])), gp([], iota(vtb, [[-1, 2]], 2)), gp([], iota(OE, [[-1, 3]], 544))
+    i_8, i_o2 = gp([], iota(io8, [[16, 16]])), gp([], iota(OE2, [[64, 2]], 32))
     si = []
     L_, D_, N_ = (0, 64), (64, 128), (0, 128)
     for (p0, p1), r0, r1, e, c, step in (
             (N_, FL1, FL2, 2, 1, 1), (N_, REMA, LBL, 3, 1, 0), (N_, LBD, FL1, 3, 1, 0),
-            (L_, HPL, SEND, 0, 1, 0), (L_, HPL, SEND, 1, 1, 0), (L_, COLL, SEND, 2, 3, 0), (L_, LAL, LBL, 2, 3, 1), (L_, NUML, NUML, 2, 4 * rank, 0),
-            (L_, REMA, LBL, 514, 1, 0), (L_, ULL, None, 0, 1, 1),
-            (D_, SEND, HPD, 0, 1, 0), (D_, SEND, HPD, 1, 1, 0), (D_, SEND, COLD, 2, 7, 0), (D_, LBD, LAD, 2, 4, -1), (D_, NUMD, NUMD, 2, 4 * rank, 0),
-            (D_, LBD, REMB, 514, 1, 0), (D_, ULD, None, 0, 1, 1)):
+            (L_, HPL, SEND, 0, 1, 0), (L_, HPL, SEND, 1, 1, 0), (L_, COLL, SEND, 2, 4, 0), (L_, LAL, LBL, 2, 3, 1), (L_, NUML, NUML, 2, 4 * rank, 0),
+            (L_, REMA, LBL, 514, 1, 0), (L_, ULL, None, 0, 1, 1), (L_, ULL1, None, 1, 1, 1),
+            (D_, SEND, HPD, 0, 1, 0), (D_, SEND, HPD, 1, 1, 0), (D_, LBD, LAD, 2, 4, -1), (D_, NUMD, NUMD, 2, 4 * rank, 0),
+            (D_, LBD, REMB, 514, 1, 0), (D_, ULD, None, 0, 1, 1), (D_, ULD1, None, 1, 1, 1)):
         if r1 is None:
-            si.append(gp([v_si], iota(T.SI[p0:p1, 4 * r0:4 * r0 + 3], [[step, 3]], c), p0 > 0))
-        elif c:
-            si.append(gp([v_si], iota(T.SI[p0:p1, 4 * r0 + e:4 * r1 + e + 1:4], [[step, r1 - r0 + 1]], c), p0 > 0))
-    K["EM"] = gp([v_one], lambda q: q.affine_select(T.EM[:], T.ones[:], [[1, 516]], A.is_equal, 0.0, -3, -4))
-    K["io2"] = [gp([], iota(io8, [[16, 8]])), gp([], iota(OE2, [[64, 2]], 32))]
-
-    uz, cst = [], []
-    for c, src, a, b in ((H1, 5, 1.0, 128.0), (AQ, 2, 4.0, 0.0), (SG, 2, -1 / 32, 1.0)):
-        cst.append(do("s", [v_fc], act(C_(c), F_(src), scale=a, bias=b)))
-    for b in range(4):
-        uz.append(do("v", [d_u, v_one], ts(T.uz[:, b:512:4], T.ones[:, 0:128], T.u0[:, b:b + 1], None, A.mult)))
-    for b in range(4):
-        uz.append(do("s", [d_z, v_zer], act(T.uz[:, 512 + b:1024:4], T.zer[:], bias=T.z0[:, b:b + 1])))
-    q_u = [do("v", uz[0:4], quant(T.qU[:, 0:128], T.sU[:, 0:128], T.uz[:, 0:512]))]
-    K["DG"] = do("v", [K["io"], v_fc], ts(T.DG[:], io64, F_(0), None, A.is_equal))
-    K["cl"] = [do("v", [K["io"]], cp(REP, rep)), do("v", [K["io"], v_fc], ts(VTL, vtb, F_(4), F_(4), A.add, A.add))]
-    q_l = do("v", [d_lv], quant(SW0[:, LB:XB], SWs0[:, LB:XB], T.t_lv[:]))
-    q_u.append(do("v", uz[4:8], quant(T.qU[:, 128:256], T.sU[:, 128:256], T.uz[:, 512:1024])))
+            si.append(gp([v_si], iota(T.SI[p0:p1, 4 * r0:4 * r0 + 3 - e], [[step, 3 - e]], c), p0 > 0))
+        else:
+            out = T.SI[p0:p1, 4 * r0 + e:4 * r1 + e + 1:4]
+            si.append(gp([v_si], iota(out, [[step, r1 - r0 + 1]], c), p0 > 0) if step else
+                      do("s", [v_si, v_one], act(out, T.ones[p0:p1, 0:r1 - r0 + 1], AF.Copy, scale=float(c))))
+    si += [do("s", [v_si, v_one], act(T.SI[p0:p1, 4 * r + 2:4 * r + 3], T.ones[p0:p1, 0:1], AF.Copy, scale=3.25)) for (p0, p1), r in ((L_, ULL1), (D_, ULD1))]
+    d_si = []
+    for o in (0, 512):
+        a = do("s", si, act(T.SI[:, o + 128:o + 256], T.SI[:, o:o + 128], AF.Copy))
+        d_si.append(do("s", [a], act(T.SI[:, o + 256:o + 512], T.SI[:, o:o + 256], AF.Copy)))
+    K["qI"] = [do("v", [d_si[j]], quant(T.qI[:, 128 * j:128 * j + 128], T.sI[:, 128 * j:128 * j + 128], T.SI[:, 512 * j:512 * j + 512])) for j in range(2)]
+    i_em = gp([v_one], lambda q: q.affine_select(T.EM[:], T.ones[:], [[1, 516]], A.is_equal, 0.0, -3, -4))
+    K["qE"] = [do("v", [i_em], quant(T.qE[:, 128 * b:128 * b + 128], T.sE[:, 128 * b:128 * b + 128], T.EM[:, 3 - b:515 - b])) for b in range(4)]
+    K["177"] = [do("s", [v_one], act(Dc[:, 208 * j + 193:208 * j + 194], T.ones[:, 0:1], AF.Copy, scale=177.0)) for j in range(2)]
+    K["F"] = [gp([z_f], iota(T.F0[0:1, 515 + 128 * c:579 + 128 * c:4], [[1, 16]])) for c in range(4)]
+    K["F"] += [do("s", [z_f, v_one], act(T.F0[64:65, 515 + 128 * c:579 + 128 * c:4], T.ones[64:65, 0:16], AF.Copy, scale=16.0 * c)) for c in range(1, 4)]
+    d_f1 = do("s", [K["F"], z_g], act(T.F1[:, 448:1024], T.F0[:, 448:1024], AF.Copy))
+    K["RC"] = gp([], iota(T.RC[:], [[16, 4], [0, 2], [1, 16]], 128))
+    K["IOTA"] = gp([], iota(T.IOTA[:], [[0, 2], [1, 256]]))
+    K["U"] = [gp([], iota(B("UL", t)[:, 192:704], [[16, 16], [0, 2], [1, 16]], -128)) for t in range(ROUNDS)]
+    c_ = {}
+    for c, src, a, b in ((H1, 5, 1.0, 128.0), (AQ, 2, 4.0, 0.0), (M1, 1, 1 / 32, 0.0), (M0, 1, -1 / 32, 1.0), (ST, 2, -TOP / 32, TOP), (NST, 2, TOP / 32, -TOP),
+                         (E4, 3, 4.0, -30.0), (SG4, 2, -1 / 128, 0.25), (EX0, 2, REMB / 64, 0.0), (UX0, 6, 1 / 8, float(ULL)), (SG, 2, -1 / 32, 1.0)):
+        c_[c] = do("s", [v_fc], act(C_(c), F_(src), scale=a, bias=b))
+    c_[TM] = do("s", [c_[ST]], act(C_(TM), F_(2), scale=1 / 64, bias=C_(ST)))
+    c_[CM] = do("s", [c_[TM]], act(C_(CM), C_(TM), bias=-1.0))
+    for c, a in ((TM1, M1), (TM0, M0)):
+        c_[c] = do("s", [c_[a], c_[TM]], act(C_(c), C_(a), scale=C_(TM)))
+    c_[EX1] = do("s", [c_[EX0]], act(C_(EX1), F_(7), scale=32.0, bias=C_(EX0)))
+    c_[EX2] = do("s", [c_[EX1], c_[SG4]], act(C_(EX2), F_(8), scale=C_(SG4), bias=C_(EX1)))
+    c_[UX1] = do("s", [c_[UX0]], act(C_(UX1), F_(9), scale=16.0, bias=C_(UX0)))
+    c_[UX2] = do("s", [c_[UX1]], act(C_(UX2), F_(10), bias=C_(UX1)))
+    uxl = do("v", [c_[UX2]], cp(UXL, C_(UX2)))
+    exl = do("v", [c_[EX2]], cp(EXL, C_(EX2)))
+    K["sgt"] = [do("s", [c_[CM], v_one], act(T.sgt[:, 32 * j:32 * j + 32], T.ones[:, 0:32], AF.Copy, scale=C_((TM, CM)[j]))) for j in range(2)]
+    K["sgu"] = [do("s", [K["sgt"][j], c_[SG]], act(T.sgt[:, 64 + 32 * j:96 + 32 * j], T.sgt[:, 32 * j:32 * j + 32], AF.Copy, scale=C_(SG))) for j in range(2)]
+    for c, a in ((SM1, M1), (SM0, M0)):
+        c_[c] = do("s", [c_[a], c_[SG]], act(C_(c), C_(a), scale=C_(SG)))
+    trl = do("v", [i_8, v_fc], ts(TRL, T.cf[:, 64:66], F_(0), F_(1), A.add, A.add))
+    K["DG"] = do("v", [i_64, v_fc], ts(T.DG[:], io64, F_(0), None, A.is_equal))
+    K["cl"] = do("v", [i_vt, v_fc], ts(VTL, vtb, F_(4), F_(4), A.add, A.add))
+    K["mark"] = [do("s", [K["DG"]], act(VT[:, 48 * j:48 * j + 16], T.DG[:, 0:16], AF.Copy, scale=64.0)) for j in range(2)]
+    K["VO"] = [do("s", [K["DG"]], act(T.VO[:, 32 * s:32 * s + 32], T.DG[:, 0:32], AF.Copy, scale=64.0 * (s + 1))) for s in range(2)]
+    K["Dc"] = [[K["177"][j], do("s", [v_fc], act(Dc[:, 208 * j + 192:208 * j + 193], F_(3), scale=2.0))] for j in range(2)]
+    K["DT"] = do("s", [c_[TM], K["DG"]], act(T.DT[:], T.DG[:, 0:16], AF.Copy, scale=C_(TM)))
+    K["dmp"] = do("s", [i_8, v_fc], act(T.dmp[:], io8, bias=F_(0)))
     sst = []
     for b in range(4):
         t, h = divmod(b, 2)
-        hi = C_(H1) if h else F_(5)
-        sst.append(do("s", [v_ss, v_mk, v_fc], act(T.SS[:, 256 * t + b:256 * t + 256:4], T.MK[:, 0:64], AF.Copy, scale=F_(0))))
-        sst.append(do("s", [cst], act(T.SS[:, 512 + 256 * t + b:768 + 256 * t:4], T.MK[:, 1:65], AF.Copy, scale=hi)))
-    i_mt = do("s", [i_mn], act(T.Mtri[:], T.Mneg[:], AF.Copy, scale=-1.0))
-    v_qs = do("v", sst, quant(T.qS[:], T.sS[:], T.SS[:]))
-    q_x = do("v", [d_dm], quant(SW0[:, XB:704], SWs0[:, XB:704], T.t_dm[:]))
-    d_nz = dma("y", [d_dm], T.t_nz[:], T.nz[:])
-    d_w = dma("y", [], T.t_w[:], T.w[:])
-    d_si = group("y", si, [(T.SI[:, o + 128 * j:o + 128 * j + 128], T.SI[:, o:o + 128]) for o in (0, 512) for j in (1, 2, 3)])
+        sst.append(do("s", [v_mk, v_fc], act(T.SS[:, 256 * t + b:256 * t + 256:4], T.MK[:, 0:64], AF.Copy, scale=F_(0))))
+        sst.append(do("s", [v_mk, v_fc, c_[H1]], act(T.SS[:, 512 + 256 * t + b:768 + 256 * t:4], T.MK[:, 1:65], AF.Copy, scale=C_(H1) if h else F_(5))))
+    v_qs = do("v", [sst, v_ss], quant(T.qS[:], T.sS[:], T.SS[:]))
 
-    def copies(t, x, dep, r):
-        SW, SWs = B("SW", t), B("SWs", t)
-        c0 = XB if x else LB
-        for dn, o, key in ((("LW", XB, "W"), ("XW", 0, "X")) if x else (("LW", LB, "W"), ("LN", 0, "L"))):
-            r.setdefault(key, []).append(group("y", [dep], [(B(dn, t)[:, o:o + 256].bitcast(U8), SW[:, c0:c0 + 256].bitcast(U8)),
-                                                            (B(dn + "s", t)[:, o:o + 256], SWs[:, c0:c0 + 256])]))
+    uz = [do("v", [d_u, v_one], ts(T.uz[:, b:512:4], T.ones[:, 0:128], T.u0[:, b:b + 1], None, A.mult)) for b in range(4)]
+    uz += [do("s", [d_z, v_zer], act(T.uz[:, 512 + b:1024:4], T.zer[:], bias=T.z0[:, b:b + 1])) for b in range(4)]
+    q_u = [do("v", uz[4 * j:4 * j + 4], quant(T.qU[:, 128 * j:128 * j + 128], T.sU[:, 128 * j:128 * j + 128], T.uz[:, 512 * j:512 * j + 512])) for j in range(2)]
+    q_l = do("v", [d_lv], quant(SW0[:, LB:NB], SWs0[:, LB:NB], T.t_lv[:]))
+    q_x = do("v", [d_dm], quant(SW0[:, XB:LB], SWs0[:, XB:LB], T.t_dm[:]))
+    K["nz"] = do("v", [d_nz], quant(T.NZ[:], T.NZs[:], T.t_nz[:]))
+    K["qW"] = do("v", [d_w], quant(T.qW[:], T.sW[:], T.t_w[:]))
 
-    sco = []
+    def copies(t, dep):
+        return group("y", [dep], [(B("XW", t)[:, 0:256].bitcast(U8), B("SW", t)[:, XB:LB].bitcast(U8)), (B("XWs", t)[:, 0:256], B("SWs", t)[:, XB:LB])])
+
+    cps = [copies(0, q_x)]
+    K["np"] = [group("y", [q_l], [(T[n][:, o:o + 64].bitcast(U8), SW0[:, LB:LB + 64].bitcast(U8)), (T[m][:, o:o + 64], SWs0[:, LB:LB + 64])])
+               for n, m, o in (("XW0", "XWs0", 384), ("XW1", "XWs1", 384), ("NP", "NPs", 128))]
+
+    rr, rows = {}, []
+    rcol = [[rk[:, c:c + 1] for c in (132, 133, 134, 131)], [rk[:, c:c + 1] for c in (1, 2, 3, 0)]]
     for ty in range(2):
-        w = LB + 256 * ty
+        w, o = (LB, XB)[ty], 512 * ty
         qu, su = T.qU[:, 128 * ty:128 * ty + 128], T.sU[:, 128 * ty:128 * ty + 128]
         pX, pY = ((T.pA, T.pC), (T.pB, T.pD))[ty]
-        r = do("p", [q_u[ty], (q_l, q_x)[ty]], mm(pX[:, 0:256], qu, su, SW0[:, w:w + 256], SWs0[:, w:w + 256]))
-        for h in range(2):
-            c = do("p", [], mm(pY[:, 512 * h:512 * h + 128], SW0[:, w + 128 * h:w + 128 * h + 128],
-                               SWs0[:, w + 128 * h:w + 128 * h + 128], qu, su))
+        pd = [q_u[ty], (q_l, q_x)[ty]]
+        r = do("p", pd, mm(pX[:, 0:256], qu, su, SW0[:, w:w + 256], SWs0[:, w:w + 256]))
+        c = [do("p", pd, mm(pY[:, 512 * h:512 * h + 128], SW0[:, w + 128 * h:w + 128 * h + 128], SWs0[:, w + 128 * h:w + 128 * h + 128], qu, su)) for h in range(2)]
         ra = do("s", [r], act(Vc[:, 256 * ty:256 * ty + 256], pX[:, 0:256], AF.Abs, bias=LIFT))
         ca = do("s", [c], act(sC[:, 2 * ty:2 * ty + 2], pY[:, 0:1024:512], AF.Abs, bias=LIFT))
         ys = [do("s", [ca, ra], act(yd[:, 256 * ty + 128 * h:256 * ty + 128 * h + 128], Vc[:, 256 * ty + 128 * h:256 * ty + 128 * h + 128],
                                     bias=sC[:, 2 * ty + h:2 * ty + h + 1], scale=-1.0)) for h in range(2)]
-        sco.append((ca, ra, ys))
-    cps = [{}, {}]
-    copies(0, 0, q_l, cps[0])
-    copies(0, 1, q_x, cps[0])
-    K["np"] = group("y", [q_l], [p for t in range(ROUNDS) for p in ((B("NP", t)[:, 0:64].bitcast(U8), SW0[:, LB:LB + 64].bitcast(U8)),
-                                                                    (B("NPs", t)[:, 0:64], SWs0[:, LB:LB + 64]))])
-
-    def ahead(ty):
-        ca, ra, ys = sco[ty]
-        o = 512 * ty
+        rows.append(ra)
         f0, f1, f2 = ((A.is_lt, A.is_le, A.is_gt), (A.is_gt, A.is_ge, A.is_lt))[ty]
         a = do("v", [ca, ra], ts(DD[:, o:o + 128], Vc[:, 256 * ty + 128:256 * ty + 256], sC[:, 2 * ty:2 * ty + 1], None, f0))
         b = do("v", [ca, ra], ts(DD[:, o + 384:o + 512], Vc[:, 256 * ty:256 * ty + 128], sC[:, 2 * ty + 1:2 * ty + 2], None, f1))
-        d = do("v", [ys, i_mn, i_mt], tt(DD[:, o + 128:o + 384], yd[:, 256 * ty:256 * ty + 256], (T.Mneg, T.Mtri)[ty][:], f2))
-        return [a, b, d]
-
-    rr = {}
-    rcol = [[rk[:, c:c + 1] for c in (132, 133, 134, 131)], [rk[:, c:c + 1] for c in (1, 2, 3, 0)]]
-
-    def total(b, dd):
-        rr[b] = do("s", dd, act(DD[:, 256 * b:256 * b + 256], DD[:, 256 * b:256 * b + 256], accum_out=rcol[0][b]))
-
-    dd = ahead(0)
-    total(0, dd)
-    total(1, dd)
-    dd = ahead(1)
-    total(2, dd)
-    rr[3] = do("v", dd, scan(rk[:, 4:132], DD[:, 768:896], DD[:, 896:1024], 0.0))
-    rk2 = do("s", [list(rr.values())], act(rk[:, 0:4], rk[:, 131:135], bias=-64.0))
-    srt = [{}, {}]
-
-    def hot(j, dep):
-        hs = [do("v", [dep(b), i_kn], ts(H[:, 512 * j + b:512 * j + 512:4], T.Kn[:], rcol[j][b], None, A.is_equal)) for b in (0, 1, 3, 2)]
-        qH, sH = T.qH[:, 128 * j:128 * j + 128], T.sH[:, 128 * j:128 * j + 128]
-        qh = do("v", hs, quant(qH, sH, H[:, 512 * j:512 * j + 512]))
-        pX = (T.pD, T.pA)[j]
-        do("p", [qh, v_qs], mm(pX[:, 0:128], T.qS[:, 0:128], T.sS[:, 0:128], qH, sH, True, False))
-        srt[j]["m"] = do("p", [], mm(pX[:, 0:128], T.qS[:, 128:256], T.sS[:, 128:256], qH, sH, False, True))
-
-    def sorted_(j):
-        k = srt[j]
-        k["trA"] = a = do("v", [k["m"]], trn(trA[:, 128 * j:128 * j + 128], (T.pD, T.pA)[j][:, 0:128]))
-        k["of"] = of = do("v", [a, cst[1]], ts(so[:, 4 * j:4 * j + 4], trA[:, 128 * j:128 * j + 128:32], C_(AQ), None, A.add))
-        k["G"] = gs = do("v", [of], cp(G[:, 64 * j:64 * j + 64], Vc[:, 0:512].indirect(so[:, 4 * j:4 * j + 4])))
-        k["M"] = tg = do("v", [gs], trn(trG[:, 64 * j:64 * j + 64], G[:, 64 * j:64 * j + 64]))
-        k["a"] = send([tg], "aM%d" % j, lambda s: trG[:, 64 * j + 31:64 * j + 33], lambda s: LM[:, 8 * j + 2 * s:8 * j + 2 * s + 2])
-
-    hot(0, lambda b: rr[b])
-    K["MS"] = []
-    for s in range(3):
-        low = others[s] < rank
-        if s and low == (others[s - 1] < rank):
-            continue
-        e = s + 1
-        while e < 3 and (others[e] < rank) == low:
-            e += 1
-        K["MS"].append(do("v", [], fill(T.MS[0:64, 64 * s:64 * e], TOP - 1 if low else TOP)))
-        K["MS"].append(do("v", [], fill(T.MS[64:128, 64 * s:64 * e], -TOP if low else 1 - TOP)))
-    for c, src, a, b in ((M1, 1, 1 / 32, 0.0), (M0, 1, -1 / 32, 1.0), (ST, 2, -TOP / 32, TOP), (E4, 3, 4.0, -30.0), (EV, 6, -1 / 16, 1.0), (OD, 6, 1 / 16, 0.0),
-                         (SG4, 2, -1 / 128, 0.25), (EX0, 2, REMB / 64, 0.0)):
-        cst.append(do("s", [v_fc], act(C_(c), F_(src), scale=a, bias=b)))
-    c1 = [do("s", [cst], act(C_(TM), F_(2), scale=1 / 64, bias=C_(ST)))]
-    for c, a, b in ((SM1, M1, SG), (SM0, M0, SG)):
-        c1.append(do("s", [], act(C_(c), C_(a), scale=C_(b))))
-    ex = do("s", [], act(C_(EX1), F_(7), scale=32.0, bias=C_(EX0)))
-    K["sgt"] = do("s", [v_one], act(T.sgt[:], T.ones[:, 0:32], AF.Copy, scale=C_(SG)))
-    K["mark"] = [do("s", [K["DG"]], act(VT[:, 96 * j:96 * j + 32], T.DG[:, 0:32], AF.Copy, scale=64.0)) for j in range(2)]
-    for c, a, b in ((TM1, M1, TM), (TM0, M0, TM)):
-        cst.append(do("s", [c1], act(C_(c), C_(a), scale=C_(b))))
-    cst.append(do("s", [], act(C_(CM), C_(TM), bias=-1.0)))
-    ex = do("s", [ex], act(C_(EX2), F_(8), scale=C_(SG4), bias=C_(EX1)))
-    sorted_(0)
-
-    K["177"] = [gp([], iota(Dc[:, 208 * j + 193:208 * j + 194], [[0, 1]], 177)) for j in range(2)]
-    K["F"] = [gp([z_f], iota(T.F0[0:1, 515:1024:4], [[0, 4], [0, 2], [1, 16]])),
-              gp([z_f], iota(T.F0[64:65, 515:1024:4], [[16, 4], [0, 2], [0, 16]]), True)]
-    d_f1 = dma("y", K["F"], T.F1[:, 512:1024], T.F0[:, 512:1024])
-    K["qE"] = []
-
-    def unpack(b):
-        K["qE"].append(do("v", [K["EM"]], quant(T.qE[:, 128 * b:128 * b + 128], T.sE[:, 128 * b:128 * b + 128], T.EM[:, 3 - b:515 - b])))
-
-    def digits(j):
-        return do("v", [srt[j]["trA"], K["cl"], K["DG"]], tt(VT[:, 96 * j + 32:96 * j + 96], trA[:, 128 * j:128 * j + 128].indirect(VTL), T.DG[:], A.mult))
-
-    def mine(j, o):
-        a = do("s", [srt[j]["M"], cst], act(own[:, o + 1:o + 2], trG[:, 64 * j + 32:64 * j + 33], scale=C_(TM1)))
-        return do("s", [a], act(own[:, o:o + 1], trG[:, 64 * j + 31:64 * j + 32], scale=C_(TM0), bias=own[:, o + 1:o + 2]))
-
-    s_a = mine(0, 0)
-    xo = [do("s", [K["sgt"]], act(XR[:, 192 + 32 * j:224 + 32 * j], T.sgt[:], AF.Copy, scale=trG[:, 31 + j:32 + j])) for j in range(2)]
-    K["VO"] = [do("s", [K["DG"]], act(T.VO[:, 32 * s:32 * s + 32], T.DG[:, 0:32], AF.Copy, scale=64.0 * (s + 1))) for s in range(2)]
-    K["Dc"] = K["177"] + [do("s", [], act(Dc[:, 208 * j + 192:208 * j + 193], F_(3), scale=2.0)) for j in range(2)]
-    K["DT"] = do("s", [cst], act(T.DT[:], T.DG[:, 0:16], AF.Copy, scale=C_(TM)))
-    K["NEW"] = do("s", [v_one], act(T.NEW[:, 0:256], T.ones[:, 0:256], AF.Copy, scale=0.0))
-    K["dmp"] = do("s", [K["io2"]], act(T.dmp[:], T.cf[:, 64:72:2], bias=F_(0)))
-    hot(1, lambda b: rk2)
-    vt = [digits(0)]
-    unpack(0)
-    K["qI"] = do("v", [d_si], quant(T.qI[:], T.sI[:], T.SI[:]))
-    sorted_(1)
-    vt.append(digits(1))
-    exl = do("v", [ex], cp(EXL, C_(EX2)))
-    for b in range(1, 4):
-        unpack(b)
-    t_b = mine(1, 2)
-    p2 = [do("s", [vt[j]], act(Mx[:, 64 * j:64 * j + 64], VT[:, 96 * j + 32:96 * j + 96], accum_out=own[:, 4 + j:5 + j])) for j in range(2)]
-    K["RC"] = gp([], iota(T.RC[:], [[16, 4], [0, 2], [1, 16]], 192))
-    K["ur"] = gp([], iota(T.urow[:], [[16, 16], [0, 2], [1, 16]], -128))
-    K["IOTA"] = gp([], iota(T.IOTA[:], [[0, 2], [2, 256]]))
-    K["U"] = [dma("y", [K["ur"]], B("UL", t)[:, 192:704], T.urow[:]) for t in range(ROUNDS)]
-
-    def signs(q, deps, at, x_of, o):
-        out, seg = [], []
-        for x in x_of:
-            tie = (others + [rank])[x] < q
-            if seg and seg[-1][1] == 64 * x and seg[-1][2] == tie:
-                seg[-1][1] += 64
+        d = [do("v", [ys[h], i_mn, i_mt], tt(DD[:, o + 128 + 128 * h:o + 256 + 128 * h], yd[:, 256 * ty + 128 * h:256 * ty + 128 * h + 128],
+                                             (T.Mneg, T.Mtri)[ty][:, 0:128], f2)) for h in range(2)]
+        for h in range(2):
+            x = 2 * ty + h
+            dd = [(a, b)[h], d[h]]
+            if x < 3:
+                rr[x] = do("s", dd, act(DD[:, 256 * x:256 * x + 256], DD[:, 256 * x:256 * x + 256], accum_out=rcol[0][x]))
             else:
-                seg.append([64 * x, 64 * x + 64, tie])
-        for (c0, c1, tie) in seg:
-            out.append(do("s", deps, act(Dc[:, at:at + c1 - c0], T.yo[:, o + c0:o + c1], AF.Sign, bias=TINY if tie else -TINY)))
-            at += c1 - c0
-        return out
+                rr[x] = do("v", dd, scan(rk[:, 4:132], DD[:, 768:896], DD[:, 896:1024], 0.0))
+    rk2 = do("s", [list(rr.values())], act(rk[:, 0:4], rk[:, 131:135], bias=-64.0))
+
+    srt, vt, p2, thr = [{}, {}], [], [], []
+    for j in range(2):
+        k = srt[j]
+        hs = [do("v", [rk2 if j else rr[b], i_kn], ts(H[:, 512 * j + b:512 * j + 512:4], T.Kn[:], rcol[j][b], None, A.is_equal)) for b in range(4)]
+        qH, sH, pX = T.qH[:, 128 * j:128 * j + 128], T.sH[:, 128 * j:128 * j + 128], (T.pD, T.pA)[j]
+        qh = do("v", hs, quant(qH, sH, H[:, 512 * j:512 * j + 512]))
+        m = do("p", [qh, v_qs], mm(pX[:, 0:128], T.qS[:, 0:128], T.sS[:, 0:128], qH, sH, True, False))
+        m = do("p", [qh, v_qs], mm(pX[:, 0:128], T.qS[:, 128:256], T.sS[:, 128:256], qH, sH, False, True))
+        k["trA"] = a = do("v", [m], trn(trA[:, 128 * j:128 * j + 128], pX[:, 0:128]))
+        k["of"] = of = do("v", [a, c_[AQ]], ts(so[:, 4 * j:4 * j + 4], trA[:, 128 * j:128 * j + 128:32], C_(AQ), None, A.add))
+        if j:
+            src = G[:, 64:128]
+            k["G"] = gs = do("v", [of, rows], cp(src, Vc[:, 0:512].indirect(so[:, 4:8])))
+        else:
+            src = T.Gs[:, 0:64]
+            gs = do("v", [of, rows, c_[SG]], ts(src, Vc[:, 0:512].indirect(so[:, 0:4]), C_(SG), None, A.mult))
+            k["G"] = do("s", [gs], act(G[:, 0:64], src, AF.Copy, scale=C_(SG)))
+            k["T"] = do("v", [gs, trl], cp(T.Gs[:, 64:96], src.indirect(TRL)))
+        tg = do("v", [gs], trn(trG[:, 64 * j:64 * j + 64], src))
+        k["a"] = send([tg], "aM%d" % j, [trG[:, 64 * j + 31:64 * j + 33]] * 3, [LM[:, 8 * j + 2 * s:8 * j + 2 * s + 2] for s in range(3)])
+        vt.append(do("v", [a, K["cl"], K["DG"]], tt(VT[:, 48 * j + 16:48 * j + 48], trA[:, 128 * j:128 * j + 128].indirect(VTL), T.DG[:, 0:32], A.mult)))
+        p2.append(do("s", [vt[j]], act(Mx[:, 256 + 64 * j:288 + 64 * j], VT[:, 48 * j + 16:48 * j + 48], accum_out=own[:, 4 + j:5 + j])))
+    a = do("s", [tg, c_[TM1]], act(own[:, 3:4], trG[:, 96:97], scale=C_(TM1)))
+    thr = [None, do("s", [a, c_[TM0]], act(own[:, 2:3], trG[:, 95:96], scale=C_(TM0), bias=own[:, 3:4]))]
+
+    def spread(dep, j, o, on_v):
+        r, f = [], 0 if j else 64
+        for c in range(6):
+            out, col = XR[:, 192 * j + 32 * c:192 * j + 32 * c + 32], LM[:, 8 * j + c:8 * j + c + 1]
+            if c in on_v:
+                r.append(do("v", [dep, c_[CM], v_one], ts(out, T.ones[:, 0:32], col, C_((TM, CM)[low[c // 2]]), A.mult, A.mult)))
+            else:
+                r.append(do("s", [dep, K["sgt"] if j else K["sgu"]], act(out, T.sgt[:, f + 32 * low[c // 2]:f + 32 * low[c // 2] + 32], AF.Copy, scale=col)))
+        return do("v", r, trn(R[:, o:o + 192], XR[:, 192 * j:192 * j + 192]))
 
     ks = [{}, {}]
 
-    def slots(t, of, n, deps, gaps):
+    def slots(t, of, n, before):
         k, lo, tr2 = ks[t], B("lo", t), B("tr2", t)
         F, qF, sF = T["F%d" % t], B("qF", t), B("sF", t)
-        sc = do("v", [of, vt, K["mark"], K["F"], d_f1], cp(F[:, 0:F.shape[1]].indirect(lo[:, 0:6 * n]), VT[:, 0:96 * n]))
-        k["qF"] = do("v", [sc], quant(qF[:], sF[:], F[:, 512:1024]))
-        m = do("p", [k["qF"], K["qI"], deps], mm(T.pD[:, 512:640], T.qI[:, 0:128], T.sI[:, 0:128], qF[:], sF[:]))
-        k["own2"] = do("p", [], mm(T.pB[:, 0:128], qF[:], sF[:], T.qI[:, 0:128], T.sI[:, 0:128]))
-        gaps[0]()
+        sc = do("v", [of, vt[0:n], K["mark"][0:n], K["F"], d_f1, z_g], cp(F[:, 0:F.shape[1]].indirect(lo[:, 0:3 * n]), VT[:, 0:48 * n]))
+        k["qF"] = do("v", [sc], quant(qF[:], sF[:], F[:, 448:1024]))
+        for o in (16, 0):
+            m = do("p", [k["qF"], K["qI"][0]], mm(T.pD[:, 512:640], T.qI[:, 0:128], T.sI[:, 0:128], qF[:, o:o + 128], sF[:, o:o + 128], o > 0, o == 0))
+        o = 16 - 16 * t
+        k["own2"] = do("p", [k["qF"], K["qI"][0]], mm(T.pB[:, 0:128], qF[:, o:o + 128], sF[:, o:o + 128], T.qI[:, 0:128], T.sI[:, 0:128]))
         k["tr2"] = a = do("v", [m], trn(tr2[:, 0:128], T.pD[:, 512:640]))
-        of = do("v", [a], ts(lo[:, 12:16], tr2[:, SEND:128:32], float(LB), 703.0, A.max, A.min))
-        gaps[1]()
+        of = do("v", [a], ts(lo[:, 12:16], tr2[:, SEND:128:32], NB - 1.0, None, A.min))
+        before()
         pd = [of, k["lt"], k["xt"]]
-        ps = do("v", pd, cp(B("PS", t)[:].bitcast(U32), B("SW", t)[:, 0:704].bitcast(U32).indirect(lo[:, 12:16])))
-        pss = do("s", pd, act(B("PSs", t)[:], B("SWs", t)[:, 0:704].indirect(lo[:, 12:16]), AF.Copy))
+        ps = do("v", pd, cp(B("PS", t)[:].bitcast(U32), B("SW", t)[:, 0:NB].bitcast(U32).indirect(lo[:, 12:16])))
+        pss = do("s", pd, act(B("PSs", t)[:], B("SWs", t)[:, 0:NB].indirect(lo[:, 12:16]), AF.Copy))
         LW, LWs = B("LW", t), B("LWs", t)
-        k["aC"] = send([ps], "aC%d" % t, lambda s: B("PS", t)[:, 0:64].bitcast(U8), lambda s: LW[:, 64 * s:64 * s + 64].bitcast(U8))
-        k["aS"] = send([pss], "aS%d" % t, lambda s: B("PSs", t)[:, 0:64], lambda s: LWs[:, 64 * s:64 * s + 64])
+        k["aC"] = send([ps], "aC%d" % t, [B("PS", t)[:, 0:64].bitcast(U8)] * 3, [LW[:, 64 * s:64 * s + 64].bitcast(U8) for s in range(3)])
+        k["aS"] = send([pss], "aS%d" % t, [B("PSs", t)[:, 0:64]] * 3, [LWs[:, 64 * s:64 * s + 64] for s in range(3)])
+        pd = [[do("v", [a], cp(lo[:, 40 + 4 * j:44 + 4 * j], tr2[:, (COLL, COLD)[j]:128:32])) for j in range(2)], k["lt"], k["xt"]]
+        k["own"] = {"v": do("v", pd, cp(LW[:, 192:320].bitcast(U32), B("SW", t)[:, 0:NB].bitcast(U32).indirect(lo[:, 40:48]))),
+                    "s": do("s", pd, act(LWs[:, 192:320], B("SWs", t)[:, 0:NB].indirect(lo[:, 40:48]), AF.Copy))}
 
     def row(t, r, h=0):
         return B("tr2", t)[:, 128 * h + r:128 * h + 128:32]
 
-    def noise_list(t):
-        ks[t]["nl"] = do("v", [ks[t]["tr2"]], cp(B("lo", t)[:, 24:28], row(t, HPL)))
-
-    def noise(t, deps):
+    def noise(t):
         k, lo = ks[t], B("lo", t)
-        nd_ = [k["nl"], K["nz"], K["np"]]
-        a = do("s", nd_, act(B("NPs", t)[:, 64:128], T.NZs[:, 0:256].indirect(lo[:, 24:28]), AF.Copy))
-        b = do("v", nd_, cp(B("NP", t)[:, 64:128].bitcast(U32), T.NZ[:, 0:256].bitcast(U32).indirect(lo[:, 24:28])))
-        k["dn"] = [do("p", [a, b, K["qE"], deps], mm(T.pC[:, 512 * j:512 * j + 128], T.qE[:, 128 * j:128 * j + 128], T.sE[:, 128 * j:128 * j + 128],
-                                                     B("NP", t)[:], B("NPs", t)[:], True, False)) for j in range(4)]
+        nd_ = [do("v", [k["tr2"]], cp(lo[:, 24:28], row(t, HPL))), K["nz"]]
+        a = do("s", nd_, act(T.NPs[:, 64 - 64 * t:128 - 64 * t], T.NZs[:, 0:256].indirect(lo[:, 24:28]), AF.Copy))
+        b = do("v", nd_, cp(T.NP[:, 64 - 64 * t:128 - 64 * t].bitcast(U32), T.NZ[:, 0:256].bitcast(U32).indirect(lo[:, 24:28])))
+        for j in range(4):
+            do("p", [a, b, K["qE"][j], K["np"][2]], mm(T.pC[:, 512 * j:512 * j + 128], T.qE[:, 128 * j:128 * j + 128], T.sE[:, 128 * j:128 * j + 128],
+                                                       T.NP[:, 64 - 64 * t:192 - 64 * t], T.NPs[:, 64 - 64 * t:192 - 64 * t], True, False))
 
-    def places(t, deps):
-        k, ix, lo, UL = ks[t], B("ix", t), B("lo", t), B("UL", t)
-        e = do("s", [k["tr2"], cst], act(ix[:, 0:4], row(t, ULL), AF.Copy, scale=C_(EV)))
-        e2 = do("s", [], act(ix[:, 4:8], row(t, ULD), AF.Copy, scale=C_(OD)))
-        yield
-        u1 = do("v", [e, e2], tt(ix[:, 8:12], ix[:, 0:4], ix[:, 4:8], A.max))
-        yield
-        u2 = do("v", [u1, K["dmp"]], tt(ix[:, 12:16], ix[:, 8:12], T.dmp[:], A.max))
-        yield
-        uo = [do("v", [u2], ts(lo[:, 48 + h:56:2], ix[:, 12:16], 16.0 * h, None, A.add)) for h in range(2)]
-        yield
+    def places(t):
+        k, ix, lo, UL, trU = ks[t], B("ix", t), B("lo", t), B("UL", t), T.trU
+        u = do("v", [k["tr2"], uxl, K["dmp"]], tt(ix[:, 0:16], B("tr2", t)[:, 0:128].indirect(UXL), T.dmp[:], A.max))
+        uo = do("v", [u], cp(lo[:, 48:56], ix[:, 0:8]))
         us = do("v", [uo, K["RC"], K["U"][t]], cp(UL[:, 0:704].indirect(lo[:, 48:56]), T.RC[:]))
-        yield
-        a = do("v", [us, deps], trn(T.trU[:], UL[:, 192:704]))
-        yield
-        k["pl"] = [do("v", [a], ts(lo[:, 64 + 16 * x:80 + 16 * x], T.trU[:, 16 * x:512:32], 128.0, None, A.add)) for x in range(2)]
-        yield
+        a = do("v", [us], trn(trU[:, 512 * t:512 * t + 512], UL[:, 192:704]))
+        k["pl"] = [do("v", [a], ts(lo[:, 64 + 16 * x:80 + 16 * x], trU[:, 512 * t + 16 * x:512 * t + 512:32], 128.0, None, A.add)) for x in range(2)]
 
-    def arrived(t):
-        k, lo = ks[t], B("lo", t)
+    def arrived(t, on_v):
+        k, lo, NEW = ks[t], B("lo", t), T.NEW
         LW, LWs, XW, XWs = (B(n, t) for n in ("LW", "LWs", "XW", "XWs"))
-        ad = [k["AB"], cps[t]["W"]]
-        b2 = do("s", [ad, k["aS"]], act(XWs[:, 256:320], LWs[:, 0:704].indirect(lo[:, 36:40]), AF.Copy))
-        b1 = do("v", [ad, k["aC"]], cp(XW[:, 256:320].bitcast(U32), LW[:, 0:704].bitcast(U32).indirect(lo[:, 36:40])))
-        k["dc"] = [do("p", [b1, b2, cps[t]["X"]], mm(T.pC[:, 512 * b:512 * b + 128], T.qE[:, 128 * b:128 * b + 128], T.sE[:, 128 * b:128 * b + 128],
-                                                     XW[:, 192:320], XWs[:, 192:320], False, True)) for b in range(4)]
-        a1 = do("v", [], cp(XW[:, 320:384].bitcast(U32), LW[:, 0:704].bitcast(U32).indirect(lo[:, 32:36])))
-        a2 = do("s", [], act(XWs[:, 320:384], LWs[:, 0:704].indirect(lo[:, 32:36]), AF.Copy))
-        k["A"] = {"v": a1, "s": a2}
+        av, as_ = [k["own"]["v"], k["aC"]], [k["own"]["s"], k["aS"]]
+        b2 = do("s", [as_, k["AB"][1]], act(XWs[:, 320:384], LWs[:, 0:320].indirect(lo[:, 36:40]), AF.Copy))
+        b1 = do("v", [av, k["AB"][1]], cp(XW[:, 320:384].bitcast(U32), LW[:, 0:320].bitcast(U32).indirect(lo[:, 36:40])))
+        dc = [do("p", [b1, b2, K["np"][t]], mm(T.pC[:, 512 * b:512 * b + 128], T.qE[:, 128 * b:128 * b + 128], T.sE[:, 128 * b:128 * b + 128],
+                                               XW[:, 320:448], XWs[:, 320:448], False, True)) for b in range(4)]
+        a1 = do("v", [av, k["AB"][0]], cp(XW[:, 256:320].bitcast(U32), LW[:, 0:320].bitcast(U32).indirect(lo[:, 32:36])))
+        a2 = do("s", [as_, k["AB"][0]], act(XWs[:, 256:320], LWs[:, 0:320].indirect(lo[:, 32:36]), AF.Copy))
+        k["A"] = {"v": [a1, b1], "s": [a2, b2]}
+        nw = [do("v", [dc[b]], ts(NEW[:, b:256:4], T.pC[:, 512 * b:512 * b + 64], 0.5, None, A.mult)) if b in on_v else
+              do("s", [dc[b]], act(NEW[:, b:256:4], T.pC[:, 512 * b:512 * b + 64], AF.Copy, scale=0.5)) for b in range(4)]
+        k["qn"] = do("v", [nw, K["NEW"]], quant(B("SW", t)[:, NB:640], B("SWs", t)[:, NB:640], NEW[:]))
 
-    def renew(t, deps):
-        k, NEW = ks[t], T.NEW
-        k["nw"] = [do("v", [k["dc"][b], deps], ts(NEW[:, 256 + b:512:4], T.pC[:, 512 * b + 64:512 * b + 128], 0.5, None, A.mult)) for b in range(4)]
-        k["qn"] = do("v", [k["nw"], K["NEW"]], quant(B("LN", t)[:, 256:384], B("LNs", t)[:, 256:384], NEW[:]))
-
-    def held(t, x, oq, os_, o, qs="vs", c0=0, c1=16):
+    def held(t, x, oq, os_, o, parts=1):
         k, lo = ks[t], B("lo", t)
-        W, Ws = (B("XW", t), B("XWs", t)) if x else (B("LN", t), B("LNs", t))
-        ld = lambda q: [k["pl"], [k["A"][q], cps[t]["X"]] if x else [k["qn"], cps[t]["L"]]]
-        li, r = lo[:, 64 + 16 * x + c0:64 + 16 * x + c1], []
-        if "s" in qs:
-            r.append(do("s", ld("s"), act(os_[:, o + 16 * c0:o + 16 * c1], Ws[:, 0:384].indirect(li), AF.Copy)))
-        if "v" in qs:
-            r.append(do("v", ld("v"), cp(oq[:, o + 16 * c0:o + 16 * c1].bitcast(U32), W[:, 0:384].bitcast(U32).indirect(li))))
+        W, Ws = (B("XW", t)[:, 0:320], B("XWs", t)[:, 0:320]) if x else (B("SW", t)[:, LB:LB + 320], B("SWs", t)[:, LB:LB + 320])
+        ld = lambda q: [k["pl"][x], [k["A"][q], cps[t]] if x else [k["qn"], k["lt"]]]
+        r, n = [[], []], 16 // parts
+        for c in range(0, 16, n):
+            li = lo[:, 64 + 16 * x + c:64 + 16 * x + c + n]
+            r[0].append(do("v", ld("v"), cp(oq[:, o + 16 * c:o + 16 * (c + n)].bitcast(U32), W.bitcast(U32).indirect(li))))
+            r[1].append(do("s", ld("s"), act(os_[:, o + 16 * c:o + 16 * (c + n)], Ws.indirect(li), AF.Copy)))
         return r
 
     k, lo, ix = ks[0], B("lo", 0), B("ix", 0)
     k["lt"], k["xt"] = q_l, q_x
-    XO, RW = 256, 768
+    RW = 512
     aM = srt[0]["a"]
-    a = do("v", [aM, K["cl"], K["MS"]], tt(XR[:, 256:448], LM[:, 0:6].indirect(REP), T.MS[:], A.mult))
-    x1 = do("v", [a], trn(R[:, XO:XO + 192], XR[:, 256:448]))
-    raw = [do("s", [aM, K["sgt"]], act(XR[:, 32 * j:32 * j + 32], T.sgt[:], AF.Copy, scale=LM[:, j:j + 1])) for j in range(6)]
-    d = do("v", [x1, s_a], ts(Dc[:, 624:816], R[:, XO:XO + 192], own[:, 0:1], 4.0, A.is_lt, A.mult))
-    Rt = do("v", [raw, xo], trn(R[:, 0:256], XR[:, 0:256]))
-    c1 = do("v", [d], scan(cs[:, 0:96], Dc[:, 624:720], Dc[:, 720:816], C_(E4)))
+    d = [do("v", [aM, srt[0]["T"]], ts(T.XC[:, 32 * c:32 * c + 32], T.Gs[:, 64:96], LM[:, c:c + 1], 4.0, A.is_ge if low[c // 2] else A.is_gt, A.mult)) for c in range(6)]
+    d = do("v", d, trn(Dc[:, 624:816], T.XC[:]))
+    x1 = spread(aM, 0, 0, ())
+    c1 = do("v", [d, c_[E4]], scan(cs[:, 0:96], Dc[:, 624:720], Dc[:, 720:816], C_(E4)))
     cn = cs[:, 95:96]
     fl = do("v", [c1], ts(sm[:, 0:1], cn, R64, R64, A.add, A.subtract))
-    of = do("v", [fl, K["io"]], ts(lo[:, 0:6], OE, sm[:, 0:1], cn, A.add, A.add))
-    o2 = [do("s", [aM, cst], act(sm[:, 8 + s:9 + s], LM[:, 2 * s + 2:2 * s + 3], scale=C_(SM0))) for s in range(2)]
+    of = do("v", [fl, i_oe], ts(lo[:, 0:3], OE, sm[:, 0:1], cn, A.add, A.add))
+    slots(0, of, 1, lambda: None)
+    c2 = []
     for s in range(2):
-        o2[s] = do("s", [o2[s]], act(sm[:, 10 + s:11 + s], LM[:, 2 * s + 3:2 * s + 4], scale=C_(SM1), bias=sm[:, 8 + s:9 + s]))
-    ys = [do("s", [o2[s], Rt], act(T.yo[:, 256 * s:256 * s + 256], R[:, 0:256], bias=sm[:, 10 + s:11 + s], scale=-1.0)) for s in range(2)]
-    sg = [signs(others[s + 1], [ys[s]], 208 * s, [x for x in range(4) if x != s + 1], 256 * s) for s in range(2)]
-    c2 = [do("s", [sg[s], K["Dc"]], act(Dc[:, 416 + 416 * s:610 + 416 * s], Dc[:, 208 * s:208 * s + 194], scale=2.0, accum_out=sm[:, 4 + s:5 + s])) for s in range(2)]
-    k1 = do("s", [c1], act(sm[:, 16:17], cn, scale=0.25, bias=135.5))
-
-    def gap0():
-        K["nz"] = do("v", [d_nz], quant(T.NZ[:], T.NZs[:], T.t_nz[:]))
-
-    slots(0, of, 1, [srt[1]["trA"]], [gap0, lambda: noise_list(0)])
-    pla = places(0, [])
-    next(pla)
+        q, yo = others[s + 1], T.yo
+        a = do("s", [aM, c_[SM0]], act(sm[:, 8 + s:9 + s], LM[:, 2 * s + 2:2 * s + 3], scale=C_(SM0)))
+        a = do("s", [a, c_[SM1]], act(sm[:, 10 + s:11 + s], LM[:, 2 * s + 3:2 * s + 4], scale=C_(SM1), bias=sm[:, 8 + s:9 + s]))
+        xs = [x for x in range(3) if x != s + 1]
+        b = [sm[:, 24 + 3 * s + f:25 + 3 * s + f] for f in range(3)]
+        o3 = [do("s", [a, c_[CM]], act(b[f], sm[:, 10 + s:11 + s], scale=C_((TM, CM, ST)[f])) if f == 2 or f in [low[x] for x in xs] else None) for f in range(3)]
+        ys = [do("s", [x1, o3[low[x]]], act(yo[:, 192 * s + 64 * n:192 * s + 64 * n + 64], R[:, 64 * x:64 * x + 64], scale=-1.0, bias=b[low[x]])) for n, x in enumerate(xs)]
+        ys.append(do("s", [o3[2], c_[NST], srt[0]["G"]], act(yo[:, 192 * s + 128:192 * s + 192], G[:, 0:64], scale=C_(NST), bias=b[2])))
+        tie = [others[x] < q for x in xs] + [rank < q]
+        sg = []
+        for n in range(3):
+            e = n + 1
+            while e < 3 and tie[e] == tie[n]:
+                e += 1
+            sg.append(do("s", ys, None if n and tie[n - 1] == tie[n] else
+                         act(Dc[:, 208 * s + 64 * n:208 * s + 64 * e], yo[:, 192 * s + 64 * n:192 * s + 64 * e], AF.Sign, bias=TINY if tie[n] else -TINY)))
+        c2.append(do("s", [sg, K["Dc"][s]], act(Dc[:, 416 + 416 * s:610 + 416 * s], Dc[:, 208 * s:208 * s + 194], scale=2.0, accum_out=sm[:, 4 + s:5 + s])))
+    noise(0)
+    places(0)
     fl = do("v", c2, ts(sm[:, 2:4], sm[:, 4:6], R64, R64, A.add, A.subtract))
-    noise(0, [])
-    of = [do("v", [fl, K["io2"]], ts(lo[:, 16 + 2 * s:18 + 2 * s], OE2, sm[:, 2 + s:3 + s], sm[:, 4 + s:5 + s], A.add, A.add)) for s in range(2)]
-    next(pla)
+    of = [do("v", [fl, i_o2], ts(lo[:, 16 + 2 * s:18 + 2 * s], OE2, sm[:, 2 + s:3 + s], sm[:, 4 + s:5 + s], A.add, A.add)) for s in range(2)]
     sc = do("v", [of, K["VO"], k["qF"]], cp(T.F0[:, 0:2560].indirect(lo[:, 16:20]), T.VO[:]))
-    next(pla)
     qg = do("v", [sc], quant(T.qG[:], T.sG[:], T.F0[:, 0:512]))
-    do("p", [k["qF"], srt[0]["trA"]], mm(T.pD[:, 0:128], T.qI[:, 0:128], T.sI[:, 0:128], B("qF", 0)[:], B("sF", 0)[:], True, False))
-    mo = do("p", [qg], mm(T.pD[:, 0:128], T.qI[:, 128:256], T.sI[:, 128:256], T.qG[:], T.sG[:], False, True))
-    w0 = do("s", [k["own2"], cst], act(T.wl[:, 0:2], T.pB[:, NUML:NUMD + 1:NUMD - NUML], AF.Copy, scale=C_(EV)))
-    next(pla)
-    k2 = do("v", [k1], ts(sm[:, 17:18], sm[:, 16:17], 192.0, sm[:, 16:17], A.is_lt, A.mult))
-    next(pla)
+    for o in (16, 0):
+        do("p", [k["qF"], K["qI"][0]], mm(T.pD[:, 0:128], T.qI[:, 0:128], T.sI[:, 0:128], B("qF", 0)[:, o:o + 128], B("sF", 0)[:, o:o + 128], o > 0, False))
+    mo = do("p", [qg, K["qI"][1]], mm(T.pD[:, 0:128], T.qI[:, 128:256], T.sI[:, 128:256], T.qG[:], T.sG[:], False, True))
+    w0 = do("s", [k["own2"]], act(T.wl[:, 0:2], T.pB[:, NUML:NUMD + 1:NUMD - NUML], AF.Copy))
     a = do("v", [mo], trn(B("tr2", 0)[:, 128:256], T.pD[:, 0:128]))
-    k3 = do("v", [k2], ts(lo[:, 112:113], sm[:, 17:18], F_(3), None, A.max))
-    m = [do("v", [a], tt(ix[:, 16 + 4 * j:20 + 4 * j], row(0, (COLL, COLD)[j]), row(0, (REMA, REMB)[j], 1), A.max)) for j in range(2)]
-    next(pla)
-    k["AB"] = do("v", m, cp(lo[:, 32:40], ix[:, 16:24]))
-    next(pla)
+    k["AB"] = [do("v", [a], cp(lo[:, 32 + 4 * j:36 + 4 * j], row(0, (LAL, LBD)[j], 1))) for j in range(2)]
     ex2 = do("v", [a, exl], cp(lo[:, 96:112], B("tr2", 0)[:, 128:256].indirect(EXL)))
-    xp = do("v", [srt[1]["a"]], tt(XR[:, 448:640], LM[:, 8:14].indirect(REP), T.MS[:], A.mult))
-
-    arrived(0)
-    qM, sM = T.qU[:, 64:192], T.sU[:, 64:192]
-    mA = do("p", [list(k["A"].values()), srt[1]["trA"]], mm(T.pA[:, 0:128], qM, sM, B("XW", 0)[:, 256:384], B("XWs", 0)[:, 256:384]))
-    n = ks[1]
-    n["xt"] = held(0, 1, B("SW", 1), B("SWs", 1), XB)
-    copies(1, 1, n["xt"], cps[1])
-    renew(0, [])
-    sA = do("s", [mA], act(G[64:128, 128:192], T.pA[64:128, 64:128], AF.Abs, bias=LIFT))
-    mN = do("p", [k["qn"], w0], mm(T.pB[:, 0:128], qM, sM, B("LN", 0)[:, 256:384], B("LNs", 0)[:, 256:384]))
-    x2 = do("v", [xp], trn(R[:, XO + 192:XO + 384], XR[:, 448:640]))
-    mo_ = do("v", [p2, K["IOTA"], srt[1]["of"]], ts(Mx[:, 0:128], T.IOTA[:, 0:512].indirect(so[:, 0:8]), own[:, 4:5], C_(CM), A.is_ge, A.add))
-    sN = do("s", [mN], act(G[0:64, 128:192], T.pB[0:64, 64:128], AF.Abs, bias=LIFT))
-    tg = do("v", [sA, sN], trn(trG[:, 128:192], G[:, 128:192]))
-    aM = send([tg], "aM2", lambda s: trG[:, 159:161], lambda s: LM[:, 16 + 2 * s:18 + 2 * s])
-
-    a = do("s", [x1, x2, t_b], act(Dc[:, 1040:1424], R[:, XO:XO + 384], AF.Sign, scale=-1.0, bias=own[:, 2:3]))
+    x2 = spread(srt[1]["a"], 1, 192, ())
+    a = do("s", [x1, x2, thr[1]], act(Dc[:, 1040:1424], R[:, 0:384], AF.Sign, scale=-1.0, bias=own[:, 2:3]))
     a = do("s", [a], act(Dc[:, 1424:1808], Dc[:, 1040:1424], AF.Relu, scale=4.0, accum_out=sm[:, 14:15]))
-    base_b = do("s", [a], act(sm[:, 15:16], sm[:, 14:15], bias=C_(E4)))
-    a = do("v", [k3, K["DT"]], tt(cs[:, 416:432], G[:, 0:192].indirect(lo[:, 112:113]), T.DT[:], A.mult))
-    xw = do("v", [mo_, srt[1]["G"]], tt(R[:, XO + 384:XO + 512], G[:, 0:128], Mx[:, 0:128], A.mult))
-    mn = [do("v", [ex2], ts(Mx[:, 128:192], T.IOTA[:, 0:256].indirect(lo[:, 108:112]), own[:, 4:5], C_(CM), A.is_ge, A.add))]
+    base_b = do("s", [a, c_[E4]], act(sm[:, 15:16], sm[:, 14:15], bias=C_(E4)))
+    k1 = do("s", [c1], act(sm[:, 16:17], cn, scale=0.25, bias=135.5))
+    k2 = do("v", [k1], ts(sm[:, 17:18], sm[:, 16:17], 192.0, sm[:, 16:17], A.is_lt, A.mult))
+    k3 = do("v", [k2], ts(lo[:, 112:113], sm[:, 17:18], F_(3), None, A.max))
+    mo_ = do("v", [p2[0], K["IOTA"], srt[0]["of"], srt[1]["of"], c_[CM]], ts(Mx[:, 0:128], T.IOTA[:, 0:512].indirect(so[:, 0:8]), own[:, 4:5], C_(CM), A.is_ge, A.add))
+    xw = do("v", [mo_, srt[0]["G"], srt[1]["G"]], tt(R[:, 384:512], G[:, 0:128], Mx[:, 0:128], A.mult))
+    mn = [do("v", [ex2, p2[j], K["IOTA"], c_[CM]], ts(Mx[:, 128 + 64 * j:192 + 64 * j], T.IOTA[:, 0:256].indirect(lo[:, 108:112]), own[:, 4 + j:5 + j], C_(CM), A.is_ge, A.add))
+          for j in range(2)]
+
+    arrived(0, (1, 3))
+    qM, sM = T.qU[:, 64:192], T.sU[:, 64:192]
+    mA = do("p", [list(k["A"].values())], mm(T.pA[:, 0:128], qM, sM, B("XW", 0)[:, 256:384], B("XWs", 0)[:, 256:384]))
+    sA = do("s", [mA], act(G[64:128, 128:192], T.pA[64:128, 0:64], AF.Abs, bias=LIFT))
+    mN = do("p", [k["qn"]], mm(T.pB[:, 0:128], qM, sM, SW0[:, NB:640], SWs0[:, NB:640]))
+    sN = do("s", [mN], act(G[0:64, 128:192], T.pB[0:64, 0:64], AF.Abs, bias=LIFT))
+    tg = do("v", [sA, sN], trn(trG[:, 128:192], G[:, 128:192]))
+    aM = send([tg], "aM2", [trG[:, 159:161]] * 3, [LM[:, 16 + 2 * s:18 + 2 * s] for s in range(3)])
+    n = ks[1]
+    n["xt"] = held(0, 1, B("SW", 1), B("SWs", 1), XB, 2)
+    cps.append(copies(1, n["xt"]))
+    n["lt"] = held(0, 0, B("SW", 1), B("SWs", 1), LB, 2)
+
+    new = [sA, sN]
+    a = do("v", [k3, K["DT"], new, srt[0]["G"], srt[1]["G"]], tt(cs[:, 416:432], G[:, 0:192].indirect(lo[:, 112:113]), T.DT[:], A.mult))
     t_a = do("v", [a], red(own[:, 6:7], cs[:, 416:432]))
-    mn.append(do("v", [], ts(Mx[:, 192:256], T.IOTA[:, 0:256].indirect(lo[:, 108:112]), own[:, 5:6], C_(CM), A.is_ge, A.add)))
-    d = do("v", [t_a, xw, x2, c2], ts(Dc[:, 0:512], R[:, XO:XO + 512], own[:, 6:7], 4.0, A.is_lt, A.mult))
-    xn = [do("v", [mn[0]], tt(R[:, RW + 192:RW + 256], G[:, 128:192], Mx[:, 128:192], A.mult))]
-    a = do("v", [d], scan(cs[:, 96:352], Dc[:, 0:256], Dc[:, 256:512], -286.0))
-    xn.append(do("v", [mn[1]], tt(R[:, RW + 256:RW + 320], G[:, 128:192], Mx[:, 192:256], A.mult)))
+    d = do("v", [t_a, xw, x1, x2], ts(Dc[:, 2080:2592], R[:, 0:512], own[:, 6:7], 4.0, A.is_lt, A.mult))
+    a = do("v", [d], scan(cs[:, 96:352], Dc[:, 2080:2336], Dc[:, 2336:2592], -286.0))
     base_a = do("v", [a], ts(sm[:, 18:19], cs[:, 351:352], -30.0, None, A.max))
-    n["lt"] = held(0, 0, B("SW", 1), B("SWs", 1), LB, "s")
+    xn = [do("v", [mn[j], new], tt(R[:, RW + 192 + 64 * j:RW + 256 + 64 * j], G[:, 128:192], Mx[:, 128 + 64 * j:192 + 64 * j], A.mult)) for j in range(2)]
 
     l0 = lo
     k, lo, ix = ks[1], B("lo", 1), B("ix", 1)
-    a = do("v", [aM], tt(XR[:, 640:832], LM[:, 16:22].indirect(REP), T.MS[:], A.mult))
-    Rt = do("v", [a], trn(R[:, RW:RW + 192], XR[:, 640:832]))
-    d = [do("v", [Rt, xn, t_a, t_b], ts(Dc[:, 1808 + 64 * j:1872 + 64 * j], R[:, RW:RW + 320].indirect(l0[:, 100 + 4 * j:104 + 4 * j]),
-                                        (own[:, 6:7], own[:, 2:3])[j], 4.0, A.is_lt, A.mult)) for j in range(2)]
-    c = [do("v", [d[j], base_a, base_b], scan(cs[:, 352 + 32 * j:384 + 32 * j], Dc[:, 1808 + 64 * j:1840 + 64 * j], Dc[:, 1840 + 64 * j:1872 + 64 * j],
-                                              (sm[:, 18:19], sm[:, 15:16])[j])) for j in range(2)]
-    fl = [do("v", [c[j]], ts(sm[:, 20 + j:21 + j], cs[:, 383 + 32 * j:384 + 32 * j], R64, R64, A.add, A.subtract)) for j in range(2)]
-    of = [do("v", [fl[j]], ts(lo[:, 6 * j:6 * j + 6], OE, sm[:, 20 + j:21 + j], cs[:, 383 + 32 * j:384 + 32 * j], A.add, A.add)) for j in range(2)]
+    x3 = spread(aM, 2, RW, (0, 1, 2, 3))
+    of = []
+    for j in range(2):
+        d = do("v", [x3, xn, ex2, (t_a, thr[1])[j]], ts(Dc[:, 1808 + 64 * j:1872 + 64 * j], R[:, RW:RW + 320].indirect(l0[:, 100 + 4 * j:104 + 4 * j]),
+                                                       (own[:, 6:7], own[:, 2:3])[j], 4.0, A.is_lt, A.mult))
+        c = do("v", [d, (base_a, base_b)[j]], scan(cs[:, 352 + 32 * j:384 + 32 * j], Dc[:, 1808 + 64 * j:1840 + 64 * j], Dc[:, 1840 + 64 * j:1872 + 64 * j],
+                                                   (sm[:, 18:19], sm[:, 15:16])[j]))
+        fl = do("v", [c], ts(sm[:, 20 + j:21 + j], cs[:, 383 + 32 * j:384 + 32 * j], R64, R64, A.add, A.subtract))
+        of.append(do("v", [fl, i_oe], ts(lo[:, 3 * j:3 * j + 3], OE, sm[:, 20 + j:21 + j], cs[:, 383 + 32 * j:384 + 32 * j], A.add, A.add)))
 
-    def gap0():
-        n["lt"] += held(0, 0, B("SW", 1), B("SWs", 1), LB, "v")
-        copies(1, 0, n["lt"], cps[1])
+    def flags():
+        f = [do("s", [k["tr2"]], act(T.fm[:, 0:4], row(1, FL1), AF.Copy)), do("v", [k["tr2"]], cp(T.fm[:, 8:12], row(1, FL2)))]
+        k["aF"] = send(f, "aF", [None, T.fm[:, 0:4], T.fm[:, 8:12]], [None, T.LF[:, 0:4], T.LF[:, 8:12]], (1, 2))
 
-    def gap1():
-        f = [do("s", [k["tr2"]], act(T.fm[:, 8 * j:8 * j + 4], row(1, (FL1, FL2)[j]), AF.Copy)) for j in range(2)]
-        k["aF"] = send(f, "aF", lambda s: T.fm[:, 8 * s - 8:8 * s - 4], lambda s: T.LF[:, 8 * s - 8:8 * s - 4], (1, 2))
-
-    slots(1, of, 2, [sN, ks[0]["tr2"]], [gap0, gap1])
+    slots(1, of, 2, flags)
     LQ, fo = T.LQ, T.fo
-    w1 = [do("s", [k["own2"], w0], act(LQ[:, 6 + j:7 + j], T.pB[:, (NUML, NUMD)[j]:(NUML, NUMD)[j] + 1], scale=C_(OD), bias=T.wl[:, j:j + 1])) for j in range(2)]
-    pla = places(1, [ks[0]["pl"]])
-    next(pla)
-    noise_list(1)
+    w1 = [do("s", [k["own2"], w0], act(LQ[:, 6 + j:7 + j], T.pB[:, (NUML, NUMD)[j]:(NUML, NUMD)[j] + 1], bias=T.wl[:, j:j + 1])) for j in range(2)]
     wu = do("v", w1, cp(T.wu[:], LQ[:, 6:8]))
-    aP = send([wu], "aP", lambda s: T.wu[:], lambda s: T.LP[:, 2 * s:2 * s + 2])
-    noise(1, [ks[0]["nw"]])
-    next(pla)
-    K["qW"] = do("v", [d_w], quant(T.qW[:], T.sW[:], T.t_w[:]))
-    next(pla)
-    z_o = do("v", [], fill(fo[:, 0:32], 0.0))
-    next(pla)
-    next(pla)
+    aP = send([wu], "aP", [T.wu[:]] * 3, [T.LP[:, 2 * s:2 * s + 2] for s in range(3)])
+    noise(1)
+    places(1)
     a = do("v", [k["aF"]], tt(ix[:, 24:28], T.LF[:, 0:4], T.LF[:, 8:12], A.add))
-    next(pla)
-    m = [do("v", [a], tt(ix[:, 16 + 4 * j:20 + 4 * j], row(1, (COLL, COLD)[j]), ix[:, 24:28], A.max)) for j in range(2)]
-    next(pla)
-    k["AB"] = do("v", m, cp(lo[:, 32:40], ix[:, 16:24]))
-    arrived(1)
+    m = [do("v", [a, k["tr2"]], tt(ix[:, 16 + 4 * j:20 + 4 * j], row(1, (LAL, LBD)[j]), ix[:, 24:28], A.max)) for j in range(2)]
+    k["AB"] = [do("v", m, ts(lo[:, 32:40], ix[:, 16:24], 319.0, None, A.min))] * 2
+    a = do("p", [K["qW"], n["lt"]], mm(T.pA[:, 0:256], T.qW[:], T.sW[:], B("SW", 1)[:, LB:NB], B("SWs", 1)[:, LB:NB]))
+    yo = do("s", [a], act(T.yw[:, 0:256], T.pA[:, 0:256], AF.Copy))
+    arrived(1, (1, 3))
     xt = held(1, 1, T.FN, T.FNs, 256)
-    lq = do("v", [aP], cp(LQ[:, 0:6], T.LP[:]))
-    renew(1, [ks[0]["qn"]])
-    dma("y", xt, T.oc[:, 1024:2048], T.FN[:, 256:512].bitcast(U8), "out")
-    nu = [do("s", [lq, w1, z_o], act(LQ[:, 8 + 4 * j:12 + 4 * j], LQ[:, j:8:2], accum_out=fo[:, j:j + 1])) for j in range(2)]
-    lt = [held(1, 0, T.FN, T.FNs, 0, "vs", 8 * h, 8 * h + 8) for h in range(2)]
-    a = do("v", nu, trn(fo[:, 32:64], fo[:, 0:32]))
-    my = [do("p", [lt[h], K["qW"], sA, w1], mm((T.pA, T.pB)[h][:, 0:128], T.qW[:], T.sW[:], T.FN[:, 128 * h:128 * h + 128], T.FNs[:, 128 * h:128 * h + 128]))
-          for h in range(2)]
-    dma("y", lt, T.oc[:, 0:1024], T.FN[:, 0:256].bitcast(U8), "out")
-    for q in range(4):
-        dma("y", [lt, xt], T.osc[4 * q:4 * q + 4, :], T.FNs[32 * q:32 * q + 4, 0:512], "out")
-    y0 = do("s", [my[0]], act(T.yt[:, 0:128], T.pA[:, 0:128], AF.Copy))
-    y1 = do("v", [my[1]], cp(T.yt[:, 128:256], T.pB[:, 0:128]))
+    lt = held(1, 0, T.FN, T.FNs, 0)
+    my = do("p", [k["qn"], K["qW"]], mm(T.pB[:, 0:128], T.qW[:], T.sW[:], B("SW", 1)[:, NB:640], B("SWs", 1)[:, NB:640]))
+    yn = do("v", [my], cp(T.yw[:, 256:320], T.pB[:, 0:64]))
+    y0 = do("v", [yn, yo, k["pl"][0]], cp(T.yt[:, 0:128], T.yw[:, 0:320].indirect(lo[:, 64:72])))
+    y1 = do("s", [yn, yo, k["pl"][0]], act(T.yt[:, 128:256], T.yw[:, 0:320].indirect(lo[:, 72:80]), AF.Copy))
     dma("s", [y0, y1], T.y[:], T.yt[:], "out")
-    for t in range(ROUNDS):
-        dma("y", [a], T.lw[t:t + 1, :], fo[0:128:32, 32 + 16 * t:48 + 16 * t], "out")
-        dma("y", [a], T.sw[t:t + 1, :], fo[1:128:32, 32 + 16 * t:48 + 16 * t], "out")
+    dma("y", xt[0], T.oc[:, 1024:2048], T.FN[:, 256:512].bitcast(U8), "out")
+    dma("y", lt[0], T.oc[:, 0:1024], T.FN[:, 0:256].bitcast(U8), "out")
+    for q in range(4):
+        dma("ys"[q % 2], [lt[1], xt[1]], T.osc[4 * q:4 * q + 4, :], T.FNs[32 * q:32 * q + 4, 0:512], "out")
+    lq = do("v", [aP], cp(LQ[:, 0:6], T.LP[:]))
+    nu = [do("s", [lq, w1, K["fo"]], act(LQ[:, 8 + 4 * j:12 + 4 * j], LQ[:, j:8:2], accum_out=fo[:, j:j + 1])) for j in range(2)]
+    a = do("v", nu, trn(fo[:, 32:64], fo[:, 0:32]))
+    group("y", [a], [(o[t:t + 1, :], fo[j:128:32, 32 + 16 * t:48 + 16 * t]) for t in range(ROUNDS) for j, o in enumerate((T.lw, T.sw))], "out")
+
+    dst = [cores[q] for q in others]
+    far = [c for c in dst if topo.chip(c) != topo.chip(core)]
+    fe = topo.engines(core, far[0])
+    eng = {}
+    for n, c in enumerate(far):
+        w = len(fe) // len(far)
+        eng[c] = fe[n * w:(n + 1) * w]
+    for c in dst:
+        if c not in eng:
+            rest = [e for e in topo.engines(core, c) if e not in fe]
+            eng[c], spare = rest[::len(far)], rest[1::len(far)]
+            near = {"aM0": eng[c][:len(far)], "aM1": rest, "aS0": spare, "aF": spare, "aS1": spare}
+
+    cnt, top, tok, behind, side, nd = {}, {}, {}, {}, [False], 0
+    know = {q: {} for q in Q}
+    also = {}
+    for a, b in ALSO:
+        also.setdefault(b, []).append(a)
+
+    def need(qn, toks):
+        want = {}
+        for s, n in toks:
+            want[s] = max(want.get(s, 0), n)
+        for s, n in want.items():
+            if know[qn].get(s, 0) >= n or any(behind.get(o, {}).get(s, 0) >= n for o in want.items() if o[0] != s):
+                continue
+            Q[qn].wait_ge(T.sem[s], n)
+            top[s] = max(top.get(s, 0), n)
+        for s, n in want.items():
+            for a, b in list(behind.get((s, n), {}).items()) + [(s, n)]:
+                know[qn][a] = max(know[qn].get(a, 0), b)
+
+    def token(qn, s, step):
+        n = cnt[s] = cnt.get(s, 0) + step
+        k = dict(behind.get((s, n - step), {}))
+        for a, b in know[qn].items():
+            k[a] = max(k.get(a, 0), b)
+        behind[(s, n)] = k
+        return [(s, n)]
+
+    for nid in ORDER or range(len(calls)):
+        kind, qn, deps, what = calls[nid]
+        toks = [x for d in deps + also.get(nid, []) for x in tok[d]]
+        if what is None:
+            tok[nid] = toks
+            continue
+        if kind in ("gp", "upper") and (kind == "upper") != side[0]:
+            side[0] = not side[0]
+            toks.append(("gc", cnt["gc"]))
+        need(qn, toks)
+        if kind == "dma":
+            pairs, s = what
+            if s is None:
+                s, nd = "d%d" % nd, nd + 1
+            for o, i in pairs:
+                Q[qn].dma_start(o, i).then_inc(T.sem[s], 16)
+            tok[nid] = token(qn, s, 16 * len(pairs))
+        elif kind == "send":
+            sem, view, land, to = what
+            tr, n = [], 0
+            for s in to:
+                rid, pid, _ = topo.addr(dst[s])
+                en = fe if dst[s] in far and not [x for x in to if x != s and dst[x] in far] else eng[dst[s]]
+                if dst[s] not in far:
+                    en = near.get(sem, en)
+                n += len(en)
+                tr.append(RemoteDMATransfer(dst_ids=[DstId(rid=rid, pnc=pid)], dma_engine_mask=sum(1 << e for e in en),
+                                            remote_sem=T.sem[sem], src=view[s], dst=land[s]))
+            g.remote_dma_fused(tr, local_sem=T.sem["ls"])
+            cnt["ls"] = cnt.get("ls", 0) + n
+            cnt[sem] = n
+            tok[nid] = [(sem, n)]
+        else:
+            what(Q[qn]).then_inc(T.sem[qn], 1)
+            tok[nid] = token(qn, qn, 1)
     for s, n in cnt.items():
         if top.get(s, 0) < n and s != "out":
             g.wait_ge(T.sem[s], n)

from concourse.bass import DstId, RemoteDMATransfer
from concourse.mybir import dt, AluOpType as A, AxisListType, ActivationFunctionType as AF

F8 = "float8_e4m3fn_x4"
TINY = 2.0 ** -118
LIFT = 2.0 ** -100
TOP = 2.0 ** 24
R64 = 1.5 * 2.0 ** 29
ROUNDS = 2
XB, LB, NB = 0, 256, 512
REMA, LAL, LBL, HPL, NUML, COLL, SEND, COLD, NUMD, HPD, LBD, LAD, REMB, FL1, FL2, ULL, ULL1, ULD, ULD1 = range(19)
_O = ("ahagaxalbvbuaoawaqajaiauakbnavanapabasboaraabibhbgbabjbfbdcoclbccaatamfqazfpbqfmfofnaybpflacdgfkbrfsdpdybecnfradfubyfifgfdftfcdderffgcgecffhfegdbbbtfvfbbsgpccgfgrdqfjgggqdzcjdtgkgigjdfghdegscgglgtaedjgvcmgmafgugxgwgagogygnfygzhdhadshbegcdhedxhfhghhhihjbzcweqcieebwhcdbethuhwcbhtdvbxcheahvfaexhkceephlcpesebhmehdhhpewdrhxdcckdwducyhyeyhzefeledejekczcqeidihoblfwiacreccxhnemibcscueoenichqdabkidinimctilgbijiviojpikisfzithrkbiuipjqifiqirixiyiziedmdkjtkclxkfjrdljajskdkeiwhsevkijbkhkgjcjvjdjwmakljulflgcvlykjjekkjfjzjgknjxjyjhjlkmkamblajijmihlclplblqkulolnlslreuldkojjltbmleiijkkplhjodnktjnkskrljkqkvlllkmfmemjmglumhdomimlliigmmkwmompkxmnmkmqmrlmkzmsmtkyezmumcmdlzmvlvnglwnmnhndmxnfnimwnamzmynsnrnjnonpnqnnnlntnknunynvnznwoanbnxobocodoeofncogneohokojoioupfomonorovfxoypgowppoqolotozphoopqplpapnoppmpcpdpeoxospbpopiprpypspxpwpkpjpvptqbpupzqeqcqaqfqdqtqiqgqhqjqvquqkqnqlqwqoqpqrqmqqqsqx")
ORDER = [26 * (ord(_O[_i]) - 97) + ord(_O[_i + 1]) - 97 for _i in range(0, len(_O), 2)]
ALSO = [(264, 267)]

SCRATCH = {
    "pA": ("psum", [128, 512], "float32"), "pB": ("psum", [128, 512], "float32"), "pC": ("psum", [128, 2048], "float32"),
    "pD": ("psum", [128, 1024], "float32"),
}
for _n, _w, _d in (
        ("t_lv", 1024, "bfloat16"), ("t_dm", 1024, "bfloat16"), ("t_nz", 1024, "bfloat16"), ("t_w", 512, "bfloat16"),
        ("u0", 4, "bfloat16"), ("z0", 4, "bfloat16"), ("uz", 1024, "bfloat16"), ("qU", 256, F8), ("sU", 256, "uint8"),
        ("qW", 128, F8), ("sW", 128, "uint8"), ("ones", 516, "bfloat16"), ("zer", 128, "bfloat16"), ("MK", 66, "bfloat16"),
        ("SS", 1024, "bfloat16"), ("SI", 1024, "bfloat16"), ("EM", 516, "bfloat16"), ("qS", 256, F8), ("sS", 256, "uint8"),
        ("qI", 256, F8), ("sI", 256, "uint8"), ("qE", 512, F8), ("sE", 512, "uint8"), ("NZ", 256, F8), ("NZs", 256, "uint8"),
        ("ii", 12, "int32"), ("fc", 36, "float32"), ("cf", 96, "float32"), ("cl", 32, "uint16"),
        ("tin", 256, "bfloat16"), ("Mneg", 256, "bfloat16"), ("Mtri", 256, "bfloat16"), ("Kn", 128, "bfloat16"), ("RC", 128, "bfloat16"),
        ("dmp", 16, "float32"), ("DG", 32, "bfloat16"), ("DT", 16, "float32"), ("yw", 384, "float32"), ("IOTA", 512, "bfloat16"),
        ("sgt", 128, "float32"), ("Gs", 96, "float32"), ("XC", 192, "bfloat16"), ("VO", 64, "bfloat16"), ("NP", 192, F8), ("NPs", 192, "uint8"),
        ("yt", 256, "float32"), ("FN", 512, F8), ("FNs", 512, "uint8"),
        ("qH", 256, F8), ("sH", 256, "uint8"), ("H", 1024, "bfloat16"), ("qG", 128, F8), ("sG", 128, "uint8"),
        ("NEW", 512, "bfloat16"), ("VT", 96, "bfloat16"), ("sC", 4, "float32"), ("Vc", 512, "float32"), ("yd", 512, "float32"),
        ("yo", 512, "float32"), ("DD", 1024, "bfloat16"), ("rk", 136, "float32"), ("trA", 256, "float32"), ("G", 192, "float32"),
        ("trG", 192, "float32"), ("own", 8, "float32"), ("LM", 24, "float32"), ("XR", 576, "float32"), ("R", 832, "float32"),
        ("Dc", 2592, "bfloat16"), ("cs", 432, "float32"), ("sm", 48, "float32"), ("Mx", 384, "float32"), ("trU", 1024, "bfloat16"),
        ("so", 8, "uint16"), ("fm", 16, "bfloat16"), ("LF", 16, "bfloat16"), ("wl", 4, "float32"), ("wu", 2, "uint16"),
        ("LP", 6, "uint16"), ("LQ", 16, "float32"), ("fo", 64, "float32"), ("F0", 2560, "bfloat16"), ("F1", 5248, "bfloat16")):
    SCRATCH[_n] = ("sbuf", [128, _w], _d)
for _n, _w, _d in (
        ("SW", 640, F8), ("SWs", 640, "uint8"), ("LW", 320, F8), ("LWs", 320, "uint8"), ("XW", 448, F8), ("XWs", 448, "uint8"),
        ("PS", 64, F8), ("PSs", 64, "uint8"),
        ("qF", 144, F8), ("sF", 144, "uint8"), ("tr2", 256, "float32"), ("ix", 32, "float32"), ("UL", 704, "bfloat16"),
        ("lo", 128, "uint16")):
    for _t in range(ROUNDS):
        SCRATCH[_n + str(_t)] = ("sbuf", [128, _w], _d)

SEMAPHORES = ["v", "s", "p", "gc", "ls", "out", "aM0", "aM1", "aM2", "aC0", "aC1", "aS0", "aS1", "aF", "aP"] + ["d%d" % k for k in range(60)]


def rank_program(g, core, T, topo):
    rank = T.rank_of(core)
    if rank is None:
        return
    cores = list(T.cores)
    others = [rank ^ d for d in (3, 1, 2)]
    low = [int(q < rank) for q in others]
    Q = {"v": g.vector, "s": g.scalar, "p": g.tensor, "gc": g, "y": g.sync}
    calls = []

    def flat(deps, out):
        for d in deps:
            if isinstance(d, list):
                flat(d, out)
            elif d is not None:
                out.append(d)
        return out

    def note(kind, qn, deps, what):
        calls.append((kind, qn, flat(deps, []), what))
        return len(calls) - 1

    def do(qn, deps, f):
        return note("do", qn, deps, f)

    def gp(deps, f, upper=False):
        return note("upper" if upper else "gp", "gc", deps, f)

    def group(qn, deps, pairs, s=None):
        return note("dma", qn, deps, (pairs, s))

    def dma(qn, deps, out, in_, s=None):
        return group(qn, deps, [(out, in_)], s)

    def send(deps, sem, view, land, to=(0, 1, 2)):
        return note("send", "gc", deps, (sem, view, land, to))

    def B(n, t):
        return T[n + str(t)]

    def ts(o, i, s1, s2, *ops):
        if len(ops) == 1:
            return lambda q: q.tensor_scalar(o, i, s1, None, ops[0])
        return lambda q: q.tensor_scalar(o, i, s1, s2, ops[0], ops[1])

    def tt(o, a, b, op):
        return lambda q: q.tensor_tensor(o, a, b, op)

    def cp(o, i):
        return lambda q: q.tensor_copy(o, i)

    def act(o, i, fn=AF.Identity, **k):
        return lambda q: q.activation(o, i, fn, **k)

    def red(o, i):
        return lambda q: q.tensor_reduce(o, i, AxisListType.X, A.add)

    def scan(o, a, b, first):
        return lambda q: q.tensor_tensor_scan(o, a, b, first, A.add, A.add)

    def trn(o, i):
        return lambda q: q.transpose(o, i)

    def fill(o, c):
        return lambda q: q.memset(o, c)

    def iota(o, pat, base=0, cm=0):
        return lambda q: q.iota(o, pat, base, cm, allow_small_or_imprecise_dtypes=True)

    def quant(o, s, i):
        return lambda q: q.quantize_mx(o, s, i)

    def mm(o, a, sa, b, sb, st=True, sp=True):
        return lambda q: q.matmul_mx(o, a, sa, b, sb, st, sp)

    U8, U32 = dt.uint8, dt.uint32
    SW0, SWs0 = B("SW", 0), B("SWs", 0)
    K = {}
    F_ = lambda c: T.fc[:, c:c + 1]
    C_ = lambda c: T.fc[:, 12 + c:13 + c]
    M1, M0, AQ, H1, EV, OD, TM, CM, E4, TM1, TM0, SG4, EX0, EX1, EX2, ST, NST, UX0, UX1, UX2, SG, SM0, SM1 = range(23)
    io64, io8, OE, OE2, vtb = T.cf[:, 0:32], T.cf[:, 64:80], T.cf[:, 80:83], T.cf[:, 86:88], T.cf[:, 92:94]
    VTL, EXL, UXL = T.cl[:, 12:14], T.cl[:, 16:17], T.cl[:, 18:19]
    TRL = T.cl[:, 20:22]
    VT, own, XR, R, Dc, cs, sm, Mx = T.VT, T.own, T.XR, T.R, T.Dc, T.cs, T.sm, T.Mx
    so, G, trA, trG, LM = T.so, T.G, T.trA, T.trG, T.LM
    sC, Vc, yd, DD, rk, H = T.sC, T.Vc, T.yd, T.DD, T.rk, T.H

    d_u = dma("s", [], T.u0[:], T.u[:, 0:4])
    d_z = dma("s", [], T.z0[:], T.z[:, 0:4])
    d_lv = dma("y", [], T.t_lv[:], T.lv[:])
    d_dm = dma("y", [], T.t_dm[:], T.dm[:])
    d_nz = dma("y", [d_dm], T.t_nz[:], T.nz[:])
    d_w = dma("y", [d_dm], T.t_w[:], T.w[:])

    i_p = gp([], lambda q: q.iota(T.ii[:, 11:12], [[0, 1]], 0, 1))
    v_tin = do("v", [], fill(T.tin[:], TINY))
    v_zer = do("v", [], fill(T.zer[:], 0.0))
    v_si = [do("v", [], fill(T.SI[:, o:o + 128], 0.0)) for o in (0, 512)]
    v_mk = do("v", [], fill(T.MK[:], 1.0))
    bits = [do("v", [i_p], ts(T.ii[:, c:c + 1], T.ii[:, 11:12], m, None, A.bitwise_and)) for c, m in enumerate((15, 32, 64, 63, 48, 112, 16, 3, 12, 6, 1))]
    v_one = do("v", [], fill(T.ones[:], 1.0))
    v_fc = do("v", bits, cp(T.fc[:, 0:11], T.ii[:, 0:11]))
    v_mk = do("v", [v_mk], fill(T.MK[:, 2:66:32], 0.0))
    v_ss = [do("s", [v_tin], act(T.SS[:, o + b:o + 256:4], T.tin[:, 0:64], AF.Copy, scale=0.0)) for b in range(4) for o in (256 - 256 * (b // 2), 768 - 256 * (b // 2))]
    z_f = [do("s", [v_tin], act(T.F0[:, o:o + 256], T.tin[:], AF.Copy, scale=0.0)) for o in (512, 768)]
    z_g = [do("s", [v_tin], act(T.F0[:, o:o + 256], T.tin[:], AF.Copy, scale=0.0)) for o in (0, 256)]
    K["NEW"] = do("s", [v_tin], act(T.NEW[:, 256:512], T.tin[:], AF.Copy, scale=0.0))
    K["fo"] = do("v", [], fill(T.fo[:, 0:32], 0.0))
    i_mn = gp([v_tin], lambda q: q.affine_select(T.Mneg[:], T.tin[:], [[0, 2], [1, 128]], A.is_ge, -TINY, 0, -1))
    i_mt = do("s", [i_mn], act(T.Mtri[:], T.Mneg[:], AF.Copy, scale=-1.0))
    i_kn = gp([], iota(T.Kn[:], [[16, 4], [0, 2], [1, 16]]))
    i_64, i_vt, i_oe = gp([], iota(io64, [[0, 2], [1, 16]])), gp([], iota(vtb, [[-1, 2]], 2)), gp([], iota(OE, [[-1, 3]], 544))
    i_8, i_o2 = gp([], iota(io8, [[16, 16]])), gp([], iota(OE2, [[64, 2]], 32))
    si = []
    L_, D_, N_ = (0, 64), (64, 128), (0, 128)
    for (p0, p1), r0, r1, e, c, step in (
            (N_, FL1, FL2, 2, 1, 1), (N_, REMA, LBL, 3, 1, 0), (N_, LBD, FL1, 3, 1, 0),
            (L_, HPL, SEND, 0, 1, 0), (L_, HPL, SEND, 1, 1, 0), (L_, COLL, SEND, 2, 4, 0), (L_, LAL, LBL, 2, 3, 1), (L_, NUML, NUML, 2, 4 * rank, 0),
            (L_, REMA, LBL, 514, 1, 0), (L_, ULL, None, 0, 1, 1), (L_, ULL1, None, 1, 1, 1),
            (D_, SEND, HPD, 0, 1, 0), (D_, SEND, HPD, 1, 1, 0), (D_, LBD, LAD, 2, 4, -1), (D_, NUMD, NUMD, 2, 4 * rank, 0),
            (D_, LBD, REMB, 514, 1, 0), (D_, ULD, None, 0, 1, 1), (D_, ULD1, None, 1, 1, 1)):
        if r1 is None:
            si.append(gp([v_si], iota(T.SI[p0:p1, 4 * r0:4 * r0 + 3 - e], [[step, 3 - e]], c), p0 > 0))
        else:
            out = T.SI[p0:p1, 4 * r0 + e:4 * r1 + e + 1:4]
            si.append(gp([v_si], iota(out, [[step, r1 - r0 + 1]], c), p0 > 0) if step else
                      do("s", [v_si, v_one], act(out, T.ones[p0:p1, 0:r1 - r0 + 1], AF.Copy, scale=float(c))))
    si += [do("s", [v_si, v_one], act(T.SI[p0:p1, 4 * r + 2:4 * r + 3], T.ones[p0:p1, 0:1], AF.Copy, scale=3.25)) for (p0, p1), r in ((L_, ULL1), (D_, ULD1))]
    d_si = []
    for o in (0, 512):
        a = do("s", si, act(T.SI[:, o + 128:o + 256], T.SI[:, o:o + 128], AF.Copy))
        d_si.append(do("s", [a], act(T.SI[:, o + 256:o + 512], T.SI[:, o:o + 256], AF.Copy)))
    K["qI"] = [do("v", [d_si[j]], quant(T.qI[:, 128 * j:128 * j + 128], T.sI[:, 128 * j:128 * j + 128], T.SI[:, 512 * j:512 * j + 512])) for j in range(2)]
    i_em = gp([v_one], lambda q: q.affine_select(T.EM[:], T.ones[:], [[1, 516]], A.is_equal, 0.0, -3, -4))
    K["qE"] = [do("v", [i_em], quant(T.qE[:, 128 * b:128 * b + 128], T.sE[:, 128 * b:128 * b + 128], T.EM[:, 3 - b:515 - b])) for b in range(4)]
    K["177"] = [do("s", [v_one], act(Dc[:, 208 * j + 193:208 * j + 194], T.ones[:, 0:1], AF.Copy, scale=177.0)) for j in range(2)]
    K["F"] = [gp([z_f], iota(T.F0[0:1, 515 + 128 * c:579 + 128 * c:4], [[1, 16]])) for c in range(4)]
    K["F"] += [do("s", [z_f, v_one], act(T.F0[64:65, 515 + 128 * c:579 + 128 * c:4], T.ones[64:65, 0:16], AF.Copy, scale=16.0 * c)) for c in range(1, 4)]
    d_f1 = do("s", [K["F"], z_g], act(T.F1[:, 448:1024], T.F0[:, 448:1024], AF.Copy))
    K["RC"] = gp([], iota(T.RC[:], [[16, 4], [0, 2], [1, 16]], 128))
    K["IOTA"] = gp([], iota(T.IOTA[:], [[0, 2], [1, 256]]))
    K["U"] = [gp([], iota(B("UL", t)[:, 192:704], [[16, 16], [0, 2], [1, 16]], -128)) for t in range(ROUNDS)]
    c_ = {}
    for c, src, a, b in ((H1, 5, 1.0, 128.0), (AQ, 2, 4.0, 0.0), (M1, 1, 1 / 32, 0.0), (M0, 1, -1 / 32, 1.0), (ST, 2, -TOP / 32, TOP), (NST, 2, TOP / 32, -TOP),
                         (E4, 3, 4.0, -30.0), (SG4, 2, -1 / 128, 0.25), (EX0, 2, REMB / 64, 0.0), (UX0, 6, 1 / 8, float(ULL)), (SG, 2, -1 / 32, 1.0)):
        c_[c] = do("s", [v_fc], act(C_(c), F_(src), scale=a, bias=b))
    c_[TM] = do("s", [c_[ST]], act(C_(TM), F_(2), scale=1 / 64, bias=C_(ST)))
    c_[CM] = do("s", [c_[TM]], act(C_(CM), C_(TM), bias=-1.0))
    for c, a in ((TM1, M1), (TM0, M0)):
        c_[c] = do("s", [c_[a], c_[TM]], act(C_(c), C_(a), scale=C_(TM)))
    c_[EX1] = do("s", [c_[EX0]], act(C_(EX1), F_(7), scale=32.0, bias=C_(EX0)))
    c_[EX2] = do("s", [c_[EX1], c_[SG4]], act(C_(EX2), F_(8), scale=C_(SG4), bias=C_(EX1)))
    c_[UX1] = do("s", [c_[UX0]], act(C_(UX1), F_(9), scale=16.0, bias=C_(UX0)))
    c_[UX2] = do("s", [c_[UX1]], act(C_(UX2), F_(10), bias=C_(UX1)))
    uxl = do("v", [c_[UX2]], cp(UXL, C_(UX2)))
    exl = do("v", [c_[EX2]], cp(EXL, C_(EX2)))
    K["sgt"] = [do("s", [c_[CM], v_one], act(T.sgt[:, 32 * j:32 * j + 32], T.ones[:, 0:32], AF.Copy, scale=C_((TM, CM)[j]))) for j in range(2)]
    K["sgu"] = [do("s", [K["sgt"][j], c_[SG]], act(T.sgt[:, 64 + 32 * j:96 + 32 * j], T.sgt[:, 32 * j:32 * j + 32], AF.Copy, scale=C_(SG))) for j in range(2)]
    for c, a in ((SM1, M1), (SM0, M0)):
        c_[c] = do("s", [c_[a], c_[SG]], act(C_(c), C_(a), scale=C_(SG)))
    trl = do("v", [i_8, v_fc], ts(TRL, T.cf[:, 64:66], F_(0), F_(1), A.add, A.add))
    K["DG"] = do("v", [i_64, v_fc], ts(T.DG[:], io64, F_(0), None, A.is_equal))
    K["cl"] = do("v", [i_vt, v_fc], ts(VTL, vtb, F_(4), F_(4), A.add, A.add))
    K["mark"] = [do("s", [K["DG"]], act(VT[:, 48 * j:48 * j + 16], T.DG[:, 0:16], AF.Copy, scale=64.0)) for j in range(2)]
    K["VO"] = [do("s", [K["DG"]], act(T.VO[:, 32 * s:32 * s + 32], T.DG[:, 0:32], AF.Copy, scale=64.0 * (s + 1))) for s in range(2)]
    K["Dc"] = [[K["177"][j], do("s", [v_fc], act(Dc[:, 208 * j + 192:208 * j + 193], F_(3), scale=2.0))] for j in range(2)]
    K["DT"] = do("s", [c_[TM], K["DG"]], act(T.DT[:], T.DG[:, 0:16], AF.Copy, scale=C_(TM)))
    K["dmp"] = do("s", [i_8, v_fc], act(T.dmp[:], io8, bias=F_(0)))
    sst = []
    for b in range(4):
        t, h = divmod(b, 2)
        sst.append(do("s", [v_mk, v_fc], act(T.SS[:, 256 * t + b:256 * t + 256:4], T.MK[:, 0:64], AF.Copy, scale=F_(0))))
        sst.append(do("s", [v_mk, v_fc, c_[H1]], act(T.SS[:, 512 + 256 * t + b:768 + 256 * t:4], T.MK[:, 1:65], AF.Copy, scale=C_(H1) if h else F_(5))))
    v_qs = do("v", [sst, v_ss], quant(T.qS[:], T.sS[:], T.SS[:]))

    uz = [do("v", [d_u, v_one], ts(T.uz[:, b:512:4], T.ones[:, 0:128], T.u0[:, b:b + 1], None, A.mult)) for b in range(4)]
    uz += [do("s", [d_z, v_zer], act(T.uz[:, 512 + b:1024:4], T.zer[:], bias=T.z0[:, b:b + 1])) for b in range(4)]
    q_u = [do("v", uz[4 * j:4 * j + 4], quant(T.qU[:, 128 * j:128 * j + 128], T.sU[:, 128 * j:128 * j + 128], T.uz[:, 512 * j:512 * j + 512])) for j in range(2)]
    q_l = do("v", [d_lv], quant(SW0[:, LB:NB], SWs0[:, LB:NB], T.t_lv[:]))
    q_x = do("v", [d_dm], quant(SW0[:, XB:LB], SWs0[:, XB:LB], T.t_dm[:]))
    K["nz"] = do("v", [d_nz], quant(T.NZ[:], T.NZs[:], T.t_nz[:]))
    K["qW"] = do("v", [d_w], quant(T.qW[:], T.sW[:], T.t_w[:]))

    def copies(t, dep):
        return group("y", [dep], [(B("XW", t)[:, 0:256].bitcast(U8), B("SW", t)[:, XB:LB].bitcast(U8)), (B("XWs", t)[:, 0:256], B("SWs", t)[:, XB:LB])])

    cps = [copies(0, q_x)]
    K["np"] = [group("y", [q_l], [(T[n][:, o:o + 64].bitcast(U8), SW0[:, LB:LB + 64].bitcast(U8)), (T[m][:, o:o + 64], SWs0[:, LB:LB + 64])])
               for n, m, o in (("XW0", "XWs0", 384), ("XW1", "XWs1", 384), ("NP", "NPs", 128))]

    rr, rows = {}, []
    rcol = [[rk[:, c:c + 1] for c in (132, 133, 134, 131)], [rk[:, c:c + 1] for c in (1, 2, 3, 0)]]
    for ty in range(2):
        w, o = (LB, XB)[ty], 512 * ty
        qu, su = T.qU[:, 128 * ty:128 * ty + 128], T.sU[:, 128 * ty:128 * ty + 128]
        pX, pY = ((T.pA, T.pC), (T.pB, T.pD))[ty]
        pd = [q_u[ty], (q_l, q_x)[ty]]
        r = do("p", pd, mm(pX[:, 0:256], qu, su, SW0[:, w:w + 256], SWs0[:, w:w + 256]))
        c = [do("p", pd, mm(pY[:, 512 * h:512 * h + 128], SW0[:, w + 128 * h:w + 128 * h + 128], SWs0[:, w + 128 * h:w + 128 * h + 128], qu, su)) for h in range(2)]
        ra = do("s", [r], act(Vc[:, 256 * ty:256 * ty + 256], pX[:, 0:256], AF.Abs, bias=LIFT))
        ca = do("s", [c], act(sC[:, 2 * ty:2 * ty + 2], pY[:, 0:1024:512], AF.Abs, bias=LIFT))
        ys = [do("s", [ca, ra], act(yd[:, 256 * ty + 128 * h:256 * ty + 128 * h + 128], Vc[:, 256 * ty + 128 * h:256 * ty + 128 * h + 128],
                                    bias=sC[:, 2 * ty + h:2 * ty + h + 1], scale=-1.0)) for h in range(2)]
        rows.append(ra)
        f0, f1, f2 = ((A.is_lt, A.is_le, A.is_gt), (A.is_gt, A.is_ge, A.is_lt))[ty]
        a = do("v", [ca, ra], ts(DD[:, o:o + 128], Vc[:, 256 * ty + 128:256 * ty + 256], sC[:, 2 * ty:2 * ty + 1], None, f0))
        b = do("v", [ca, ra], ts(DD[:, o + 384:o + 512], Vc[:, 256 * ty:256 * ty + 128], sC[:, 2 * ty + 1:2 * ty + 2], None, f1))
        d = [do("v", [ys[h], i_mn, i_mt], tt(DD[:, o + 128 + 128 * h:o + 256 + 128 * h], yd[:, 256 * ty + 128 * h:256 * ty + 128 * h + 128],
                                             (T.Mneg, T.Mtri)[ty][:, 0:128], f2)) for h in range(2)]
        for h in range(2):
            x = 2 * ty + h
            dd = [(a, b)[h], d[h]]
            if x < 3:
                rr[x] = do("s", dd, act(DD[:, 256 * x:256 * x + 256], DD[:, 256 * x:256 * x + 256], accum_out=rcol[0][x]))
            else:
                rr[x] = do("v", dd, scan(rk[:, 4:132], DD[:, 768:896], DD[:, 896:1024], 0.0))
    rk2 = do("s", [list(rr.values())], act(rk[:, 0:4], rk[:, 131:135], bias=-64.0))

    srt, vt, p2, thr = [{}, {}], [], [], []
    for j in range(2):
        k = srt[j]
        hs = [do("v", [rk2 if j else rr[b], i_kn], ts(H[:, 512 * j + b:512 * j + 512:4], T.Kn[:], rcol[j][b], None, A.is_equal)) for b in range(4)]
        qH, sH, pX = T.qH[:, 128 * j:128 * j + 128], T.sH[:, 128 * j:128 * j + 128], (T.pD, T.pA)[j]
        qh = do("v", hs, quant(qH, sH, H[:, 512 * j:512 * j + 512]))
        m = do("p", [qh, v_qs], mm(pX[:, 0:128], T.qS[:, 0:128], T.sS[:, 0:128], qH, sH, True, False))
        m = do("p", [qh, v_qs], mm(pX[:, 0:128], T.qS[:, 128:256], T.sS[:, 128:256], qH, sH, False, True))
        k["trA"] = a = do("v", [m], trn(trA[:, 128 * j:128 * j + 128], pX[:, 0:128]))
        k["of"] = of = do("v", [a, c_[AQ]], ts(so[:, 4 * j:4 * j + 4], trA[:, 128 * j:128 * j + 128:32], C_(AQ), None, A.add))
        if j:
            src = G[:, 64:128]
            k["G"] = gs = do("v", [of, rows], cp(src, Vc[:, 0:512].indirect(so[:, 4:8])))
        else:
            src = T.Gs[:, 0:64]
            gs = do("v", [of, rows, c_[SG]], ts(src, Vc[:, 0:512].indirect(so[:, 0:4]), C_(SG), None, A.mult))
            k["G"] = do("s", [gs], act(G[:, 0:64], src, AF.Copy, scale=C_(SG)))
            k["T"] = do("v", [gs, trl], cp(T.Gs[:, 64:96], src.indirect(TRL)))
        tg = do("v", [gs], trn(trG[:, 64 * j:64 * j + 64], src))
        k["a"] = send([tg], "aM%d" % j, [trG[:, 64 * j + 31:64 * j + 33]] * 3, [LM[:, 8 * j + 2 * s:8 * j + 2 * s + 2] for s in range(3)])
        vt.append(do("v", [a, K["cl"], K["DG"]], tt(VT[:, 48 * j + 16:48 * j + 48], trA[:, 128 * j:128 * j + 128].indirect(VTL), T.DG[:, 0:32], A.mult)))
        p2.append(do("s", [vt[j]], act(Mx[:, 256 + 64 * j:288 + 64 * j], VT[:, 48 * j + 16:48 * j + 48], accum_out=own[:, 4 + j:5 + j])))
    a = do("s", [tg, c_[TM1]], act(own[:, 3:4], trG[:, 96:97], scale=C_(TM1)))
    thr = [None, do("s", [a, c_[TM0]], act(own[:, 2:3], trG[:, 95:96], scale=C_(TM0), bias=own[:, 3:4]))]

    def spread(dep, j, o, on_v):
        r, f = [], 0 if j else 64
        for c in range(6):
            out, col = XR[:, 192 * j + 32 * c:192 * j + 32 * c + 32], LM[:, 8 * j + c:8 * j + c + 1]
            if c in on_v:
                r.append(do("v", [dep, c_[CM], v_one], ts(out, T.ones[:, 0:32], col, C_((TM, CM)[low[c // 2]]), A.mult, A.mult)))
            else:
                r.append(do("s", [dep, K["sgt"] if j else K["sgu"]], act(out, T.sgt[:, f + 32 * low[c // 2]:f + 32 * low[c // 2] + 32], AF.Copy, scale=col)))
        return do("v", r, trn(R[:, o:o + 192], XR[:, 192 * j:192 * j + 192]))

    ks = [{}, {}]

    def slots(t, of, n, before):
        k, lo, tr2 = ks[t], B("lo", t), B("tr2", t)
        F, qF, sF = T["F%d" % t], B("qF", t), B("sF", t)
        sc = do("v", [of, vt[0:n], K["mark"][0:n], K["F"], d_f1, z_g], cp(F[:, 0:F.shape[1]].indirect(lo[:, 0:3 * n]), VT[:, 0:48 * n]))
        k["qF"] = do("v", [sc], quant(qF[:], sF[:], F[:, 448:1024]))
        for o in (16, 0):
            m = do("p", [k["qF"], K["qI"][0]], mm(T.pD[:, 512:640], T.qI[:, 0:128], T.sI[:, 0:128], qF[:, o:o + 128], sF[:, o:o + 128], o > 0, o == 0))
        o = 16 - 16 * t
        k["own2"] = do("p", [k["qF"], K["qI"][0]], mm(T.pB[:, 0:128], qF[:, o:o + 128], sF[:, o:o + 128], T.qI[:, 0:128], T.sI[:, 0:128]))
        k["tr2"] = a = do("v", [m], trn(tr2[:, 0:128], T.pD[:, 512:640]))
        of = do("v", [a], ts(lo[:, 12:16], tr2[:, SEND:128:32], NB - 1.0, None, A.min))
        before()
        pd = [of, k["lt"], k["xt"]]
        ps = do("v", pd, cp(B("PS", t)[:].bitcast(U32), B("SW", t)[:, 0:NB].bitcast(U32).indirect(lo[:, 12:16])))
        pss = do("s", pd, act(B("PSs", t)[:], B("SWs", t)[:, 0:NB].indirect(lo[:, 12:16]), AF.Copy))
        LW, LWs = B("LW", t), B("LWs", t)
        k["aC"] = send([ps], "aC%d" % t, [B("PS", t)[:, 0:64].bitcast(U8)] * 3, [LW[:, 64 * s:64 * s + 64].bitcast(U8) for s in range(3)])
        k["aS"] = send([pss], "aS%d" % t, [B("PSs", t)[:, 0:64]] * 3, [LWs[:, 64 * s:64 * s + 64] for s in range(3)])
        pd = [[do("v", [a], cp(lo[:, 40 + 4 * j:44 + 4 * j], tr2[:, (COLL, COLD)[j]:128:32])) for j in range(2)], k["lt"], k["xt"]]
        k["own"] = {"v": do("v", pd, cp(LW[:, 192:320].bitcast(U32), B("SW", t)[:, 0:NB].bitcast(U32).indirect(lo[:, 40:48]))),
                    "s": do("s", pd, act(LWs[:, 192:320], B("SWs", t)[:, 0:NB].indirect(lo[:, 40:48]), AF.Copy))}

    def row(t, r, h=0):
        return B("tr2", t)[:, 128 * h + r:128 * h + 128:32]

    def noise(t):
        k, lo = ks[t], B("lo", t)
        nd_ = [do("v", [k["tr2"]], cp(lo[:, 24:28], row(t, HPL))), K["nz"]]
        a = do("s", nd_, act(T.NPs[:, 64 - 64 * t:128 - 64 * t], T.NZs[:, 0:256].indirect(lo[:, 24:28]), AF.Copy))
        b = do("v", nd_, cp(T.NP[:, 64 - 64 * t:128 - 64 * t].bitcast(U32), T.NZ[:, 0:256].bitcast(U32).indirect(lo[:, 24:28])))
        for j in range(4):
            do("p", [a, b, K["qE"][j], K["np"][2]], mm(T.pC[:, 512 * j:512 * j + 128], T.qE[:, 128 * j:128 * j + 128], T.sE[:, 128 * j:128 * j + 128],
                                                       T.NP[:, 64 - 64 * t:192 - 64 * t], T.NPs[:, 64 - 64 * t:192 - 64 * t], True, False))

    def places(t):
        k, ix, lo, UL, trU = ks[t], B("ix", t), B("lo", t), B("UL", t), T.trU
        u = do("v", [k["tr2"], uxl, K["dmp"]], tt(ix[:, 0:16], B("tr2", t)[:, 0:128].indirect(UXL), T.dmp[:], A.max))
        uo = do("v", [u], cp(lo[:, 48:56], ix[:, 0:8]))
        us = do("v", [uo, K["RC"], K["U"][t]], cp(UL[:, 0:704].indirect(lo[:, 48:56]), T.RC[:]))
        a = do("v", [us], trn(trU[:, 512 * t:512 * t + 512], UL[:, 192:704]))
        k["pl"] = [do("v", [a], ts(lo[:, 64 + 16 * x:80 + 16 * x], trU[:, 512 * t + 16 * x:512 * t + 512:32], 128.0, None, A.add)) for x in range(2)]

    def arrived(t, on_v):
        k, lo, NEW = ks[t], B("lo", t), T.NEW
        LW, LWs, XW, XWs = (B(n, t) for n in ("LW", "LWs", "XW", "XWs"))
        av, as_ = [k["own"]["v"], k["aC"]], [k["own"]["s"], k["aS"]]
        b2 = do("s", [as_, k["AB"][1]], act(XWs[:, 320:384], LWs[:, 0:320].indirect(lo[:, 36:40]), AF.Copy))
        b1 = do("v", [av, k["AB"][1]], cp(XW[:, 320:384].bitcast(U32), LW[:, 0:320].bitcast(U32).indirect(lo[:, 36:40])))
        dc = [do("p", [b1, b2, K["np"][t]], mm(T.pC[:, 512 * b:512 * b + 128], T.qE[:, 128 * b:128 * b + 128], T.sE[:, 128 * b:128 * b + 128],
                                               XW[:, 320:448], XWs[:, 320:448], False, True)) for b in range(4)]
        a1 = do("v", [av, k["AB"][0]], cp(XW[:, 256:320].bitcast(U32), LW[:, 0:320].bitcast(U32).indirect(lo[:, 32:36])))
        a2 = do("s", [as_, k["AB"][0]], act(XWs[:, 256:320], LWs[:, 0:320].indirect(lo[:, 32:36]), AF.Copy))
        k["A"] = {"v": [a1, b1], "s": [a2, b2]}
        nw = [do("v", [dc[b]], ts(NEW[:, b:256:4], T.pC[:, 512 * b:512 * b + 64], 0.5, None, A.mult)) if b in on_v else
              do("s", [dc[b]], act(NEW[:, b:256:4], T.pC[:, 512 * b:512 * b + 64], AF.Copy, scale=0.5)) for b in range(4)]
        k["qn"] = do("v", [nw, K["NEW"]], quant(B("SW", t)[:, NB:640], B("SWs", t)[:, NB:640], NEW[:]))

    def held(t, x, oq, os_, o, parts=1):
        k, lo = ks[t], B("lo", t)
        W, Ws = (B("XW", t)[:, 0:320], B("XWs", t)[:, 0:320]) if x else (B("SW", t)[:, LB:LB + 320], B("SWs", t)[:, LB:LB + 320])
        ld = lambda q: [k["pl"][x], [k["A"][q], cps[t]] if x else [k["qn"], k["lt"]]]
        r, n = [[], []], 16 // parts
        for c in range(0, 16, n):
            li = lo[:, 64 + 16 * x + c:64 + 16 * x + c + n]
            r[0].append(do("v", ld("v"), cp(oq[:, o + 16 * c:o + 16 * (c + n)].bitcast(U32), W.bitcast(U32).indirect(li))))
            r[1].append(do("s", ld("s"), act(os_[:, o + 16 * c:o + 16 * (c + n)], Ws.indirect(li), AF.Copy)))
        return r

    k, lo, ix = ks[0], B("lo", 0), B("ix", 0)
    k["lt"], k["xt"] = q_l, q_x
    RW = 512
    aM = srt[0]["a"]
    d = [do("v", [aM, srt[0]["T"]], ts(T.XC[:, 32 * c:32 * c + 32], T.Gs[:, 64:96], LM[:, c:c + 1], 4.0, A.is_ge if low[c // 2] else A.is_gt, A.mult)) for c in range(6)]
    d = do("v", d, trn(Dc[:, 624:816], T.XC[:]))
    x1 = spread(aM, 0, 0, ())
    c1 = do("v", [d, c_[E4]], scan(cs[:, 0:96], Dc[:, 624:720], Dc[:, 720:816], C_(E4)))
    cn = cs[:, 95:96]
    fl = do("v", [c1], ts(sm[:, 0:1], cn, R64, R64, A.add, A.subtract))
    of = do("v", [fl, i_oe], ts(lo[:, 0:3], OE, sm[:, 0:1], cn, A.add, A.add))
    slots(0, of, 1, lambda: None)
    c2 = []
    for s in range(2):
        q, yo = others[s + 1], T.yo
        a = do("s", [aM, c_[SM0]], act(sm[:, 8 + s:9 + s], LM[:, 2 * s + 2:2 * s + 3], scale=C_(SM0)))
        a = do("s", [a, c_[SM1]], act(sm[:, 10 + s:11 + s], LM[:, 2 * s + 3:2 * s + 4], scale=C_(SM1), bias=sm[:, 8 + s:9 + s]))
        xs = [x for x in range(3) if x != s + 1]
        b = [sm[:, 24 + 3 * s + f:25 + 3 * s + f] for f in range(3)]
        o3 = [do("s", [a, c_[CM]], act(b[f], sm[:, 10 + s:11 + s], scale=C_((TM, CM, ST)[f])) if f == 2 or f in [low[x] for x in xs] else None) for f in range(3)]
        ys = [do("s", [x1, o3[low[x]]], act(yo[:, 192 * s + 64 * n:192 * s + 64 * n + 64], R[:, 64 * x:64 * x + 64], scale=-1.0, bias=b[low[x]])) for n, x in enumerate(xs)]
        ys.append(do("s", [o3[2], c_[NST], srt[0]["G"]], act(yo[:, 192 * s + 128:192 * s + 192], G[:, 0:64], scale=C_(NST), bias=b[2])))
        tie = [others[x] < q for x in xs] + [rank < q]
        sg = []
        for n in range(3):
            e = n + 1
            while e < 3 and tie[e] == tie[n]:
                e += 1
            sg.append(do("s", ys, None if n and tie[n - 1] == tie[n] else
                         act(Dc[:, 208 * s + 64 * n:208 * s + 64 * e], yo[:, 192 * s + 64 * n:192 * s + 64 * e], AF.Sign, bias=TINY if tie[n] else -TINY)))
        c2.append(do("s", [sg, K["Dc"][s]], act(Dc[:, 416 + 416 * s:610 + 416 * s], Dc[:, 208 * s:208 * s + 194], scale=2.0, accum_out=sm[:, 4 + s:5 + s])))
    noise(0)
    places(0)
    fl = do("v", c2, ts(sm[:, 2:4], sm[:, 4:6], R64, R64, A.add, A.subtract))
    of = [do("v", [fl, i_o2], ts(lo[:, 16 + 2 * s:18 + 2 * s], OE2, sm[:, 2 + s:3 + s], sm[:, 4 + s:5 + s], A.add, A.add)) for s in range(2)]
    sc = do("v", [of, K["VO"], k["qF"]], cp(T.F0[:, 0:2560].indirect(lo[:, 16:20]), T.VO[:]))
    qg = do("v", [sc], quant(T.qG[:], T.sG[:], T.F0[:, 0:512]))
    for o in (16, 0):
        do("p", [k["qF"], K["qI"][0]], mm(T.pD[:, 0:128], T.qI[:, 0:128], T.sI[:, 0:128], B("qF", 0)[:, o:o + 128], B("sF", 0)[:, o:o + 128], o > 0, False))
    mo = do("p", [qg, K["qI"][1]], mm(T.pD[:, 0:128], T.qI[:, 128:256], T.sI[:, 128:256], T.qG[:], T.sG[:], False, True))
    w0 = do("s", [k["own2"]], act(T.wl[:, 0:2], T.pB[:, NUML:NUMD + 1:NUMD - NUML], AF.Copy))
    a = do("v", [mo], trn(B("tr2", 0)[:, 128:256], T.pD[:, 0:128]))
    k["AB"] = [do("v", [a], cp(lo[:, 32 + 4 * j:36 + 4 * j], row(0, (LAL, LBD)[j], 1))) for j in range(2)]
    ex2 = do("v", [a, exl], cp(lo[:, 96:112], B("tr2", 0)[:, 128:256].indirect(EXL)))
    x2 = spread(srt[1]["a"], 1, 192, ())
    a = do("s", [x1, x2, thr[1]], act(Dc[:, 1040:1424], R[:, 0:384], AF.Sign, scale=-1.0, bias=own[:, 2:3]))
    a = do("s", [a], act(Dc[:, 1424:1808], Dc[:, 1040:1424], AF.Relu, scale=4.0, accum_out=sm[:, 14:15]))
    base_b = do("s", [a, c_[E4]], act(sm[:, 15:16], sm[:, 14:15], bias=C_(E4)))
    k1 = do("s", [c1], act(sm[:, 16:17], cn, scale=0.25, bias=135.5))
    k2 = do("v", [k1], ts(sm[:, 17:18], sm[:, 16:17], 192.0, sm[:, 16:17], A.is_lt, A.mult))
    k3 = do("v", [k2], ts(lo[:, 112:113], sm[:, 17:18], F_(3), None, A.max))
    mo_ = do("v", [p2[0], K["IOTA"], srt[0]["of"], srt[1]["of"], c_[CM]], ts(Mx[:, 0:128], T.IOTA[:, 0:512].indirect(so[:, 0:8]), own[:, 4:5], C_(CM), A.is_ge, A.add))
    xw = do("v", [mo_, srt[0]["G"], srt[1]["G"]], tt(R[:, 384:512], G[:, 0:128], Mx[:, 0:128], A.mult))
    mn = [do("v", [ex2, p2[j], K["IOTA"], c_[CM]], ts(Mx[:, 128 + 64 * j:192 + 64 * j], T.IOTA[:, 0:256].indirect(lo[:, 108:112]), own[:, 4 + j:5 + j], C_(CM), A.is_ge, A.add))
          for j in range(2)]

    arrived(0, (1, 3))
    qM, sM = T.qU[:, 64:192], T.sU[:, 64:192]
    mA = do("p", [list(k["A"].values())], mm(T.pA[:, 0:128], qM, sM, B("XW", 0)[:, 256:384], B("XWs", 0)[:, 256:384]))
    sA = do("s", [mA], act(G[64:128, 128:192], T.pA[64:128, 0:64], AF.Abs, bias=LIFT))
    mN = do("p", [k["qn"]], mm(T.pB[:, 0:128], qM, sM, SW0[:, NB:640], SWs0[:, NB:640]))
    sN = do("s", [mN], act(G[0:64, 128:192], T.pB[0:64, 0:64], AF.Abs, bias=LIFT))
    tg = do("v", [sA, sN], trn(trG[:, 128:192], G[:, 128:192]))
    aM = send([tg], "aM2", [trG[:, 159:161]] * 3, [LM[:, 16 + 2 * s:18 + 2 * s] for s in range(3)])
    n = ks[1]
    n["xt"] = held(0, 1, B("SW", 1), B("SWs", 1), XB, 2)
    cps.append(copies(1, n["xt"]))
    n["lt"] = held(0, 0, B("SW", 1), B("SWs", 1), LB, 2)

    new = [sA, sN]
    a = do("v", [k3, K["DT"], new, srt[0]["G"], srt[1]["G"]], tt(cs[:, 416:432], G[:, 0:192].indirect(lo[:, 112:113]), T.DT[:], A.mult))
    t_a = do("v", [a], red(own[:, 6:7], cs[:, 416:432]))
    d = do("v", [t_a, xw, x1, x2], ts(Dc[:, 2080:2592], R[:, 0:512], own[:, 6:7], 4.0, A.is_lt, A.mult))
    a = do("v", [d], scan(cs[:, 96:352], Dc[:, 2080:2336], Dc[:, 2336:2592], -286.0))
    base_a = do("v", [a], ts(sm[:, 18:19], cs[:, 351:352], -30.0, None, A.max))
    xn = [do("v", [mn[j], new], tt(R[:, RW + 192 + 64 * j:RW + 256 + 64 * j], G[:, 128:192], Mx[:, 128 + 64 * j:192 + 64 * j], A.mult)) for j in range(2)]

    l0 = lo
    k, lo, ix = ks[1], B("lo", 1), B("ix", 1)
    x3 = spread(aM, 2, RW, (0, 1, 2, 3))
    of = []
    for j in range(2):
        d = do("v", [x3, xn, ex2, (t_a, thr[1])[j]], ts(Dc[:, 1808 + 64 * j:1872 + 64 * j], R[:, RW:RW + 320].indirect(l0[:, 100 + 4 * j:104 + 4 * j]),
                                                       (own[:, 6:7], own[:, 2:3])[j], 4.0, A.is_lt, A.mult))
        c = do("v", [d, (base_a, base_b)[j]], scan(cs[:, 352 + 32 * j:384 + 32 * j], Dc[:, 1808 + 64 * j:1840 + 64 * j], Dc[:, 1840 + 64 * j:1872 + 64 * j],
                                                   (sm[:, 18:19], sm[:, 15:16])[j]))
        fl = do("v", [c], ts(sm[:, 20 + j:21 + j], cs[:, 383 + 32 * j:384 + 32 * j], R64, R64, A.add, A.subtract))
        of.append(do("v", [fl, i_oe], ts(lo[:, 3 * j:3 * j + 3], OE, sm[:, 20 + j:21 + j], cs[:, 383 + 32 * j:384 + 32 * j], A.add, A.add)))

    def flags():
        f = [do("s", [k["tr2"]], act(T.fm[:, 0:4], row(1, FL1), AF.Copy)), do("v", [k["tr2"]], cp(T.fm[:, 8:12], row(1, FL2)))]
        k["aF"] = send(f, "aF", [None, T.fm[:, 0:4], T.fm[:, 8:12]], [None, T.LF[:, 0:4], T.LF[:, 8:12]], (1, 2))

    slots(1, of, 2, flags)
    LQ, fo = T.LQ, T.fo
    w1 = [do("s", [k["own2"], w0], act(LQ[:, 6 + j:7 + j], T.pB[:, (NUML, NUMD)[j]:(NUML, NUMD)[j] + 1], bias=T.wl[:, j:j + 1])) for j in range(2)]
    wu = do("v", w1, cp(T.wu[:], LQ[:, 6:8]))
    aP = send([wu], "aP", [T.wu[:]] * 3, [T.LP[:, 2 * s:2 * s + 2] for s in range(3)])
    noise(1)
    places(1)
    a = do("v", [k["aF"]], tt(ix[:, 24:28], T.LF[:, 0:4], T.LF[:, 8:12], A.add))
    m = [do("v", [a, k["tr2"]], tt(ix[:, 16 + 4 * j:20 + 4 * j], row(1, (LAL, LBD)[j]), ix[:, 24:28], A.max)) for j in range(2)]
    k["AB"] = [do("v", m, ts(lo[:, 32:40], ix[:, 16:24], 319.0, None, A.min))] * 2
    a = do("p", [K["qW"], n["lt"]], mm(T.pA[:, 0:256], T.qW[:], T.sW[:], B("SW", 1)[:, LB:NB], B("SWs", 1)[:, LB:NB]))
    yo = do("s", [a], act(T.yw[:, 0:256], T.pA[:, 0:256], AF.Copy))
    arrived(1, (1, 3))
    xt = held(1, 1, T.FN, T.FNs, 256)
    lt = held(1, 0, T.FN, T.FNs, 0)
    my = do("p", [k["qn"], K["qW"]], mm(T.pB[:, 0:128], T.qW[:], T.sW[:], B("SW", 1)[:, NB:640], B("SWs", 1)[:, NB:640]))
    yn = do("v", [my], cp(T.yw[:, 256:320], T.pB[:, 0:64]))
    y0 = do("v", [yn, yo, k["pl"][0]], cp(T.yt[:, 0:128], T.yw[:, 0:320].indirect(lo[:, 64:72])))
    y1 = do("s", [yn, yo, k["pl"][0]], act(T.yt[:, 128:256], T.yw[:, 0:320].indirect(lo[:, 72:80]), AF.Copy))
    dma("s", [y0, y1], T.y[:], T.yt[:], "out")
    dma("y", xt[0], T.oc[:, 1024:2048], T.FN[:, 256:512].bitcast(U8), "out")
    dma("y", lt[0], T.oc[:, 0:1024], T.FN[:, 0:256].bitcast(U8), "out")
    for q in range(4):
        dma("ys"[q % 2], [lt[1], xt[1]], T.osc[4 * q:4 * q + 4, :], T.FNs[32 * q:32 * q + 4, 0:512], "out")
    lq = do("v", [aP], cp(LQ[:, 0:6], T.LP[:]))
    nu = [do("s", [lq, w1, K["fo"]], act(LQ[:, 8 + 4 * j:12 + 4 * j], LQ[:, j:8:2], accum_out=fo[:, j:j + 1])) for j in range(2)]
    a = do("v", nu, trn(fo[:, 32:64], fo[:, 0:32]))
    group("y", [a], [(o[t:t + 1, :], fo[j:128:32, 32 + 16 * t:48 + 16 * t]) for t in range(ROUNDS) for j, o in enumerate((T.lw, T.sw))], "out")

    dst = [cores[q] for q in others]
    far = [c for c in dst if topo.chip(c) != topo.chip(core)]
    fe = topo.engines(core, far[0])
    eng = {}
    for n, c in enumerate(far):
        w = len(fe) // len(far)
        eng[c] = fe[n * w:(n + 1) * w]
    for c in dst:
        if c not in eng:
            rest = [e for e in topo.engines(core, c) if e not in fe]
            eng[c], spare = rest[::len(far)], rest[1::len(far)]
            near = {"aM0": eng[c][:len(far)], "aM1": rest, "aS0": spare, "aF": spare, "aS1": spare}

    cnt, top, tok, behind, side, nd = {}, {}, {}, {}, [False], 0
    know = {q: {} for q in Q}
    also = {}
    for a, b in ALSO:
        also.setdefault(b, []).append(a)

    def need(qn, toks):
        want = {}
        for s, n in toks:
            want[s] = max(want.get(s, 0), n)
        for s, n in want.items():
            if know[qn].get(s, 0) >= n or any(behind.get(o, {}).get(s, 0) >= n for o in want.items() if o[0] != s):
                continue
            Q[qn].wait_ge(T.sem[s], n)
            top[s] = max(top.get(s, 0), n)
        for s, n in want.items():
            for a, b in list(behind.get((s, n), {}).items()) + [(s, n)]:
                know[qn][a] = max(know[qn].get(a, 0), b)

    def token(qn, s, step):
        n = cnt[s] = cnt.get(s, 0) + step
        k = dict(behind.get((s, n - step), {}))
        for a, b in know[qn].items():
            k[a] = max(k.get(a, 0), b)
        behind[(s, n)] = k
        return [(s, n)]

    for nid in ORDER or range(len(calls)):
        kind, qn, deps, what = calls[nid]
        toks = [x for d in deps + also.get(nid, []) for x in tok[d]]
        if what is None:
            tok[nid] = toks
            continue
        if kind in ("gp", "upper") and (kind == "upper") != side[0]:
            side[0] = not side[0]
            toks.append(("gc", cnt["gc"]))
        need(qn, toks)
        if kind == "dma":
            pairs, s = what
            if s is None:
                s, nd = "d%d" % nd, nd + 1
            for o, i in pairs:
                Q[qn].dma_start(o, i).then_inc(T.sem[s], 16)
            tok[nid] = token(qn, s, 16 * len(pairs))
        elif kind == "send":
            sem, view, land, to = what
            tr, n = [], 0
            for s in to:
                rid, pid, _ = topo.addr(dst[s])
                en = fe if dst[s] in far and not [x for x in to if x != s and dst[x] in far] else eng[dst[s]]
                if dst[s] not in far:
                    en = near.get(sem, en)
                n += len(en)
                tr.append(RemoteDMATransfer(dst_ids=[DstId(rid=rid, pnc=pid)], dma_engine_mask=sum(1 << e for e in en),
                                            remote_sem=T.sem[sem], src=view[s], dst=land[s]))
            g.remote_dma_fused(tr, local_sem=T.sem["ls"])
            cnt["ls"] = cnt.get("ls", 0) + n
            cnt[sem] = n
            tok[nid] = [(sem, n)]
        else:
            what(Q[qn]).then_inc(T.sem[qn], 1)
            tok[nid] = token(qn, qn, 1)
    for s, n in cnt.items():
        if top.get(s, 0) < n and s != "out":
            g.wait_ge(T.sem[s], n)
    g.wait_ge(T.sem["out"], cnt["out"])
